import numpy as np, ml_dtypes
CORES = [83,85,87,115,117,119]
N = 6
BF = ml_dtypes.bfloat16
def gentries(a):
    return np.ascontiguousarray(a.reshape(8, 16, -1).transpose(0, 2, 1)).reshape(8, -1)
def gtable(e):
    e = np.asarray(e); return np.ascontiguousarray(e.reshape(8, -1, 16).transpose(0, 2, 1)).reshape(128, -1).astype(np.int32)
V, W, G, CAP, ST, L, M, RO = 3072, 4032, 192, 48, 12, 256, 2, 4
TOP = 61440 + W - 1
def pick(rng, shape):
    a = rng.integers(0, W, shape); b = ST * rng.integers(0, L, shape) + rng.integers(0, M, shape)
    return np.where(rng.random(shape) < 0.5, b, a)
def parts(rng):
    x = (rng.integers(1, 257, (N, 8, 1, W)) * rng.random((N, 8, 16, W))).astype(np.int64)
    w = np.minimum(rng.integers(0, 16, (N, 8, 16, V)), rng.integers(3, 16, (N, 8, 1, V)))
    k = 4096 * w + pick(rng, (N, 8, 16, V))
    f = (rng.random((N, 8, V)) < rng.choice(np.array([0.3, 0.5, 0.7]), (N, 8, 1))).astype(np.int64)
    t = np.where(rng.random((N, 8, M * L)) < 0.6, rng.integers(0, 2601, (N, 8, M * L)), rng.integers(0, 601, (N, 8, M * L)))
    s = np.ascontiguousarray(np.argsort(rng.random((N, 8, N - 1, L)), axis=-1)[..., :G])
    return x, k, f, t, s
def pack(x, k, f, t, s):
    return {"x0": np.ascontiguousarray(x.reshape(N, 128, W)).astype(np.float32).astype(BF), "kt": np.ascontiguousarray(k.reshape(N, 128, V)).astype(np.int32),
            "f0": np.ascontiguousarray(f).astype(np.int32), "th": np.ascontiguousarray(t).astype(np.int32), "shw": np.stack([gtable(a.reshape(8, -1)) for a in s])}
def setup_inputs(rng):
    return pack(*parts(rng))
def setup_inputs_spread(rng):
    x, k, f, t, s = parts(rng)
    x = np.minimum(np.exp2(8.2 * rng.random((N, 8, 1, W)) * rng.random((N, 8, 16, W))).astype(np.int64) - 1, 255)
    w = np.minimum((16 * rng.random((N, 8, 16, V)) ** rng.choice(np.array([0.3, 1.0, 3.0]), (N, 8, 1, V))).astype(np.int64), 15)
    o = np.argsort(rng.random((N, 8, W)), axis=-1); j = np.minimum((W * rng.random((N, 8, 16 * V)) ** 3).astype(np.int64), W - 1)
    k = 4096 * w + np.take_along_axis(o, j, 2).reshape(N, 8, 16, V)
    f = (rng.random((N, 8, V)) < rng.choice(np.array([0.05, 0.5, 0.95]), (N, 8, 1))).astype(np.int64)
    t = np.minimum(np.exp2(12 * rng.random((N, 8, M * L))).astype(np.int64) - 1, 4080)
    s = np.minimum((L * rng.random((N, 8, N - 1, G)) ** 2).astype(np.int64), L - 1)
    return pack(x, k, f, t, s)
def setup_inputs_ends(rng):
    last = ST * (L - 1) + M - 1
    x = 255 * rng.integers(0, 2, (N, 8, 16, W)); kind = rng.integers(0, 3, (N, 8, 1, W))
    x = np.where(kind == 0, 0, np.where(kind == 1, 255, x))
    x[..., W - 1] = 255; x[:, 3, :, W - 1] = 255 * rng.integers(0, 2, (N, 16)); x[:, 5, :, W - 1] = 0
    k = TOP * rng.integers(0, 2, (N, 8, 16, V)); kind = rng.integers(0, 10, (N, 8, 1, V))
    e = 61440 * rng.integers(0, 2, (N, 8, 16, V)) + rng.choice(np.array([0, 1, V - 1, last, V, W - 1]), (N, 8, 16, V))
    k = np.where(kind < 2, 0, np.where(kind < 4, TOP, np.where(kind < 7, k, e)))
    for m in range(M):
        for i in (1, 2, L - 1):
            x[..., ST * i + m] = 0; k[..., ST * i + m] = TOP
        x[..., ST * (L - 2) + m] = 0; k[..., ST * (L - 2) + m] = 0
        x[..., ST * 3 + m] = 255; k[..., ST * 3 + m] = 0
    k[..., V - 1] = TOP
    f = rng.integers(0, 2, (N, 8, V)); f[:, ::2, V - 1] = 1
    t = 4080 * rng.integers(0, 2, (N, 8, M * L))
    z = ST * np.arange(L); xv = x[..., z]; flat = np.all(xv == xv[:, :, :1], axis=2)
    f[..., z] = np.where(flat, 1, f[..., z]); t[..., :L] = 4080 * (1 - f[..., z])
    f[1::2, 7, ST * (L - 1)] = 0; t[1::2, 7, L - 1] = 4080
    for m in range(1, M):
        t[..., m * L + 2] = 4080; t[..., m * L + L - 1] = 4080
    s = np.where(rng.random((N, 8, N - 1, G)) < 0.75, (L - 1) * rng.integers(0, 2, (N, 8, N - 1, G)), rng.integers(0, L, (N, 8, N - 1, G)))
    return pack(x, k, f, t, s)
def setup_inputs_corners(rng):
    x, k, f, t, s = parts(rng); own = np.arange(V); h = L // 2
    k = 4096 * rng.choice(np.array([0, 15, 15]), (N, 8, 16, V)) + (k & 4095)
    f[:, 2] = 0; f[:, 4] = 1; f[:, 6] = 1
    k[:, 1] = (k[:, 1] & 61440) + own; k[:, 3] = k[:, 3] & 61440
    k[:, 5] = (k[:, 5] & 61440) + rng.choice(np.array([V - 1, W - 1]), (N, 16, V)); k[:, 6] = 61440 + np.maximum(own - 1, 0)
    t = np.where(rng.random(t.shape) < 0.3, 4080 * rng.integers(0, 2, t.shape), t)
    x[..., W - 1] = rng.integers(2, 256, (N, 8, 16))
    for q in range(N):
        for g in range(8):
            o = rng.permutation(L); a, b = o[:h], o[h:]; xx = x[q, g]; kk = k[q, g]
            xx[:, ST * a] = 0; kk[rng.integers(0, 16, h), ST * a] = TOP
            kk[:, ST * b] = 61440 + ST * b
            b2 = b[:h // 4]; u = rng.integers(0, 2, (16, h // 4)); u[0] = 1
            xx[:, ST * b2] = xx[:, W - 1:W] - u; kk[:, ST * b2] = TOP; t[q, g, b2] = 0
            for d in range(N - 1):
                n = int(rng.choice(np.array([0, 1, CAP - 1, CAP, CAP + 1, G])))
                if (q == 0 and d == 0) or (q == N - 1 and d == N - 2): n = (CAP, CAP + 1, G, CAP - 1, 1, 0, CAP + 1, CAP)[g]
                s[q, g, d] = rng.permutation(np.concatenate([a[rng.integers(0, h, n)], b[rng.integers(0, h, G - n)]]))
    return pack(x, k, f, t, s)
def setup_inputs_crowd(rng):
    x, k, f, t, s = parts(rng); z = ST * np.arange(L); h2 = L // 2
    for q in range(N):
        for g in range(8):
            xx = x[q, g]; kk = k[q, g]
            if g % 2 == 1:
                hub = int(ST * rng.integers(0, L) + M - 1); was = np.array(kk); j = int(rng.integers(0, V)); one = int(rng.integers(0, L))
                kk[:] = (kk & 61440) + hub; kk[:, hub] = was[:, hub]; s[q, g] = one
                if g < 4: f[q, g, hub] = 1
                if g % 4 == 3:
                    kk[:, j] = was[:, j]; s[q, g, :, G - 1] = (one + 1) % L
            flip = np.ones(L, bool)
            if q % 4 == 1 and g == 7: flip[L - 1] = False
            if q % 4 == 2 and g % 2 == 1: flip[int(rng.integers(0, L))] = False
            if q % 4 == 3:
                flip[:] = g == 0
                flip[int(rng.integers(0, L))] = False
            xx[0, z] = rng.integers(1, 255, L)
            t[q, g, :L] = np.where(flip == (f[q, g, z] == 1), 0, 4080)
            xx[:, V - 1] = 255; f[q, g, V - 1] = 0
            i = rng.permutation(L)[:h2]; u = rng.integers(4, 255, (16, h2))
            xx[:, ST * i + 1] = 255 - u; kk[:, ST * i + 1] = 61440 + V - 1
            t[q, g, L + i] = np.add.reduce(u, axis=0) - rng.integers(0, 64, h2)
    return pack(x, k, f, t, s)
def setup_inputs_ties(rng):
    x, k, f, t, s = parts(rng); h = L // 2
    rec = 4096 * rng.integers(0, 16, (N, 8, 16, 1)) + pick(rng, (N, 8, 16, 1))
    lane = (np.arange(V) % ST) < M
    e = np.where(lane & (rng.random((N, 8, 16, V)) < 0.5), 61440 + pick(rng, (N, 8, 16, V)), rec)
    k[:, 1::2] = e[:, 1::2]; k[:, 2, 8:] = k[:, 2, :8]; k[:, 4, 1:] = np.where(rng.random((N, 15, V)) < 0.5, k[:, 4, :1], k[:, 4, 1:])
    x[..., V - 1] = 255; f[..., V - 1] = 0
    for q in range(N):
        for g in range(8):
            i = rng.permutation(L)[:h]; u = rng.integers(4, 255, (16, h)); xx = x[q, g]; kk = k[q, g]
            xx[:, ST * i] = 255 - u; kk[:, ST * i] = 61440 + V - 1
            t[q, g, i] = np.add.reduce(u, axis=0) + rng.integers(-1, 2, h)
    return pack(x, k, f, t, s)
def check_inputs(d):
    bad = []
    for a, lo, hi in (("x0", 0, 255), ("kt", 0, TOP), ("f0", 0, 1), ("th", 0, 4080), ("shw", 0, L - 1)):
        v = np.asarray(d[a]).astype(np.float64)
        if not (np.min(v) >= lo and np.max(v) <= hi): bad.append("range of " + a)
    v = np.asarray(d["x0"]).astype(np.float64)
    if not np.all(v == np.floor(v)): bad.append("whole numbers of x0")
    if np.max(np.asarray(d["kt"]).astype(np.int64) & 4095) >= W: bad.append("masters of kt")
    return bad
def reference(x0, kt, f0, th, shw):
    x = x0.astype(np.float32).astype(np.int64).reshape(N, 8, 16, W)
    k0 = kt.astype(np.int64).reshape(N, 8, 16, V); k = np.array(k0)
    f = np.zeros((N, 8, W), np.int64); f[..., :V] = f0
    o = np.zeros((N, 8, 16, V), np.int64) + np.arange(V)
    lim = th.astype(np.int64).reshape(N, 8, M, L)
    s = np.stack([gentries(a) for a in shw]).astype(np.int64).reshape(N, 8, N - 1, G)
    num = np.zeros(N, np.int64)
    for rnd in range(RO):
        m = rnd % M; v = ST * np.arange(L) + m
        ov = o[..., v]; fo = np.take_along_axis(f, ov.reshape(N, 8, 16 * L), 2).reshape(N, 8, 16, L)
        back = (ov != v) & (fo == 0)
        kv = np.where(back, k0[..., v], k[..., v]); ov = np.where(back, v, ov); k[..., v] = kv
        c = kv & 4095; w = kv >> 12
        fc = np.take_along_axis(f, c.reshape(N, 8, 16 * L), 2).reshape(N, 8, 16, L)
        best = np.where(fc == 0, kv, -1)
        for j in range(16):
            e = np.take_along_axis(k, np.minimum(c[:, :, j], V - 1)[:, :, None, :], 3)
            cand = 4096 * np.minimum(w[:, :, j][:, :, None, :], e >> 12) + (e & 4095)
            win = (fc[:, :, j] == 1)[:, :, None, :] & (cand > best)
            best = np.where(win, cand, best); ov = np.where(win, c[:, :, j][:, :, None, :], ov)
        k[..., v] = best; o[..., v] = ov
        c = best & 4095; w = best >> 12; y = np.zeros((N, 8, 16, L), np.int64)
        for j in range(16):
            e = np.take_along_axis(x, c[:, :, j][:, :, None, :], 3)
            y = np.maximum(y, np.minimum(e, 17 * w[:, :, j][:, :, None, :]))
        xv = x[..., v]; dist = np.add.reduce(np.abs(xv - y), axis=2)
        st = (dist < lim[:, :, m] + (num & 63)[:, None, None]).astype(np.int64)
        nx = np.where((st == 1)[:, :, None, :], y, (xv + y) >> 1)
        num = np.add.reduce((st != f[..., v]).astype(np.int64).reshape(N, 8 * L), axis=1)
        f[..., v] = st; x[..., v] = nx
        ch = np.any(nx != xv, axis=2).astype(np.int64)
        for a in range(N):
            for d in range(N - 1):
                q = (a + 1 + d) % N; ix = s[q, :, d]; h = np.take_along_axis(ch[q], ix, 1)
                go = (h == 1) & (np.add.accumulate(h, axis=1) - h < CAP); lo = V + d * G
                x[a, :, :, lo:lo + G] = np.where(go[:, None, :], np.take_along_axis(nx[q], ix[:, None, :], 2), x[a, :, :, lo:lo + G])
    yk = np.add.reduce(k.reshape(N, 128, L, ST)[..., :M], axis=3); yo = np.add.reduce(o.reshape(N, 128, L, ST)[..., :M], axis=3)
    return {"yx": x.reshape(N, 128, W).astype(np.float32).astype(BF), "yf": f[..., :V].astype(np.float32), "yk": yk.astype(np.float32), "yo": yo.astype(np.float32)}

@@ -1,0 +1,666 @@
+import math
+import numpy as np
+from concourse.bass import DstId, RemoteDMATransfer
+from concourse.mybir import AluOpType as ALU, ActivationFunctionType as AF
+
+N, V, W, G, CAP, ST, L, RO = 6, 3072, 4032, 192, 48, 12, 256, 4
+NG = (N - 1) * G
+BIG = 131072.0
+U = 262144.0
+MAGIC = 25165824.0
+NC, NH = 4, 2
+CL, HL = L // NC, L // NH
+CW = 16 * CL
+TWICE = ("kf", "wexp", "cu", "kc", "chi", "clo", "pw", "z16", "d2")
+PASSES, TRIES, SEED, FOUND = 3, 600, 0, {}
+
+SCRATCH = {
+    "psw": ("psum", [128, 1024], "float32"), "psd": ("psum", [128, 1024], "float32"),
+    "psx": ("psum", [128, 1024], "float32"), "psa": ("psum", [128, 512], "float32"),
+    "psb": ("psum", [128, 512], "float32"),
+}
+for _n, _c, _d in [
+    ("kti", V, "int32"), ("etab", W + 16, "float32"), ("xw", NG + W, "bfloat16"), ("fout", V, "float32"),
+    ("fi", 768, "int32"), ("fb", 768, "bfloat16"), ("thi", 128, "int32"), ("thh", 128, "bfloat16"),
+    ("thl", 128, "bfloat16"), ("thn", 128, "float32"), ("shi", 60, "int32"), ("shu", 60, "uint16"),
+    ("eg", 4096, "float32"), ("tb", 4096, "bfloat16"), ("rb", 4112, "bfloat16"), ("vs", 4096, "float32"),
+    ("xg", 4096, "bfloat16"), ("mn", 2 * CW, "bfloat16"), ("ys", 4096, "bfloat16"), ("og", 4096, "bfloat16"),
+    ("wo", 33 * L, "bfloat16"), ("wk", 2048, "bfloat16"),
+    ("zr", 1024, "bfloat16"), ("sel4", 512, "bfloat16"), ("idn", 128, "bfloat16"), ("nid", 128, "bfloat16"),
+    ("bones", 128, "bfloat16"), ("s1", 1024, "bfloat16"), ("s17", 1024, "bfloat16"), ("dg", 2048, "bfloat16"),
+    ("dgb", 2048, "bfloat16"), ("ox", 2048, "bfloat16"), ("o16", 128, "bfloat16"), ("c29", L, "bfloat16"),
+    ("cst", 512, "bfloat16"), ("rmask", CW, "bfloat16"), ("bmask", NG, "bfloat16"),
+    ("pci", 4, "int32"), ("pc", 16, "float32"), ("j8", 8, "float32"), ("m8", 8, "float32"),
+    ("ib", L, "bfloat16"), ("vhi", L, "bfloat16"), ("i32", 128, "float32"), ("ni32", 128, "float32"),
+    ("m32", 128, "float32"), ("p32", 128, "bfloat16"), ("n4k", 128, "bfloat16"), ("n256", 128, "bfloat16"),
+    ("nbon", 128, "bfloat16"), ("mh", L, "bfloat16"),
+    ("vlo0", L, "bfloat16"), ("vlo1", L, "bfloat16"), ("base", 60, "float32"), ("dlt", 60, "float32"),
+    ("ci", L, "int32"), ("cu", L, "uint16"), ("wexp", 2 * L, "bfloat16"), ("kc", L, "float32"),
+    ("chi", L, "bfloat16"), ("clo", L, "bfloat16"), ("ohi", L, "bfloat16"), ("olo", L, "bfloat16"),
+    ("own", L, "float32"), ("za", L, "float32"), ("cu2", L, "uint16"),
+    ("w17", 2 * L, "bfloat16"), ("kn0", L, "float32"), ("kn1", L, "float32"), ("kf", L, "float32"), ("zf", L, "float32"),
+    ("ou", L, "uint16"),
+    ("on0", L, "float32"), ("fu0", L, "uint16"), ("fu1", L, "uint16"), ("dk0", L, "float32"), ("dk1", L, "float32"),
+    ("pw", L, "bfloat16"), ("z16", L, "float32"), ("d2", L, "float32"), ("bit", L, "int32"),
+    ("ub", L, "bfloat16"), ("rl", L, "bfloat16"), ("a2", L, "float32"), ("hd", L, "float32"),
+    ("chg", L, "bfloat16"), ("chw", L, "bfloat16"), ("nbo0", L, "bfloat16"), ("nbo1", L, "bfloat16"),
+    ("nbe0", L, "bfloat16"), ("nbe1", L, "bfloat16"), ("nbn", L, "bfloat16"),
+    ("nq", L, "bfloat16"), ("junk", L, "float32"), ("asum", 4, "float32"), ("ai", 4, "int32"), ("am", 4, "float32"),
+    ("hb", NG, "bfloat16"), ("cnt", NG, "bfloat16"), ("q1", 60, "float32"), ("q2", 60, "float32"),
+    ("q3", 60, "float32"), ("qu", 60, "uint16"),
+    ("mir0", L + NG, "bfloat16"), ("mir1", L + NG, "bfloat16"), ("mir2", L + NG, "bfloat16"),
+    ("mir3", L + NG, "bfloat16"), ("mir4", L + NG, "bfloat16"),
+]:
+    for _s in (("0", "1") if _n in TWICE else ("",)):
+        SCRATCH[_n + _s] = ("sbuf", [128, _c], _d)
+
+NDMA = 40
+SEMAPHORES = (["ev", "ea", "ep", "eg"] + ["d%d" % _i for _i in range(NDMA)]
+              + ["arr%d" % _i for _i in range(RO + 1)] + ["snt%d" % _i for _i in range(2 * RO + 2)])
+
+SIZE = {"float32": 4, "int32": 4, "bfloat16": 2, "uint16": 2}
+CYC, PCYC, GATH = 1.04, 0.52, 1.56
+FIX = {"v": 60.0, "a": 90.0, "p": 30.0, "g": 160.0, "s": 60.0}
+FO, EG, RB, SM = "avav", "aaaa", "vvvv", "a"
+ZA, AB, OG, INT1 = "v", "a", ["aaaaaaaa", "aaaaaaaa", "aaaaaaaa", "avavavav"], False
+EARLY = [0.0, 0.0, 0.0, 0.0]
+XG, PARTS, PARTS4 = "aaaa", [(0, 2), (2, 3), (3, 4)], [(0, 2), (2, 4)]
+HB, MG = ["aa", "aa", "aa", "av"], ["aa", "aa", "aa", "va"]
+COFF = 144.0 * 4096 - 2016
+HOP, SELF, SLACK = 120.0, 60.0, 250.0
+
+
+def calls_of(T, topo, src, dests):
+    me = T.cores[src]
+    far = [x for x in dests if topo.chip(T.cores[x[1]]) != topo.chip(me)]
+    near = [x for x in dests if topo.chip(T.cores[x[1]]) == topo.chip(me)]
+    fe = topo.engines(me, T.cores[far[0][1]])
+    ne = [e for e in topo.engines(me, T.cores[near[0][1]]) if e not in fe]
+    hf, hn = len(fe) // 2, len(ne) // len(near)
+    first = [(far[0][0], far[0][1], fe[:hf]), (far[1][0], far[1][1], fe[hf:])]
+    first += [(x[0], x[1], ne[hn * i:hn * (i + 1)]) for i, x in enumerate(near)]
+    return [first] + [[(x[0], x[1], fe)] for x in far[2:]]
+
+
+def build(g, rank, T, topo):
+    ops, hist, cls, early = [], {}, [0], [0.0]
+    Q = {"v": g.vector, "a": g.scalar, "p": g.tensor, "g": g, "s": g.sync}
+
+    def R(name, a=0, b=None, s=1, p=None):
+        if name in TWICE:
+            name += str(cls[0])
+        if b is None:
+            b = SCRATCH[name][1][1]
+        cols = slice(a, b) if s == 1 else slice(a, b, s)
+        n = len(range(a, b, s))
+        return {"ap": T[name][(slice(None) if p is None else p, cols)], "reg": [(name, a, a + (n - 1) * s + 1)], "n": n,
+                "ps": name[:2] == "ps", "b": SIZE[SCRATCH[name][2]], "ind": False}
+
+    def IND(win, off):
+        return {"ap": win["ap"].indirect(off["ap"]), "reg": win["reg"] + off["reg"], "n": 16 * off["n"], "ps": False,
+                "b": win["b"], "ind": True}
+
+    def add(alts, outs, ins, kind="c", extra=(), lat=0.0, sem=None):
+        me, deps = len(ops), {}
+        for e in extra:
+            deps[e] = True
+        acc = [(r, True) for x in outs for r in x["reg"]] + [(r, False) for x in ins for r in x["reg"]]
+        for (name, a, b), wr in acc:
+            ps = name[:2] == "ps"
+            gr = 512 if ps else 16 // SIZE[SCRATCH[name][2]]
+            lo, hi = a // gr * gr, -(-b // gr) * gr
+            for j, a2, b2, lo2, hi2, wr2 in hist.setdefault(name, []):
+                if lo < hi2 and lo2 < hi and (wr or wr2):
+                    if (a < b2 and a2 < b) or kind != "c" or ops[j]["kind"] != "c":
+                        deps[j] = True
+        for (name, a, b), wr in acc:
+            gr = 512 if name[:2] == "ps" else 16 // SIZE[SCRATCH[name][2]]
+            hist[name].append((me, a, b, a // gr * gr, -(-b // gr) * gr, wr))
+        banks = sorted(set((name, k) for (name, a, b), wr in acc if name[:2] == "ps" for k in range(a // 512, (b - 1) // 512 + 1)))
+        ops.append({"alts": alts, "deps": deps, "kind": kind, "lat": lat, "sem": sem, "banks": banks, "early": early[0]})
+        return me
+
+    def one(x, *rest):
+        if x["ind"]:
+            return GATH
+        return 0.5 if all(y["b"] == 2 for y in (x,) + rest) else 1.0
+
+    def vc(n, k):
+        return FIX["v"] + max(64.0, n * k) * CYC
+
+    def act_alt(out, in_, func, bias, scale, accum=None):
+        kw = {}
+        if bias is not None:
+            kw["bias"] = bias
+        if scale is not None:
+            kw["scale"] = scale
+        if accum is not None:
+            kw["accum_out"] = accum["ap"]
+        return (FIX["a"] + max(64.0, in_["n"] * (GATH if in_["ind"] else 1.0)) * CYC,
+                lambda q: q.activation(out["ap"], in_["ap"], func, **kw))
+
+    def act(out, in_, func, bias=None, scale=None, accum=None):
+        return add({"a": act_alt(out, in_, func, bias, scale, accum)}, [out] + ([accum] if accum else []), [in_])
+
+    def tt(out, a, b, op):
+        k = 1.0 if (a["ps"] or b["ps"]) else 2.0
+        return add({"v": (vc(out["n"], k), lambda q: q.tensor_tensor(out["ap"], a["ap"], b["ap"], op))}, [out], [a, b])
+
+    def val(s):
+        return s["ap"] if isinstance(s, dict) else s
+
+    def ts(out, a, s1, op0, s2=None, op1=None):
+        ins = [a] + [s for s in (s1, s2) if isinstance(s, dict)]
+        if s2 is None:
+            f = lambda q: q.tensor_scalar(out["ap"], a["ap"], val(s1), None, op0)
+        else:
+            f = lambda q: q.tensor_scalar(out["ap"], a["ap"], val(s1), val(s2), op0, op1)
+        return add({"v": (vc(out["n"], one(a, out)), f)}, [out], ins)
+
+    def lin(out, a, scale=None, bias=None, eng="va"):
+        alts = {}
+        if "v" in eng:
+            if scale is None and bias is None:
+                f = lambda q: q.tensor_copy(out["ap"], a["ap"])
+            elif bias is None:
+                f = lambda q: q.tensor_scalar(out["ap"], a["ap"], scale, None, ALU.mult)
+            else:
+                f = lambda q: q.tensor_scalar(out["ap"], a["ap"], val(scale), val(bias), ALU.mult, ALU.add)
+            alts["v"] = (vc(out["n"], one(a, out)), f)
+        if "a" in eng:
+            alts["a"] = act_alt(out, a, AF.Copy if bias is None else AF.Identity, val(bias), val(scale))
+        return add(alts, [out], [a] + [s for s in (scale, bias) if isinstance(s, dict)])
+
+    def scan(out, d0, d1, init, op0, op1):
+        return add({"v": (vc(out["n"], one(d0, d1, out)),
+                          lambda q: q.tensor_tensor_scan(out["ap"], d0["ap"], d1["ap"], init, op0, op1))}, [out], [d0, d1])
+
+    def fill(out, c):
+        return add({"v": (vc(out["n"], one(out)), lambda q: q.memset(out["ap"], c))}, [out], [])
+
+    def mm(ms):
+        def f(q):
+            for o, l, r, st, sp in ms:
+                last = q.matmul(o["ap"], l["ap"], r["ap"], st, sp)
+            return last
+        cost = FIX["p"] + sum(max(64, m[0]["n"]) * PCYC * (4 if m[2]["b"] == 4 else 1) + 4.0 for m in ms)
+        return add({"p": (cost, f)}, [m[0] for m in ms], [m[1] for m in ms] + [m[2] for m in ms])
+
+    def group(out, pairs):
+        return [(out, l, r, i == 0, i == len(pairs) - 1) for i, (l, r) in enumerate(pairs)]
+
+    def iota(out, pat, base, cm):
+        kw = {} if SCRATCH[out["reg"][0][0]][2] == "int32" else {"allow_small_or_imprecise_dtypes": True}
+        return add({"g": (FIX["g"] + 2 * out["n"] * CYC, lambda q: q.iota(out["ap"], pat, base, cm, **kw))}, [out], [])
+
+    def asel(out, in_, pat, op, fl, base, cm):
+        return add({"g": (FIX["g"] + 2 * out["n"] * CYC,
+                          lambda q: q.affine_select(out["ap"], in_["ap"], pat, op, fl, base, cm))}, [out], [in_])
+
+    ndma = [0]
+
+    def dma(out, in_, nbytes, eng="s", extra=()):
+        sem = "d%d" % ndma[0]
+        ndma[0] += 1
+        hb = lambda x: x if isinstance(x, dict) else {"ap": x, "reg": []}
+        o, i = hb(out), hb(in_)
+        return add({eng: (FIX["s"], lambda q: q.dma_start(o["ap"], i["ap"]))}, [o], [i], kind="d", extra=extra,
+                   lat=nbytes / 200.0, sem=(sem, 16))
+
+    nsnt = [0]
+
+    def exchange(k, dests_of, src, dst):
+        mine = []
+        for call in calls_of(T, topo, rank, dests_of(rank)):
+            sem = "snt%d" % nsnt[0]
+            nsnt[0] += 1
+            trs = []
+            for d, r, es in call:
+                rid, pid, _ = topo.addr(T.cores[r])
+                trs.append(RemoteDMATransfer(dst_ids=[DstId(rid=rid, pnc=pid)], dma_engine_mask=sum(1 << e for e in es),
+                                             remote_sem=T.sem["arr%d" % k], src=src(d)["ap"], dst=dst(d)["ap"]))
+            f = lambda q, trs=trs, sem=sem: q.remote_dma_fused(trs, local_sem=T.sem[sem])
+            mine.append(add({"g": (900.0, f)}, [], [src(c[0]) for c in call], kind="r", lat=3500.0,
+                            sem=(sem, sum(len(c[2]) for c in call))))
+        total = sum(len(es) for q in range(N) if q != rank
+                    for call in calls_of(T, topo, q, dests_of(q)) for d, r, es in call if r == rank)
+        return add({"x": (0.0, None)}, [dst(d) for d in range(N - 1)], [], kind="x", extra=mine, lat=1500.0,
+                   sem=("arr%d" % k, total))
+
+    def lanes(name, m, a=0, b=L):
+        o = m + (NG if name == "xw" else 0)
+        return R(name, ST * a + o, ST * (b - 1) + o + 1, ST)
+
+    P32 = slice(0, 32)
+    pc = lambda j: R("pc", j, j + 1)
+    blk = lambda name, k: R(name, 128 * k, 128 * (k + 1))
+
+    dma(R("fi", p=P32), T.f0[:], 98304)
+    kts = [dma(R("kti", 1024 * j, 1024 * (j + 1)), T.kt[:, 1024 * j:1024 * (j + 1)], 524288, eng="sa"[j == 1]) for j in range(3)]
+    dma(R("thi", p=P32), T.th[:], 16384, extra=kts[:1])
+    dma(R("shi"), T.shw[:], 30720, extra=kts[:1])
+    dma(R("xw", NG + V, NG + W), T.x0[:, V:W], 128 * NG * 2, extra=kts[1:2])
+    dma(R("xw", NG, NG + V), T.x0[:, 0:V], 128 * V * 2, extra=kts)
+
+    fill(R("zr", 0, 512), 0.0)
+    fill(R("zr", 512, 1024), 0.0)
+    asel(R("sel4", p=P32), R("zr", 0, 512, p=P32), [[-1, 4], [-4, 8], [0, 16]], ALU.not_equal, 1.0, 0, 1)
+    iota(R("pci", 0, 1), [[0, 1]], 0, 1)
+    iota(R("j8"), [[1, 8]], 0, 0)
+    asel(R("bones"), R("zr", 0, 128), [[-16, 8], [0, 16]], ALU.is_ge, 1.0, -16, 1)
+    asel(R("bones"), R("bones"), [[-16, 8], [0, 16]], ALU.is_ge, 0.0, 0, 1)
+    asel(R("idn"), R("zr", 0, 128), [[-1, 128]], ALU.not_equal, 1.0, 0, 1)
+    asel(R("nid"), R("zr", 0, 128), [[-1, 128]], ALU.not_equal, -1.0, 0, 1)
+    for hh in range(2):
+        asel(R("dg", 1024 * hh, 1024 * (hh + 1)), R("zr"), [[-256, 8], [-16, 8], [255, 16]], ALU.not_equal, -32.0, -2048 * hh, 1)
+    iota(R("base"), [[16, 60]], L, 0)
+    for m in range(2):
+        iota(R("vlo%d" % m), [[0, 16], [ST, 16]], m, 0)
+    iota(R("vhi"), [[16 * ST, 16], [0, 16]], 0, 0)
+    iota(R("ib"), [[1, L]], 0, 0)
+    for name, c in (("i32", 1.0), ("p32", 1.0 / 64), ("n4k", -4096.0), ("ni32", -1.0), ("m32", -64.0), ("n256", -1.0 / L)):
+        lin(R(name), R("idn"), c, eng="a")
+    for k in range(16):
+        lin(blk("wk", k), R("idn"), 2.0 ** (k - 1) * (1.0 if k == 15 else -1.0))
+    lin(R("nbon"), R("bones"), -1.0, eng="a")
+    fill(R("mh"), -0.5)
+    for hh in range(2):
+        o, z = R("ox", 1024 * hh, 1024 * (hh + 1)), R("zr", 0, 1024)
+        asel(o, z, [[-256, 8], [-16, 8], [256, 16]], ALU.not_equal, 1.0, -2048 * hh, 1)
+        asel(o, o, [[-256, 8], [-16, 8], [256, 16]], ALU.not_equal, 1.0, -2048 * hh - 1, 1)
+        asel(R("dgb", 1024 * hh, 1024 * (hh + 1)), z, [[-256, 8], [-16, 8], [255, 16]], ALU.not_equal, 8192.0, -2048 * hh, 1)
+    ts(R("pci", 1, 2), R("pci", 0, 1), 15, ALU.bitwise_and)
+    ts(R("pci", 2, 3), R("pci", 0, 1), 7, ALU.bitwise_and)
+    lin(R("pc", 0, 2), R("pci", 1, 3), eng="v")
+    ts(pc(2), pc(0), 8.0, ALU.is_lt)
+    ts(pc(3), pc(0), 8.0, ALU.is_ge)
+    lin(R("pc", 4, 6), R("pc", 2, 4), -64.0, eng="v")
+    lin(R("pc", 6, 8), R("pc", 2, 4), U * (144 + 63.0 / 64), -U * 63 / 128, eng="v")
+    lin(R("pc", 8, 10), R("pc", 2, 4), 1.0 / U, eng="v")
+    lin(R("pc", 10, 12), R("pc", 2, 4), 255.5078125, -128.0, eng="v")
+    ts(R("m8"), R("j8"), pc(1), ALU.is_equal)
+    for j in range(8):
+        ts(blk("s1", j), R("bones"), R("m8", j, j + 1), ALU.mult)
+    lin(R("s17"), R("s1"), 17.0)
+    fill(R("o16"), 0.0625)
+    fill(R("c29"), 32 * 128 * U)
+    fill(R("cst"), 1.0)
+    fill(R("cst", 0, 512, 16), -128 * U)
+    fill(R("rmask"), 1.0)
+    fill(R("rmask", 0, CW, 16), 0.0)
+    fill(R("bmask"), 1.0)
+    fill(R("bmask", 0, NG, G), 0.0)
+    fill(R("rb", 0, 16), 0.0)
+    fill(R("wo", 4096, 4112), 0.0)
+    fill(R("wo", 8208, 33 * L), 0.0)
+    fill(R("etab", V, W), -BIG)
+    fill(R("etab", W, W + 16), 1.0)
+    ts(R("base"), R("base"), pc(0), ALU.add)
+    tt(R("dlt"), R("shi"), R("base"), ALU.subtract)
+    lin(R("shu"), R("shi"), eng="v")
+
+    lin(R("fb", p=P32), R("fi", p=P32), BIG, -BIG, eng="v")
+    for j, ps in enumerate(("psw", "psd", "psx")):
+        cuts = sorted(set([1024 * j, 1024 * j + 512, 1024 * j + 1024] + [c for c in range(0, V, 768) if 1024 * j < c < 1024 * j + 1024]))
+        ms = []
+        for a, b in zip(cuts[:-1], cuts[1:]):
+            s = a // 768
+            ms.append((R(ps, a - 1024 * j, b - 1024 * j), R("sel4", 128 * s, 128 * (s + 1), p=P32),
+                       R("fb", a - 768 * s, b - 768 * s, p=P32), True, True))
+        mm(ms)
+        lin(R("fout", 1024 * j, 1024 * (j + 1)), R(ps), 1.0 / BIG, 1.0, eng="a")
+        tt(R("etab", 1024 * j, 1024 * (j + 1)), R("kti", 1024 * j, 1024 * (j + 1)), R(ps), ALU.add)
+    lin(R("thn", p=P32), R("thi", p=P32), -1.0, eng="v")
+    lin(R("thh", p=P32), R("thn", p=P32))
+    tt(R("thl", p=P32), R("thn", p=P32), R("thh", p=P32), ALU.subtract)
+    for m in range(2):
+        lin(R("nbo%d" % m), lanes("fout", m), BIG, -BIG)
+
+    exchange(RO, lambda q: [(d, (q + 1 + d) % N) for d in range(N - 1)],
+             lambda d: R("xw", NG + V + G * d, NG + V + G * (d + 1)), lambda d: R("mir0", L + G * d, L + G * (d + 1)))
+
+    for t in range(RO):
+        m, late, last = t % 2, t >= 2, t == RO - 1
+        cls[0], early[0] = m, 0.0
+        kn, dk, fu, nbo = ["%s%d" % (x, m) for x in ("kn", "dk", "fu", "nbo")]
+        tb, tb0 = ("wo", 0) if t == 0 else ("tb", 0)
+        xg, xg0 = "xg", 0
+        rb = (lambda a, b, s=1: R("wo", 4096 + a, 4096 + b, s)) if t == 0 else (lambda a, b, s=1: R("rb", a, b, s))
+        H = [(HL * h, HL * (h + 1)) for h in range(NH)]
+        if late:
+            for c in range(NC):
+                out, src = R("xg", CW * c, CW * (c + 1)), IND(R("etab"), R(fu, CL * c, CL * (c + 1)))
+                if FO[c] == "a":
+                    act(out, src, AF.Sign, bias=0.5)
+                else:
+                    ts(out, src, 0.0, ALU.is_lt, -2.0, ALU.mult)
+                mm(group(R("psw", CL * c, CL * (c + 1)), [(blk("wk", k), R("xg", CW * c + k, CW * (c + 1), 16)) for k in range(16)]
+                         + ([(R("idn"), R("mh", 0, CL))] if FO[c] == "a" else [])))
+            for a, b in H:
+                bk, pk = R("bit", a, b), R("psw", 512 + a, 512 + b)
+                tt(bk, R("pw", a, b), R("psw", a, b), ALU.mult)
+                ts(bk, bk, 15, ALU.arith_shift_right, 1, ALU.bitwise_and)
+                tt(pk, R(dk, a, b), bk, ALU.mult)
+                tt(R("ci", a, b), R(kn, a, b), pk, ALU.add)
+                ts(R("ci", a, b), R("ci", a, b), 4095, ALU.bitwise_and)
+                lin(R("cu", a, b), R("ci", a, b), eng="v")
+                tt(R("kf", a, b), R(kn, a, b), pk, ALU.add)
+                tt(lanes("etab", m, a, b), lanes("etab", m, a, b), pk, ALU.add)
+                tt(R("psw", 768 + a, 768 + b), R("d2", a, b), bk, ALU.mult)
+                tt(R("kc", a, b), R("z16", a, b), R("psw", 768 + a, 768 + b), ALU.add)
+        master = lambda a, b: [(R("i32"), R("kf", a, b)), (R("p32"), R("wexp", 2 * a, 2 * b, 2)), (R("p32"), R("wexp", 2 * a + 1, 2 * b, 2))]
+        for a, b in H:
+            if not late:
+                lin(R("kf", a, b), lanes("kti", m, a, b), eng="v")
+            for kk in range(2):
+                lin(R("wexp", 2 * a + kk, 2 * b, 2), R("kf", a, b), pc(4 + kk), pc(6 + kk), eng=SM)
+            if not late:
+                ts(R("ci", a, b), lanes("kti", m, a, b), 4095, ALU.bitwise_and)
+                lin(R("cu", a, b), R("ci", a, b), eng="v")
+            if not late:
+                lin(R("kc", a, b), R("kf", a, b), 64.0, 16.0, eng=SM)
+        for c0, c1 in PARTS:
+            a, b = CL * c0, CL * c1
+            for c in range(c0, c1):
+                w0, w1, ps = CW * c, CW * (c + 1), ("psx", "psw")[c % 2]
+                lin(R("eg", w0, w1), IND(R("etab"), R("cu", CL * c, CL * (c + 1))), 64.0, eng=EG[c])
+                mm([(R(ps, 512 * k + j, 512 * (k + 1), 8), blk("s1", j), R("wexp", 2 * CL * c + 64 * k, 2 * CL * c + 64 * (k + 1)), True, True)
+                    for k in range(CW // 512) for j in range(8)])
+                tt(R(tb, tb0 + w0, tb0 + w1), R("eg", w0, w1), R(ps, 0, CW), ALU.add)
+                if RB[c] == "v":
+                    ts(rb(16 + w0, 16 + w1), R(tb, tb0 + w0, tb0 + w1), 144.0 * U, ALU.max, 144.0 * U, ALU.subtract)
+                else:
+                    act(rb(16 + w0, 16 + w1), R(tb, tb0 + w0, tb0 + w1), AF.Relu, bias=-144.0 * U)
+                for k in range(CW // 512):
+                    x = w0 + 512 * k
+                    d0 = R("psd", 512 * k, 512 * (k + 1))
+                    mm(group(d0, [(R("idn"), R("cst")), (R("idn"), rb(x + 16, x + 528)), (R("nid"), rb(x + 15, x + 527))]))
+                    scan(R("vs", x, x + 512), d0, R("eg", x, x + 512), 0.0, ALU.add, ALU.max)
+            mm(group(R("psa", a, b), [(R("idn"), R("c29", 0, b - a))]
+                     + [(blk("dg", k), R(tb, tb0 + 16 * a + k, tb0 + 16 * b, 16)) for k in range(16)]))
+            tt(R("own", a, b), R("kc", a, b), R("psa", a, b), ALU.min)
+            mm(group(R("psa", L + a, L + b), [(R("nid"), rb(16 + 16 * a + 15, 16 + 16 * b, 16)), (R("i32"), R("vs", 16 * a + 15, 16 * b, 16))]))
+            tt(R("zf", a, b), R("own", a, b), R("psa", L + a, L + b), ALU.max)
+            lin(R("za", a, b), R("zf", a, b), 1.0 / 64, -0.25, eng=ZA)
+            ts(R(kn, a, b), R("za", a, b), 0.5 * MAGIC, ALU.add, 0.5 * MAGIC, ALU.subtract)
+            for kk in range(2):
+                lin(R("w17", 2 * a + kk, 2 * b, 2), R("zf", a, b), pc(8 + kk), pc(10 + kk), eng=SM)
+            mm(group(R("psa", a, b), [(R("n4k"), R("w17", 2 * a, 2 * b, 2)), (R("n4k"), R("w17", 2 * a + 1, 2 * b, 2)), (R("i32"), R(kn, a, b))]))
+            if m:
+                ts(R("za", a, b), R("psa", a, b), float(V), ALU.is_ge, -float(W), ALU.mult)
+                tt(R("za", a, b), R("za", a, b), R("psa", a, b), ALU.add)
+                lin(R("cu2", a, b), R("za", a, b), 1.0, float(NG), eng="v")
+            else:
+                lin(R("cu2", a, b), R("psa", a, b), eng="v")
+        early[0] = EARLY[t]
+        p0, p1 = R("psb", 0, L), R("psb", L, 2 * L)
+        pa, pb = R("psd", L, 2 * L), R("psd", 3 * L, 4 * L)
+        hi, lo = ("ohi", "olo") if late else ("chi", "clo")
+        mm(group(pa, master(0, L)))
+        lin(R(hi), pa, 1.0, -COFF, eng=SM)
+        mm(group(pb, master(0, L) + [(R("nid"), R(hi))]))
+        lin(R(lo), pb, 1.0, -COFF, eng=SM)
+        if late:
+            for a, b in H:
+                mm(group(R("psb", L + a, L + b), [(R("i32"), R("zf", a, b)), (R("m32"), R(kn, a, b)), (R("n256"), R("ib", a, b))]))
+                lin(R("ou", a, b), R("psb", L + a, L + b), -float(L), 32.0 * L, eng="v")
+        else:
+            mm(group(p0, master(0, L) + [(R("nid"), R("vhi")), (R("nid"), R("vlo%d" % m))]))
+            ts(R("junk"), p0, COFF, ALU.is_equal, COFF + W, ALU.mult)
+            tt(R("junk"), R("junk"), pa, ALU.max)
+            lin(R(fu), R("junk"), 1.0, -COFF, eng="v")
+            mm(group(p1, [(R("i32"), R("zf")), (R("m32"), R(kn))]))
+            act(R("pw"), p1, AF.Exp, scale=math.log(2.0))
+            mm(group(p0, [(R("i32"), R("kf")), (R("ni32"), R(kn))]))
+            lin(R(dk), p0, eng="a")
+            mm(group(p1, [(R("i32"), R("kc")), (R("ni32"), R("zf"))]))
+            lin(R("d2"), p1, eng="a")
+            lin(R("z16"), R("zf"), 1.0, 16.0, eng="a")
+        early[0] = 0.0
+        for c in range(NC):
+            w0, w1, ps = CW * c, CW * (c + 1), ("psx", "psw")[c % 2]
+            lin(R(xg, xg0 + w0, xg0 + w1), IND(R("xw", NG * (1 - m), NG * (1 - m) + W), R("cu2", CL * c, CL * (c + 1))), eng=XG[c])
+            mm([(R(ps, 512 * k + j, 512 * (k + 1), 8), blk("s17", j), R("w17", 2 * CL * c + 64 * k, 2 * CL * c + 64 * (k + 1)), True, True)
+                for k in range(CW // 512) for j in range(8)])
+            mn = R("mn", CW * (c % 2), CW * (c % 2 + 1))
+            tt(mn, R(xg, xg0 + w0, xg0 + w1), R(ps, 0, CW), ALU.min)
+            scan(R("ys", w0, w1), R("rmask"), mn, 0.0, ALU.mult, ALU.max)
+        mir, nxt = "mir%d" % t, "mir%d" % (t + 1)
+        old, new = ("nbe%d" % m, "nbn") if late else (nbo, "nbe%d" % m)
+        for a, b in [(CL * c0, CL * c1) for c0, c1 in PARTS4]:
+            y, xv = R("ys", 16 * a + 15, 16 * b, 16), lanes("xw", m, a, b)
+            nb, dm, nx, ex = R("psd", a, b), R("psd", 512 + a, 512 + b), R("psx", 512 + a, 512 + b), R("psx", 768 + a, 768 + b)
+            mm(group(dm, [(R("idn"), R("mh", 0, b - a)), (R("idn"), xv), (R("nid"), y)]))
+            if AB == "a":
+                act(R("rl", a, b), dm, AF.Abs, bias=0.5)
+            else:
+                ts(R("rl", a, b), dm, 0.5, ALU.add, 0.0, ALU.min)
+            ms = []
+            for s in range(a // 128, -(-b // 128)):
+                a1, b1 = max(a, 128 * s), min(b, 128 * (s + 1))
+                sel = R("sel4", 128 * (2 * m + s), 128 * (2 * m + s + 1), p=P32)
+                dist = [(R("bones"), R("rl", a1, b1))] if AB == "a" else [
+                    (R("bones"), lanes("xw", m, a1, b1)), (R("nbon"), R("ys", 16 * a1 + 15, 16 * b1, 16)),
+                    (R("nbon"), R("rl", a1, b1)), (R("nbon"), R("rl", a1, b1))]
+                ms += group(R("psd", a1, b1), [(sel, R("thh", a1 - 128 * s, b1 - 128 * s, p=P32)),
+                                               (sel, R("thl", a1 - 128 * s, b1 - 128 * s, p=P32))] + dist)
+            mm(ms)
+            lin(R("a2", a, b), dm, 1.0, MAGIC, eng=SM)
+            lin(R("hd", a, b), R("a2", a, b), -0.5 / BIG, 0.5 * MAGIC / BIG, eng=SM)
+            ts(nb, nb, R("am", 0, 1) if t else 0.0, ALU.is_ge, -BIG, ALU.mult)
+            if not last:
+                tt(lanes("etab", m, a, b), R(kn, a, b), nb, ALU.add)
+            tt(R("ub", a, b), R("hd", a, b), nb, ALU.mult)
+            if not last:
+                lin(R(new, a, b), nb, eng=SM)
+            if late:
+                lin(lanes("fout", m, a, b), nb, 1.0 / BIG, 1.0, eng=SM)
+            mm(group(ex, [(R("idn"), y), (R("nid"), xv), (R("idn"), R("ub", a, b))])
+               + group(nx, [(R("idn"), y), (R("idn"), R("ub", a, b))]))
+            act(R("chg", a, b), ex, AF.Abs)
+            lin(R(mir, a, b), nx, eng="va" if last else SM)
+            mm([(R("psa", a, b), R("bones"), R("chg", a, b), True, True)])
+            act(R("chw", a, b), R("psa", a, b), AF.Sign)
+        lin(lanes("xw", m), R(mir, 0, L), eng="va" if last else SM)
+        if not last:
+            mm(group(R("psb", L, 2 * L), [(R("idn"), R(new)), (R("nid"), R(old))]))
+            act(R("nq"), R("psb", L, 2 * L), AF.Abs, scale=1.0 / BIG)
+            mm([(R("psb", L, 2 * L), R("o16"), R("nq"), True, True)])
+            act(R("junk"), R("psb", L, 2 * L), AF.Copy, accum=R("asum", 0, 1))
+            lin(R("ai", 0, 1), R("asum", 0, 1), eng="v")
+            ts(R("ai", 1, 2), R("ai", 0, 1), 63, ALU.bitwise_and)
+            lin(R("am", 0, 1), R("ai", 1, 2), eng="v")
+        for (a, b), e in zip(((0, 3), (3, 5)), HB[t]):
+            lin(R("hb", G * a, G * b), IND(R("chw"), R("shu", 12 * a, 12 * b)), eng=e)
+            scan(R("cnt", G * a, G * b), R("bmask", G * a, G * b), R("hb", G * a, G * b), 0.0, ALU.mult, ALU.add)
+        qp = R("psa", L, L + 60)
+        mm(group(qp, [(blk("dgb", k), R("hb", k, NG, 16)) for k in range(16)] + [(blk("dg", k), R("cnt", k, NG, 16)) for k in range(16)]))
+        ts(R("q1"), qp, 32.0 * (256 - CAP), ALU.is_ge)
+        tt(R("q2"), R("q1"), R("dlt"), ALU.mult)
+        tt(R("q3"), R("q2"), R("base"), ALU.add)
+        lin(R("qu"), R("q3"), eng="v")
+        for (a, b), e in zip(((0, 2), (2, 5)), MG[t]):
+            lin(R(nxt, L + G * a, L + G * b), IND(R(mir), R("qu", 12 * a, 12 * b)), eng=e)
+        g0 = (NG + V) * m
+        exchange(t, lambda q: [(d, (q - 1 - d) % N) for d in range(N - 1)],
+                 lambda d: R(nxt, L + G * d, L + G * (d + 1)), lambda d: R("xw", g0 + G * d, g0 + G * (d + 1)))
+        if last:
+            dma(T.yx[:, V:W], R("xw", g0, g0 + NG), 128 * NG * 2)
+            dma(T.yx[:, 0:V], R("xw", NG, NG + V), 128 * V * 2)
+            dma(T.yf[:], R("fout", p=slice(0, 128, 16)), 98304)
+            tt(R("dk0"), R("kn0"), R("kn1"), ALU.add)
+            dma(T.yk[:], R("dk0"), 131072)
+        early[0] = EARLY[t]
+        if not late:
+            continue
+        for row, (x0, x1, x2) in enumerate((("vhi", "chi", "ohi"), ("vlo%d" % m, "clo", "olo"))):
+            rows = slice(row, 128, 16)
+            dma(R("wo", 0, L, p=rows), R(x0, p=rows), 4096)
+            dma(R("wo", L, 17 * L, p=rows), R(x1), 65536)
+            dma(R("wo", 17 * L, 33 * L, p=rows), R(x2), 65536)
+        for c, e in enumerate(OG[t]):
+            n = L // len(OG[t])
+            lin(R("og", 16 * n * c, 16 * n * (c + 1)), IND(R("wo"), R("ou", n * c, n * (c + 1))), eng=e)
+        onat = R("psb", 0, L)
+        for c in range(NC):
+            mm(group(R("psb", CL * c, CL * (c + 1)), [(blk("ox", k), R("og", CW * c + k, CW * (c + 1), 16)) for k in range(16)]))
+        if last:
+            tt(R("dk1"), R("on0"), onat, ALU.add)
+            dma(T.yo[:], R("dk1"), 131072)
+        else:
+            lin(R("on0"), onat, eng="a")
+    return ops, Q
+
+
+def schedule(ops, noise=None):
+    n = len(ops)
+    deps = [list(o["deps"]) for o in ops]
+    users = [[] for _ in range(n)]
+    for i in range(n):
+        for j in deps[i]:
+            users[j].append(i)
+    prio = [0.0] * n
+    for i in range(n - 1, -1, -1):
+        o = ops[i]
+        own = min(c for c, _ in o["alts"].values()) + o["lat"] + (2000.0 if o["kind"] == "d" else 0.0)
+        prio[i] = own + max([prio[u] + SELF for u in users[i]] + [0.0])
+    if noise is not None:
+        prio = [p + x for p, x in zip(prio, noise)]
+    best = now = lay_out(ops, deps, users, prio, False)
+    for _ in range(PASSES):
+        back = lay_out(ops, users, deps, now[3], True)
+        now = lay_out(ops, deps, users, back[3], False)
+        if max(now[3]) < max(best[3]):
+            best = now
+    if "start" in FOUND:
+        return lay_out(ops, deps, users, [-s for s in FOUND["start"]], False)
+    rng = np.random.default_rng(SEED)
+    score = lambda s: max(s[3]) + 0.02 * sum(s[3]) / n
+    now = best
+    for k in range(TRIES):
+        at = np.array(now[2])
+        near = np.abs(at - rng.uniform(0, max(now[3]))) < (2000, 5000, 10000)[k % 3]
+        move = rng.normal(0, (300, 1000, 2500)[int(rng.integers(3))], n) * (rng.random(n) < 0.4) * near
+        s = lay_out(ops, deps, users, [float(x) for x in move - at], False)
+        if k % 10 == 9:
+            s = lay_out(ops, deps, users, lay_out(ops, users, deps, s[3], True)[3], False)
+        if score(s) <= score(now) + 30:
+            now = s
+        if max(s[3]) < max(best[3]):
+            best = s
+    if TRIES:
+        FOUND["start"] = best[2]
+    return best
+
+
+def lay_out(ops, deps, users, prio, back):
+    n = len(ops)
+    if not back:
+        prio = [p + o["early"] for p, o in zip(prio, ops)]
+    left = [len(d) for d in deps]
+    ready = [i for i in range(n) if left[i] == 0]
+    busy = {}
+    eng, fin, start = [None] * n, [0.0] * n, [0.0] * n
+
+    def gap(at, c, e, banks):
+        lanes = [(busy.setdefault(e, []), 0.0)] + [(busy.setdefault(b, []), HOP) for b in banks]
+        moved = True
+        while moved:
+            moved = False
+            for iv, pad in lanes:
+                for s, f, who in iv:
+                    if s - pad >= at + c:
+                        break
+                    if f + pad > at and (pad == 0.0 or who != e):
+                        at, moved = f + pad, True
+        return at
+
+    def put(key, item):
+        iv = busy.setdefault(key, [])
+        k = len(iv)
+        while k and iv[k - 1] > item:
+            k -= 1
+        iv.insert(k, item)
+
+    while ready:
+        i = max(ready, key=lambda x: (prio[x], -x))
+        o = ops[i]
+        cand = []
+        for e, (c, _) in o["alts"].items():
+            at = max([0.0] + [fin[j] + (HOP if eng[j] != e else SELF) for j in deps[i]])
+            if back:
+                at += o["lat"] + (2000.0 if o["kind"] == "d" else 0.0)
+            at = gap(at, max(c, 1.0), e, o["banks"])
+            cand.append((at + c, at, e))
+        end, at, e = min(cand)
+        eng[i], start[i] = e, at
+        for key in [e] + o["banks"]:
+            put(key, (at, max(end, at + 1.0), e))
+        if back:
+            fin[i] = end
+        elif o["kind"] == "d" and o["lat"] < 500.0:
+            fin[i] = end + 2000.0 + o["lat"]
+        elif o["kind"] == "d":
+            w = gap(end + 1300.0, o["lat"], "w", [])
+            put("w", (w, w + o["lat"], "w"))
+            fin[i] = w + o["lat"] + 700.0
+        else:
+            fin[i] = end + o["lat"]
+        ready.remove(i)
+        for u in users[i]:
+            left[u] -= 1
+            if left[u] == 0:
+                ready.append(u)
+    order = sorted(range(n), key=lambda x: (start[x], x))
+    return order, eng, start, fin
+
+
+def bank_order(ops, order, eng):
+    lastop = {}
+    for i in order:
+        for b in ops[i]["banks"]:
+            at = lastop.setdefault(b, {})
+            for e, j in at.items():
+                if e != eng[i]:
+                    ops[i]["deps"][j] = True
+            at[eng[i]] = i
+
+
+def rank_program(g, core, T, topo):
+    rank = T.rank_of(core)
+    if rank is None:
+        return
+    ops, Q = build(g, rank, T, topo)
+    order, eng, start, fin = schedule(ops)
+    bank_order(ops, order, eng)
+    need = [False] * len(ops)
+    for i, o in enumerate(ops):
+        o["wait"] = [j for j in o["deps"] if o["kind"] != "x"]
+        for j in o["wait"]:
+            need[j] = True
+    count, seen, top = {}, {}, {}
+    for i in order:
+        o, e = ops[i], eng[i]
+        if o["kind"] == "c" and need[i]:
+            count[e] = count.get(e, 0) + 1
+            o["sem"] = ("e" + e, count[e])
+        if o["sem"]:
+            top[o["sem"][0]] = o["sem"][1]
+        if o["kind"] == "x":
+            continue
+        want = {}
+        for j in o["wait"]:
+            s, c = ops[j]["sem"]
+            want[s] = max(want.get(s, 0), c)
+        for s, c in want.items():
+            if seen.get((e, s), 0) < c:
+                Q[e].wait_ge(T.sem[s], c)
+                seen[(e, s)] = c
+        ins = o["alts"][e][1](Q[e])
+        if o["kind"] == "d":
+            ins.then_inc(T.sem[o["sem"][0]], 16)
+        elif o["kind"] == "c" and need[i]:
+            ins.then_inc(T.sem[o["sem"][0]], 1)
+    for s, c in top.items():
+        if max(seen.get((e, s), 0) for e in Q) < c:
+            g.wait_ge(T.sem[s], c)

@@ -12,7 +12,7 @@ NC, NH = 4, 2
 CL, HL = L // NC, L // NH
 CW = 16 * CL
 TWICE = ("kf", "wexp", "cu", "kc", "chi", "clo", "pw", "z16", "d2")
-PASSES, TRIES, SEED, FOUND = 3, 600, 0, {}
+PASSES, TRIES, SEED, FOUND = 3, 1900, 0, {}
 
 SCRATCH = {
     "psw": ("psum", [128, 1024], "float32"), "psd": ("psum", [128, 1024], "float32"),
@@ -47,7 +47,7 @@ for _n, _c, _d in [
     ("nbe0", L, "bfloat16"), ("nbe1", L, "bfloat16"), ("nbn", L, "bfloat16"),
     ("nq", L, "bfloat16"), ("junk", L, "float32"), ("asum", 4, "float32"), ("ai", 4, "int32"), ("am", 4, "float32"),
     ("hb", NG, "bfloat16"), ("cnt", NG, "bfloat16"), ("q1", 60, "float32"), ("q2", 60, "float32"),
-    ("q3", 60, "float32"), ("qu", 60, "uint16"),
+    ("capc", 60, "bfloat16"), ("zi", L, "int32"), ("qu", 60, "uint16"),
     ("mir0", L + NG, "bfloat16"), ("mir1", L + NG, "bfloat16"), ("mir2", L + NG, "bfloat16"),
     ("mir3", L + NG, "bfloat16"), ("mir4", L + NG, "bfloat16"),
 ]:
@@ -56,16 +56,20 @@ for _n, _c, _d in [
 
 NDMA = 40
 SEMAPHORES = (["ev", "ea", "ep", "eg"] + ["d%d" % _i for _i in range(NDMA)]
-              + ["arr%d" % _i for _i in range(RO + 1)] + ["snt%d" % _i for _i in range(2 * RO + 2)])
+              + ["arr%d" % _i for _i in range(2 * RO + 2)] + ["snt%d" % _i for _i in range(2 * RO + 2)])
 
 SIZE = {"float32": 4, "int32": 4, "bfloat16": 2, "uint16": 2}
-CYC, PCYC, GATH = 1.04, 0.52, 1.56
+CYC, PCYC, GATH = 0.96, 0.48, 1.56
 FIX = {"v": 60.0, "a": 90.0, "p": 30.0, "g": 160.0, "s": 60.0}
 FO, EG, RB, SM = "avav", "aaaa", "vvvv", "a"
-ZA, AB, OG, INT1 = "v", "a", ["aaaaaaaa", "aaaaaaaa", "aaaaaaaa", "avavavav"], False
+ZA, AB, OG, INT1 = "a", "a", ["", "", "aaaavavv", "avavavav"], True
 EARLY = [0.0, 0.0, 0.0, 0.0]
-XG, PARTS, PARTS4 = "aaaa", [(0, 2), (2, 3), (3, 4)], [(0, 2), (2, 4)]
-HB, MG = ["aa", "aa", "aa", "av"], ["aa", "aa", "aa", "va"]
+PARTS, PARTS4 = [(0, 4), (4, 8)], [(0, 4), (4, 8)]
+CH2 = [(0, 1, "a"), (1, 2, "a"), (2, 4, "a"), (4, 6, "a"), (6, 8, "a")]
+CH3 = [(0, 2, "a"), (2, 4, "a"), (4, 6, "a"), (6, 8, "a")]
+SPEEDS = [(0.83, 1.1), (0.9, 1.56), (1.1, 1.3), (1.1, 2.0)]
+HB, MG = ["aa", "aa", "aa", "av"], ["aaaaa", "aaaaa", "aaaaa", "avava"]
+CH = "vvvv"
 COFF = 144.0 * 4096 - 2016
 HOP, SELF, SLACK = 120.0, 60.0, 250.0
 
@@ -78,8 +82,8 @@ def calls_of(T, topo, src, dests):
     ne = [e for e in topo.engines(me, T.cores[near[0][1]]) if e not in fe]
     hf, hn = len(fe) // 2, len(ne) // len(near)
     first = [(far[0][0], far[0][1], fe[:hf]), (far[1][0], far[1][1], fe[hf:])]
-    first += [(x[0], x[1], ne[hn * i:hn * (i + 1)]) for i, x in enumerate(near)]
-    return [first] + [[(x[0], x[1], fe)] for x in far[2:]]
+    second = [(far[2][0], far[2][1], fe)] + [(x[0], x[1], ne[hn * i:hn * (i + 1)]) for i, x in enumerate(near)]
+    return [first, second]
 
 
 def build(g, rank, T, topo):
@@ -117,7 +121,8 @@ def build(g, rank, T, topo):
             gr = 512 if name[:2] == "ps" else 16 // SIZE[SCRATCH[name][2]]
             hist[name].append((me, a, b, a // gr * gr, -(-b // gr) * gr, wr))
         banks = sorted(set((name, k) for (name, a, b), wr in acc if name[:2] == "ps" for k in range(a // 512, (b - 1) // 512 + 1)))
-        ops.append({"alts": alts, "deps": deps, "kind": kind, "lat": lat, "sem": sem, "banks": banks, "early": early[0]})
+        ops.append({"alts": alts, "deps": deps, "kind": kind, "lat": lat, "sem": sem, "banks": banks, "early": early[0],
+                    "ind": any(x.get("ind") for x in ins)})
         return me
 
     def one(x, *rest):
@@ -211,21 +216,21 @@ def build(g, rank, T, topo):
 
     def exchange(k, dests_of, src, dst):
         mine = []
-        for call in calls_of(T, topo, rank, dests_of(rank)):
+        for c, call in enumerate(calls_of(T, topo, rank, dests_of(rank))):
             sem = "snt%d" % nsnt[0]
             nsnt[0] += 1
             trs = []
             for d, r, es in call:
                 rid, pid, _ = topo.addr(T.cores[r])
                 trs.append(RemoteDMATransfer(dst_ids=[DstId(rid=rid, pnc=pid)], dma_engine_mask=sum(1 << e for e in es),
-                                             remote_sem=T.sem["arr%d" % k], src=src(d)["ap"], dst=dst(d)["ap"]))
+                                             remote_sem=T.sem["arr%d" % (2 * k + c)], src=src(d)["ap"], dst=dst(d)["ap"]))
             f = lambda q, trs=trs, sem=sem: q.remote_dma_fused(trs, local_sem=T.sem[sem])
             mine.append(add({"g": (900.0, f)}, [], [src(c[0]) for c in call], kind="r", lat=3500.0,
                             sem=(sem, sum(len(c[2]) for c in call))))
-        total = sum(len(es) for q in range(N) if q != rank
-                    for call in calls_of(T, topo, q, dests_of(q)) for d, r, es in call if r == rank)
-        return add({"x": (0.0, None)}, [dst(d) for d in range(N - 1)], [], kind="x", extra=mine, lat=1500.0,
-                   sem=("arr%d" % k, total))
+        for c in range(2):
+            got = [(d, len(es)) for q in range(N) if q != rank for d, r, es in calls_of(T, topo, q, dests_of(q))[c] if r == rank]
+            add({"x": (0.0, None)}, [dst(d) for d, n in got], [], kind="x", extra=mine, lat=1500.0,
+                sem=("arr%d" % (2 * k + c), sum(n for d, n in got)) if got else None)
 
     def lanes(name, m, a=0, b=L):
         o = m + (NG if name == "xw" else 0)
@@ -236,7 +241,8 @@ def build(g, rank, T, topo):
     blk = lambda name, k: R(name, 128 * k, 128 * (k + 1))
 
     dma(R("fi", p=P32), T.f0[:], 98304)
-    kts = [dma(R("kti", 1024 * j, 1024 * (j + 1)), T.kt[:, 1024 * j:1024 * (j + 1)], 524288, eng="sa"[j == 1]) for j in range(3)]
+    pieces = ((0, 1024), (1024, 2048), (2048, 2560), (2560, V))
+    kts = [dma(R("kti", a, b), T.kt[:, a:b], 512 * (b - a), eng="sa"[j % 2]) for j, (a, b) in enumerate(pieces)]
     dma(R("thi", p=P32), T.th[:], 16384, extra=kts[:1])
     dma(R("shi"), T.shw[:], 30720, extra=kts[:1])
     dma(R("xw", NG + V, NG + W), T.x0[:, V:W], 128 * NG * 2, extra=kts[1:2])
@@ -296,7 +302,9 @@ def build(g, rank, T, topo):
     fill(R("etab", V, W), -BIG)
     fill(R("etab", W, W + 16), 1.0)
     ts(R("base"), R("base"), pc(0), ALU.add)
-    tt(R("dlt"), R("shi"), R("base"), ALU.subtract)
+    lin(R("base"), R("base"), -1.0 / 64, eng="v")
+    lin(R("dlt"), R("shi"), -1.0 / 64, eng="v")
+    fill(R("capc"), -32.0 * (256 - CAP))
     lin(R("shu"), R("shi"), eng="v")
 
     lin(R("fb", p=P32), R("fi", p=P32), BIG, -BIG, eng="v")
@@ -309,7 +317,9 @@ def build(g, rank, T, topo):
                        R("fb", a - 768 * s, b - 768 * s, p=P32), True, True))
         mm(ms)
         lin(R("fout", 1024 * j, 1024 * (j + 1)), R(ps), 1.0 / BIG, 1.0, eng="a")
-        tt(R("etab", 1024 * j, 1024 * (j + 1)), R("kti", 1024 * j, 1024 * (j + 1)), R(ps), ALU.add)
+        for a, b in pieces:
+            if a // 1024 == j:
+                tt(R("etab", a, b), R("kti", a, b), R(ps, a - 1024 * j, b - 1024 * j), ALU.add)
     lin(R("thn", p=P32), R("thi", p=P32), -1.0, eng="v")
     lin(R("thh", p=P32), R("thn", p=P32))
     tt(R("thl", p=P32), R("thn", p=P32), R("thh", p=P32), ALU.subtract)
@@ -360,20 +370,17 @@ def build(g, rank, T, topo):
             if not late:
                 lin(R("kc", a, b), R("kf", a, b), 64.0, 16.0, eng=SM)
         for c0, c1 in PARTS:
-            a, b = CL * c0, CL * c1
-            for c in range(c0, c1):
-                w0, w1, ps = CW * c, CW * (c + 1), ("psx", "psw")[c % 2]
-                lin(R("eg", w0, w1), IND(R("etab"), R("cu", CL * c, CL * (c + 1))), 64.0, eng=EG[c])
-                mm([(R(ps, 512 * k + j, 512 * (k + 1), 8), blk("s1", j), R("wexp", 2 * CL * c + 64 * k, 2 * CL * c + 64 * (k + 1)), True, True)
-                    for k in range(CW // 512) for j in range(8)])
-                tt(R(tb, tb0 + w0, tb0 + w1), R("eg", w0, w1), R(ps, 0, CW), ALU.add)
-                if RB[c] == "v":
-                    ts(rb(16 + w0, 16 + w1), R(tb, tb0 + w0, tb0 + w1), 144.0 * U, ALU.max, 144.0 * U, ALU.subtract)
-                else:
-                    act(rb(16 + w0, 16 + w1), R(tb, tb0 + w0, tb0 + w1), AF.Relu, bias=-144.0 * U)
-                for k in range(CW // 512):
-                    x = w0 + 512 * k
-                    d0 = R("psd", 512 * k, 512 * (k + 1))
+            a, b = 32 * c0, 32 * c1
+            for u0, u1, e in [x for x in CH2 if c0 <= x[0] < c1]:
+                w0, w1, ps = 512 * u0, 512 * u1, ("psx", "psw")[u0 // 2 % 2]
+                lin(R("eg", w0, w1), IND(R("etab"), R("cu", 32 * u0, 32 * u1)), 64.0, eng=e)
+                mm([(R(ps, 512 * (k % 2) + j, 512 * (k % 2 + 1), 8), blk("s1", j), R("wexp", 64 * k, 64 * (k + 1)), True, True)
+                    for k in range(u0, u1) for j in range(8)])
+                tt(R(tb, tb0 + w0, tb0 + w1), R("eg", w0, w1), R(ps, w0 % CW, w0 % CW + w1 - w0), ALU.add)
+                ts(rb(16 + w0, 16 + w1), R(tb, tb0 + w0, tb0 + w1), 144.0 * U, ALU.max, 144.0 * U, ALU.subtract)
+                for k in range(u0, u1):
+                    x = 512 * k
+                    d0 = R("psd", x % CW, x % CW + 512)
                     mm(group(d0, [(R("idn"), R("cst")), (R("idn"), rb(x + 16, x + 528)), (R("nid"), rb(x + 15, x + 527))]))
                     scan(R("vs", x, x + 512), d0, R("eg", x, x + 512), 0.0, ALU.add, ALU.max)
             mm(group(R("psa", a, b), [(R("idn"), R("c29", 0, b - a))]
@@ -385,6 +392,15 @@ def build(g, rank, T, topo):
             ts(R(kn, a, b), R("za", a, b), 0.5 * MAGIC, ALU.add, 0.5 * MAGIC, ALU.subtract)
             for kk in range(2):
                 lin(R("w17", 2 * a + kk, 2 * b, 2), R("zf", a, b), pc(8 + kk), pc(10 + kk), eng=SM)
+            if INT1:
+                zi = R("zi", a, b)
+                tt(zi, R("own", a, b), R("psa", L + a, L + b), ALU.max)
+                ts(zi, zi, 6, ALU.arith_shift_right, 4095, ALU.bitwise_and)
+                if m:
+                    ts(R("own", a, b), zi, float(V), ALU.is_ge, -float(W), ALU.mult)
+                    tt(zi, zi, R("own", a, b), ALU.add)
+                lin(R("cu2", a, b), zi, 1.0, float(NG * m), eng="v")
+                continue
             mm(group(R("psa", a, b), [(R("n4k"), R("w17", 2 * a, 2 * b, 2)), (R("n4k"), R("w17", 2 * a + 1, 2 * b, 2)), (R("i32"), R(kn, a, b))]))
             if m:
                 ts(R("za", a, b), R("psa", a, b), float(V), ALU.is_ge, -float(W), ALU.mult)
@@ -417,17 +433,17 @@ def build(g, rank, T, topo):
             lin(R("d2"), p1, eng="a")
             lin(R("z16"), R("zf"), 1.0, 16.0, eng="a")
         early[0] = 0.0
-        for c in range(NC):
-            w0, w1, ps = CW * c, CW * (c + 1), ("psx", "psw")[c % 2]
-            lin(R(xg, xg0 + w0, xg0 + w1), IND(R("xw", NG * (1 - m), NG * (1 - m) + W), R("cu2", CL * c, CL * (c + 1))), eng=XG[c])
-            mm([(R(ps, 512 * k + j, 512 * (k + 1), 8), blk("s17", j), R("w17", 2 * CL * c + 64 * k, 2 * CL * c + 64 * (k + 1)), True, True)
-                for k in range(CW // 512) for j in range(8)])
-            mn = R("mn", CW * (c % 2), CW * (c % 2 + 1))
-            tt(mn, R(xg, xg0 + w0, xg0 + w1), R(ps, 0, CW), ALU.min)
-            scan(R("ys", w0, w1), R("rmask"), mn, 0.0, ALU.mult, ALU.max)
+        for u0, u1, e in CH3:
+            w0, w1, ps = 512 * u0, 512 * u1, ("psx", "psw")[u0 // 2 % 2]
+            lin(R(xg, xg0 + w0, xg0 + w1), IND(R("xw", NG * (1 - m), NG * (1 - m) + W), R("cu2", 32 * u0, 32 * u1)), eng=e)
+            mm([(R(ps, 512 * (k % 2) + j, 512 * (k % 2 + 1), 8), blk("s17", j), R("w17", 64 * k, 64 * (k + 1)), True, True)
+                for k in range(u0, u1) for j in range(8)])
+            mn = R("mn", w0 % (2 * CW), w0 % (2 * CW) + w1 - w0)
+            tt(mn, R(xg, xg0 + w0, xg0 + w1), R(ps, w0 % CW, w0 % CW + w1 - w0), ALU.min)
+            scan(R("ys", w0, w1), R("rmask", 0, w1 - w0), mn, 0.0, ALU.mult, ALU.max)
         mir, nxt = "mir%d" % t, "mir%d" % (t + 1)
         old, new = ("nbe%d" % m, "nbn") if late else (nbo, "nbe%d" % m)
-        for a, b in [(CL * c0, CL * c1) for c0, c1 in PARTS4]:
+        for a, b in [(32 * c0, 32 * c1) for c0, c1 in PARTS4]:
             y, xv = R("ys", 16 * a + 15, 16 * b, 16), lanes("xw", m, a, b)
             nb, dm, nx, ex = R("psd", a, b), R("psd", 512 + a, 512 + b), R("psx", 512 + a, 512 + b), R("psx", 768 + a, 768 + b)
             mm(group(dm, [(R("idn"), R("mh", 0, b - a)), (R("idn"), xv), (R("nid"), y)]))
@@ -455,9 +471,14 @@ def build(g, rank, T, topo):
                 lin(R(new, a, b), nb, eng=SM)
             if late:
                 lin(lanes("fout", m, a, b), nb, 1.0 / BIG, 1.0, eng=SM)
-            mm(group(ex, [(R("idn"), y), (R("nid"), xv), (R("idn"), R("ub", a, b))])
-               + group(nx, [(R("idn"), y), (R("idn"), R("ub", a, b))]))
-            act(R("chg", a, b), ex, AF.Abs)
+            if CH[t] == "a":
+                mm(group(ex, [(R("idn"), y), (R("nid"), xv), (R("idn"), R("ub", a, b))])
+                   + group(nx, [(R("idn"), y), (R("idn"), R("ub", a, b))]))
+                act(R("chg", a, b), ex, AF.Abs)
+            else:
+                mm(group(ex, [(R("idn"), xv), (R("nid"), y)]))
+                tt(R("chg", a, b), R("ub", a, b), ex, ALU.not_equal)
+                mm(group(nx, [(R("idn"), y), (R("idn"), R("ub", a, b))]))
             lin(R(mir, a, b), nx, eng="va" if last else SM)
             mm([(R("psa", a, b), R("bones"), R("chg", a, b), True, True)])
             act(R("chw", a, b), R("psa", a, b), AF.Sign)
@@ -474,18 +495,19 @@ def build(g, rank, T, topo):
             lin(R("hb", G * a, G * b), IND(R("chw"), R("shu", 12 * a, 12 * b)), eng=e)
             scan(R("cnt", G * a, G * b), R("bmask", G * a, G * b), R("hb", G * a, G * b), 0.0, ALU.mult, ALU.add)
         qp = R("psa", L, L + 60)
-        mm(group(qp, [(blk("dgb", k), R("hb", k, NG, 16)) for k in range(16)] + [(blk("dg", k), R("cnt", k, NG, 16)) for k in range(16)]))
-        ts(R("q1"), qp, 32.0 * (256 - CAP), ALU.is_ge)
-        tt(R("q2"), R("q1"), R("dlt"), ALU.mult)
-        tt(R("q3"), R("q2"), R("base"), ALU.add)
-        lin(R("qu"), R("q3"), eng="v")
-        for (a, b), e in zip(((0, 2), (2, 5)), MG[t]):
-            lin(R(nxt, L + G * a, L + G * b), IND(R(mir), R("qu", 12 * a, 12 * b)), eng=e)
+        mm(group(qp, [(R("idn"), R("capc"))] + [(blk("dgb", k), R("hb", k, NG, 16)) for k in range(16)]
+                 + [(blk("dg", k), R("cnt", k, NG, 16)) for k in range(16)]))
+        tt(R("q1"), R("dlt"), qp, ALU.min)
+        tt(R("q2"), R("q1"), R("base"), ALU.max)
+        lin(R("qu"), R("q2"), -64.0, eng="v")
+        down = lambda q: [(d, (q - 1 - d) % N) for d in range(N - 1)]
+        for (d, r, es), e in zip([x for call in calls_of(T, topo, rank, down(rank)) for x in call], MG[t]):
+            lin(R(nxt, L + G * d, L + G * (d + 1)), IND(R(mir), R("qu", 12 * d, 12 * (d + 1))), eng=e)
         g0 = (NG + V) * m
-        exchange(t, lambda q: [(d, (q - 1 - d) % N) for d in range(N - 1)],
-                 lambda d: R(nxt, L + G * d, L + G * (d + 1)), lambda d: R("xw", g0 + G * d, g0 + G * (d + 1)))
+        exchange(t, down, lambda d: R(nxt, L + G * d, L + G * (d + 1)), lambda d: R("xw", g0 + G * d, g0 + G * (d + 1)))
         if last:
-            dma(T.yx[:, V:W], R("xw", g0, g0 + NG), 128 * NG * 2)
+            for d in range(N - 1):
+                dma(T.yx[:, V + G * d:V + G * (d + 1)], R("xw", g0 + G * d, g0 + G * (d + 1)), 128 * G * 2, eng="sa"[d % 2])
             dma(T.yx[:, 0:V], R("xw", NG, NG + V), 128 * V * 2)
             dma(T.yf[:], R("fout", p=slice(0, 128, 16)), 98304)
             tt(R("dk0"), R("kn0"), R("kn1"), ALU.add)
@@ -535,8 +557,10 @@ def schedule(ops, noise=None):
     if "start" in FOUND:
         return lay_out(ops, deps, users, [-s for s in FOUND["start"]], False)
     rng = np.random.default_rng(SEED)
-    score = lambda s: max(s[3]) + 0.02 * sum(s[3]) / n
-    now = best
+    ends = lambda s: [replay(ops, deps, s[0], s[1], x) for x in SPEEDS]
+    unit = ends(best)
+    score = lambda s: sum(x / y for x, y in zip(ends(s), unit)) / len(unit)
+    now, sn, sb = best, 1.0, 1.0
     for k in range(TRIES):
         at = np.array(now[2])
         near = np.abs(at - rng.uniform(0, max(now[3]))) < (2000, 5000, 10000)[k % 3]
@@ -544,13 +568,42 @@ def schedule(ops, noise=None):
         s = lay_out(ops, deps, users, [float(x) for x in move - at], False)
         if k % 10 == 9:
             s = lay_out(ops, deps, users, lay_out(ops, users, deps, s[3], True)[3], False)
-        if score(s) <= score(now) + 30:
-            now = s
-        if max(s[3]) < max(best[3]):
-            best = s
+        x = score(s)
+        if x <= sn + 0.0003:
+            now, sn = s, x
+        if x < sb:
+            best, sb = s, x
     if TRIES:
         FOUND["start"] = best[2]
     return best
+
+
+def replay(ops, deps, order, eng, speed):
+    cyc, gath = speed
+    free, fin, bank, wire = {}, [0.0] * len(ops), {}, 0.0
+    for i in order:
+        o, e = ops[i], eng[i]
+        at = free.get(e, 0.0)
+        for j in deps[i]:
+            x = fin[j] + (HOP if eng[j] != e else SELF)
+            if x > at:
+                at = x
+        for b in o["banks"]:
+            for e2, x in bank.setdefault(b, {}).items():
+                if e2 != e and x + HOP > at:
+                    at = x + HOP
+        c = o["alts"][e][0]
+        if o["kind"] == "c":
+            c = FIX[e] + (c - FIX[e]) * cyc / CYC * (gath / GATH if o["ind"] else 1.0)
+        free[e] = at + c
+        for b in o["banks"]:
+            bank[b][e] = at + c
+        if o["kind"] == "d" and o["lat"] >= 500.0:
+            wire = max(wire, at + c + 1300.0) + o["lat"]
+            fin[i] = wire + 700.0
+        else:
+            fin[i] = at + c + o["lat"] + (2000.0 if o["kind"] == "d" else 0.0)
+    return max(fin)
 
 
 def lay_out(ops, deps, users, prio, back):
@@ -638,7 +691,8 @@ def rank_program(g, core, T, topo):
         o["wait"] = [j for j in o["deps"] if o["kind"] != "x"]
         for j in o["wait"]:
             need[j] = True
-    count, seen, top = {}, {}, {}
+    count, seen, top, known = {}, {}, {}, {}
+    place = {i: k for k, i in enumerate(order)}
     for i in order:
         o, e = ops[i], eng[i]
         if o["kind"] == "c" and need[i]:
@@ -648,14 +702,16 @@ def rank_program(g, core, T, topo):
             top[o["sem"][0]] = o["sem"][1]
         if o["kind"] == "x":
             continue
-        want = {}
-        for j in o["wait"]:
+        mine = known.setdefault(e, {})
+        for j in sorted(o["wait"], key=lambda x: -place[x]):
             s, c = ops[j]["sem"]
-            want[s] = max(want.get(s, 0), c)
-        for s, c in want.items():
-            if seen.get((e, s), 0) < c:
+            if mine.get(s, 0) < c:
                 Q[e].wait_ge(T.sem[s], c)
-                seen[(e, s)] = c
+                seen[(e, s)] = mine[s] = c
+                for s2, c2 in ops[j].get("knew", {}).items():
+                    if mine.get(s2, 0) < c2:
+                        mine[s2] = c2
+        o["knew"] = dict(mine)
         ins = o["alts"][e][1](Q[e])
         if o["kind"] == "d":
             ins.then_inc(T.sem[o["sem"][0]], 16)

@@ -6,13 +6,20 @@ from concourse.mybir import AluOpType as ALU, ActivationFunctionType as AF
 N, V, W, G, CAP, ST, L, RO = 6, 3072, 4032, 192, 48, 12, 256, 4
 NG = (N - 1) * G
 BIG = 131072.0
-U = 262144.0
-MAGIC = 25165824.0
+U = 65536.0
+OFF = 144 * U - 32256
+OWN = 7.75 / 16
+MAGIC = 12582912.0
+PAD = 8
 NC, NH = 4, 2
 CL, HL = L // NC, L // NH
 CW = 16 * CL
-TWICE = ("kf", "wexp", "cu", "kc", "chi", "clo", "pw", "z16", "d2")
-PASSES, TRIES, SEED, FOUND = 3, 1900, 0, {}
+TWICE = ("kf", "wexp", "cu", "keep", "chi", "clo", "pw", "fu", "kn", "ou")
+PASSES, TRIES, HEAT, MEAN, WINDOW, STAY, FIRST, SEED, FOUND = 3, 380000, 0.002, 2.0, 130, 400, 1000.0, 0, {}
+MF = {"i32": 1.0, "ni32": -1.0, "i16": 1.0 / 16, "ni16": -1.0 / 16}
+MB = {"idn": 1.0, "nid": -1.0, "n16": -1.0 / 16, "n4k": -4096.0, "nub": -0.5 / BIG, "p2b": 2 * BIG, "n2b": -2 * BIG}
+CM = {"flag": 32 * 136 * U, "up": 144 * 4096.0, "b2": None, "half": -0.5,
+      "own": OWN, "dk": -OWN / 16, "now": 14.5, "mi32": -MAGIC, "mni32": MAGIC, "mni16": MAGIC / 16, "m2": -2 * MAGIC}
 
 SCRATCH = {
     "psw": ("psum", [128, 1024], "float32"), "psd": ("psum", [128, 1024], "float32"),
@@ -20,34 +27,32 @@ SCRATCH = {
     "psb": ("psum", [128, 512], "float32"),
 }
 for _n, _c, _d in [
-    ("kti", V, "int32"), ("etab", W + 16, "float32"), ("xw", NG + W, "bfloat16"), ("fout", V, "float32"),
-    ("fi", 768, "int32"), ("fb", 768, "bfloat16"), ("thi", 128, "int32"), ("thh", 128, "bfloat16"),
+    ("kti", V, "int32"), ("etab", PAD + W, "float32"), ("xw0", W, "bfloat16"), ("xw1", W, "bfloat16"),
+    ("ff", 768, "float32"), ("fi", 768, "int32"), ("fb", 768, "bfloat16"), ("thi", 128, "int32"), ("thh", 128, "bfloat16"),
     ("thl", 128, "bfloat16"), ("thn", 128, "float32"), ("shi", 60, "int32"), ("shu", 60, "uint16"),
-    ("eg", 4096, "float32"), ("tb", 4096, "bfloat16"), ("rb", 4112, "bfloat16"), ("vs", 4096, "float32"),
+    ("eg", 4096, "float32"), ("wb", 4096, "bfloat16"), ("qb", 4112, "bfloat16"), ("vs", 4096, "float32"),
     ("xg", 4096, "bfloat16"), ("mn", 2 * CW, "bfloat16"), ("ys", 4096, "bfloat16"), ("og", 4096, "bfloat16"),
     ("wo", 33 * L, "bfloat16"), ("wk", 2048, "bfloat16"),
-    ("zr", 1024, "bfloat16"), ("sel4", 512, "bfloat16"), ("idn", 128, "bfloat16"), ("nid", 128, "bfloat16"),
-    ("bones", 128, "bfloat16"), ("s1", 1024, "bfloat16"), ("s17", 1024, "bfloat16"), ("dg", 2048, "bfloat16"),
-    ("dgb", 2048, "bfloat16"), ("ox", 2048, "bfloat16"), ("o16", 128, "bfloat16"), ("c29", L, "bfloat16"),
-    ("cst", 512, "bfloat16"), ("rmask", CW, "bfloat16"), ("bmask", NG, "bfloat16"),
-    ("pci", 4, "int32"), ("pc", 16, "float32"), ("j8", 8, "float32"), ("m8", 8, "float32"),
-    ("ib", L, "bfloat16"), ("vhi", L, "bfloat16"), ("i32", 128, "float32"), ("ni32", 128, "float32"),
-    ("m32", 128, "float32"), ("p32", 128, "bfloat16"), ("n4k", 128, "bfloat16"), ("n256", 128, "bfloat16"),
-    ("nbon", 128, "bfloat16"), ("mh", L, "bfloat16"),
-    ("vlo0", L, "bfloat16"), ("vlo1", L, "bfloat16"), ("base", 60, "float32"), ("dlt", 60, "float32"),
-    ("ci", L, "int32"), ("cu", L, "uint16"), ("wexp", 2 * L, "bfloat16"), ("kc", L, "float32"),
+    ("zr", 1024, "bfloat16"), ("sel4", 512, "bfloat16"), ("selt", 128, "bfloat16"),
+    ("mf", 128 * len(MF), "float32"), ("mb", 128 * len(MB), "bfloat16"), ("cm", 128 * len(CM), "bfloat16"),
+    ("bones", 128, "bfloat16"), ("s1", 1024, "bfloat16"), ("sd", 1024, "bfloat16"), ("s17", 1024, "bfloat16"),
+    ("sx", 128, "bfloat16"), ("s15", 128, "bfloat16"), ("mend", 128, "bfloat16"), ("dg", 2048, "bfloat16"),
+    ("dd", 2048 + 128, "bfloat16"), ("ox", 2048, "bfloat16"), ("o16", 128, "float32"), ("one", L, "bfloat16"),
+    ("rmask", CW, "bfloat16"), ("capt", G, "bfloat16"),
+    ("pci", 4, "int32"), ("pc", 24, "float32"), ("j8", 8, "float32"), ("m8", 12, "float32"), ("md8", 8, "float32"),
+    ("ib", L, "bfloat16"), ("vhi", L, "bfloat16"), ("vlo0", L, "bfloat16"), ("vlo1", L, "bfloat16"),
+    ("bhi", 60, "bfloat16"), ("blo", 60, "bfloat16"),
+    ("ci", L, "int32"), ("cu", L, "uint16"), ("wexp", 2 * L + 2, "bfloat16"),
     ("chi", L, "bfloat16"), ("clo", L, "bfloat16"), ("ohi", L, "bfloat16"), ("olo", L, "bfloat16"),
-    ("own", L, "float32"), ("za", L, "float32"), ("cu2", L, "uint16"),
-    ("w17", 2 * L, "bfloat16"), ("kn0", L, "float32"), ("kn1", L, "float32"), ("kf", L, "float32"), ("zf", L, "float32"),
-    ("ou", L, "uint16"),
-    ("on0", L, "float32"), ("fu0", L, "uint16"), ("fu1", L, "uint16"), ("dk0", L, "float32"), ("dk1", L, "float32"),
-    ("pw", L, "bfloat16"), ("z16", L, "float32"), ("d2", L, "float32"), ("bit", L, "int32"),
-    ("ub", L, "bfloat16"), ("rl", L, "bfloat16"), ("a2", L, "float32"), ("hd", L, "float32"),
-    ("chg", L, "bfloat16"), ("chw", L, "bfloat16"), ("nbo0", L, "bfloat16"), ("nbo1", L, "bfloat16"),
-    ("nbe0", L, "bfloat16"), ("nbe1", L, "bfloat16"), ("nbn", L, "bfloat16"),
-    ("nq", L, "bfloat16"), ("junk", L, "float32"), ("asum", 4, "float32"), ("ai", 4, "int32"), ("am", 4, "float32"),
-    ("hb", NG, "bfloat16"), ("cnt", NG, "bfloat16"), ("q1", 60, "float32"), ("q2", 60, "float32"),
-    ("capc", 60, "bfloat16"), ("zi", L, "int32"), ("qu", 60, "uint16"),
+    ("own", L, "float32"), ("cu2", L, "uint16"), ("w17", 2 * L, "bfloat16"),
+    ("kn", L, "float32"), ("kf", L, "float32"), ("kg", L, "float32"), ("zf", L, "float32"), ("pk", L, "float32"),
+    ("ou", L, "uint16"), ("oc", L, "bfloat16"), ("oa", L, "bfloat16"), ("slot", L, "bfloat16"), ("self", L, "bfloat16"),
+    ("on0", L, "float32"), ("fu", L, "uint16"), ("yks", L, "float32"), ("yos", L, "float32"),
+    ("pw", L, "bfloat16"), ("keep", L, "bfloat16"), ("bit", L, "int32"), ("a2", L, "float32"),
+    ("ub", L, "bfloat16"), ("rl", L, "bfloat16"), ("chg", L, "bfloat16"), ("chw", L, "bfloat16"),
+    ("new0", L, "bfloat16"), ("new1", L, "bfloat16"), ("new2", L, "bfloat16"), ("new3", L, "bfloat16"),
+    ("junk", L, "bfloat16"), ("asum", 4, "float32"), ("ai", 4, "int32"), ("am", 4, "float32"),
+    ("hb", NG, "bfloat16"), ("cnt", NG, "bfloat16"), ("q1", 60, "float32"), ("qu", 60, "uint16"),
     ("mir0", L + NG, "bfloat16"), ("mir1", L + NG, "bfloat16"), ("mir2", L + NG, "bfloat16"),
     ("mir3", L + NG, "bfloat16"), ("mir4", L + NG, "bfloat16"),
 ]:
@@ -61,17 +66,19 @@ SEMAPHORES = (["ev", "ea", "ep", "eg"] + ["d%d" % _i for _i in range(NDMA)]
 SIZE = {"float32": 4, "int32": 4, "bfloat16": 2, "uint16": 2}
 CYC, PCYC, GATH = 0.96, 0.48, 1.56
 FIX = {"v": 60.0, "a": 90.0, "p": 30.0, "g": 160.0, "s": 60.0}
-FO, EG, RB, SM = "avav", "aaaa", "vvvv", "a"
-ZA, AB, OG, INT1 = "a", "a", ["", "", "aaaavavv", "avavavav"], True
-EARLY = [0.0, 0.0, 0.0, 0.0]
-PARTS, PARTS4 = [(0, 4), (4, 8)], [(0, 4), (4, 8)]
-CH2 = [(0, 1, "a"), (1, 2, "a"), (2, 4, "a"), (4, 6, "a"), (6, 8, "a")]
-CH3 = [(0, 2, "a"), (2, 4, "a"), (4, 6, "a"), (6, 8, "a")]
-SPEEDS = [(0.83, 1.1), (0.9, 1.56), (1.1, 1.3), (1.1, 2.0)]
-HB, MG = ["aa", "aa", "aa", "av"], ["aaaaa", "aaaaa", "aaaaa", "avava"]
-CH = "vvvv"
-COFF = 144.0 * 4096 - 2016
-HOP, SELF, SLACK = 120.0, 60.0, 250.0
+PAR = {
+    "fo": "avav", "int1": True, "h2": "aavv", "chg": "vvvv", "kn": "vvvv", "et": "vvvv", "lo": "v",
+    "og": ["", "", ["a", "va"] * 4, ["va"] * 8],
+    "parts": [[(0, 4), (4, 6), (6, 8)]] * 4, "parts4": [(0, 4), (4, 8)],
+    "ch2": [(0, 1, "a", "g"), (1, 2, "a", "g"), (2, 4, "a", "g"), (4, 6, "a", ["g", "ga"]), (6, 8, "a", ["g", "ga"])],
+    "ch3": [(0, 2, "a"), (2, 4, "a"), (4, 6, "a"), (6, 7, "a"), (7, 8, "va")],
+    "hb": [[(0, 2, "va"), (2, 5, "va")]] * 4, "qp": [[(0, 5)]] * 3 + [[(0, 2), (2, 5)]],
+    "mg": [[(0, 2, "va"), (2, 5, "va")]] * 3 + [[(0, 1, "va"), (1, 2, "va"), (2, 4, "va"), (4, 5, "va")]],
+}
+REACH, EACH = 50.0, 5.0
+SPEEDS = [{"cyc": 1.0, "gath": 1.75, "issue": 1.0, "far": 1.0, "dma": 1.0, "fix": 1.0},
+          {"cyc": 0.87, "gath": 1.25, "issue": 2.0, "far": 1.6, "dma": 0.55, "fix": 1.6}]
+HOP, SELF = 120.0, 60.0
 
 
 def calls_of(T, topo, src, dests):
@@ -87,7 +94,7 @@ def calls_of(T, topo, src, dests):
 
 
 def build(g, rank, T, topo):
-    ops, hist, cls, early = [], {}, [0], [0.0]
+    ops, hist, cls = [], {}, [0]
     Q = {"v": g.vector, "a": g.scalar, "p": g.tensor, "g": g, "s": g.sync}
 
     def R(name, a=0, b=None, s=1, p=None):
@@ -121,7 +128,7 @@ def build(g, rank, T, topo):
             gr = 512 if name[:2] == "ps" else 16 // SIZE[SCRATCH[name][2]]
             hist[name].append((me, a, b, a // gr * gr, -(-b // gr) * gr, wr))
         banks = sorted(set((name, k) for (name, a, b), wr in acc if name[:2] == "ps" for k in range(a // 512, (b - 1) // 512 + 1)))
-        ops.append({"alts": alts, "deps": deps, "kind": kind, "lat": lat, "sem": sem, "banks": banks, "early": early[0],
+        ops.append({"alts": alts, "deps": deps, "kind": kind, "lat": lat, "sem": sem, "banks": banks,
                     "ind": any(x.get("ind") for x in ins)})
         return me
 
@@ -144,8 +151,9 @@ def build(g, rank, T, topo):
         return (FIX["a"] + max(64.0, in_["n"] * (GATH if in_["ind"] else 1.0)) * CYC,
                 lambda q: q.activation(out["ap"], in_["ap"], func, **kw))
 
-    def act(out, in_, func, bias=None, scale=None, accum=None):
-        return add({"a": act_alt(out, in_, func, bias, scale, accum)}, [out] + ([accum] if accum else []), [in_])
+    def act(out, in_, func, bias=None, scale=None, accum=None, table=0.0):
+        c, f = act_alt(out, in_, func, bias, scale, accum)
+        return add({"a": (c + table, f)}, [out] + ([accum] if accum else []), [in_])
 
     def tt(out, a, b, op):
         k = 1.0 if (a["ps"] or b["ps"]) else 2.0
@@ -168,12 +176,15 @@ def build(g, rank, T, topo):
             if scale is None and bias is None:
                 f = lambda q: q.tensor_copy(out["ap"], a["ap"])
             elif bias is None:
-                f = lambda q: q.tensor_scalar(out["ap"], a["ap"], scale, None, ALU.mult)
+                f = lambda q: q.tensor_scalar(out["ap"], a["ap"], val(scale), None, ALU.mult)
             else:
                 f = lambda q: q.tensor_scalar(out["ap"], a["ap"], val(scale), val(bias), ALU.mult, ALU.add)
             alts["v"] = (vc(out["n"], one(a, out)), f)
         if "a" in eng:
             alts["a"] = act_alt(out, a, AF.Copy if bias is None else AF.Identity, val(bias), val(scale))
+        if "g" in eng:
+            alts["g"] = (FIX["g"] + 2 * out["n"] * CYC,
+                         lambda q: q.affine_select(out["ap"], a["ap"], [[0, out["n"]]], ALU.is_ge, 0.0, 0, 0))
         return add(alts, [out], [a] + [s for s in (scale, bias) if isinstance(s, dict)])
 
     def scan(out, d0, d1, init, op0, op1):
@@ -188,7 +199,7 @@ def build(g, rank, T, topo):
             for o, l, r, st, sp in ms:
                 last = q.matmul(o["ap"], l["ap"], r["ap"], st, sp)
             return last
-        cost = FIX["p"] + sum(max(64, m[0]["n"]) * PCYC * (4 if m[2]["b"] == 4 else 1) + 4.0 for m in ms)
+        cost = FIX["p"] + sum(max(64, m[0]["n"]) * PCYC * (4 if m[2]["b"] == 4 else 1) + EACH for m in ms)
         return add({"p": (cost, f)}, [m[0] for m in ms], [m[1] for m in ms] + [m[2] for m in ms])
 
     def group(out, pairs):
@@ -223,296 +234,351 @@ def build(g, rank, T, topo):
             for d, r, es in call:
                 rid, pid, _ = topo.addr(T.cores[r])
                 trs.append(RemoteDMATransfer(dst_ids=[DstId(rid=rid, pnc=pid)], dma_engine_mask=sum(1 << e for e in es),
-                                             remote_sem=T.sem["arr%d" % (2 * k + c)], src=src(d)["ap"], dst=dst(d)["ap"]))
+                                             remote_sem=T.sem["arr%d" % (2 * k + c)], src=src(d)["ap"], dst=dst(d, r)["ap"]))
             f = lambda q, trs=trs, sem=sem: q.remote_dma_fused(trs, local_sem=T.sem[sem])
             mine.append(add({"g": (900.0, f)}, [], [src(c[0]) for c in call], kind="r", lat=3500.0,
                             sem=(sem, sum(len(c[2]) for c in call))))
         for c in range(2):
             got = [(d, len(es)) for q in range(N) if q != rank for d, r, es in calls_of(T, topo, q, dests_of(q))[c] if r == rank]
-            add({"x": (0.0, None)}, [dst(d) for d, n in got], [], kind="x", extra=mine, lat=1500.0,
+            add({"x": (0.0, None)}, [dst(d, rank) for d, n in got], [], kind="x", extra=mine[:c + 1], lat=1500.0,
                 sem=("arr%d" % (2 * k + c), sum(n for d, n in got)) if got else None)
 
+    down = lambda q: [(d, (q - 1 - d) % N) for d in range(N - 1)]
+    turn = lambda q: [x[0] for call in calls_of(T, topo, q, down(q)) for x in call]
+    place = lambda q, d: (L + G * turn(q).index(d), L + G * (turn(q).index(d) + 1))
+
     def lanes(name, m, a=0, b=L):
-        o = m + (NG if name == "xw" else 0)
+        o = m + (PAD if name == "etab" else 0)
         return R(name, ST * a + o, ST * (b - 1) + o + 1, ST)
 
     P32 = slice(0, 32)
     pc = lambda j: R("pc", j, j + 1)
-    blk = lambda name, k: R(name, 128 * k, 128 * (k + 1))
+    blk = lambda name, k, p=None: R(name, 128 * k, 128 * (k + 1), p=p)
+
+    def M(name, p=None):
+        for buf, tab in (("mf", MF), ("mb", MB), ("cm", CM)):
+            if name in tab:
+                return blk(buf, list(tab).index(name), p)
+
+    K = lambda name, n: (M(name), R("one", 0, n))
+    H = [(HL * h, HL * (h + 1)) for h in range(NH)]
 
     dma(R("fi", p=P32), T.f0[:], 98304)
     pieces = ((0, 1024), (1024, 2048), (2048, 2560), (2560, V))
     kts = [dma(R("kti", a, b), T.kt[:, a:b], 512 * (b - a), eng="sa"[j % 2]) for j, (a, b) in enumerate(pieces)]
-    dma(R("thi", p=P32), T.th[:], 16384, extra=kts[:1])
-    dma(R("shi"), T.shw[:], 30720, extra=kts[:1])
-    dma(R("xw", NG + V, NG + W), T.x0[:, V:W], 128 * NG * 2, extra=kts[1:2])
-    dma(R("xw", NG, NG + V), T.x0[:, 0:V], 128 * V * 2, extra=kts)
+    dma(R("xw0", V, W), T.x0[:, V:W], 128 * NG * 2, extra=kts[2:3])
+    x0 = dma(R("xw0", 0, V), T.x0[:, 0:V], 128 * V * 2, extra=kts[2:3])
+    dma(R("thi", p=P32), T.th[:], 16384, extra=[x0])
+    for e, d in enumerate(turn(rank)):
+        dma(R("shi", 12 * e, 12 * (e + 1)), T.shw[:, 12 * d:12 * (d + 1)], 6144, extra=[x0])
+    dma(R("xw1", 0, V), T.x0[:, 0:V], 128 * V * 2, extra=[x0])
 
     fill(R("zr", 0, 512), 0.0)
     fill(R("zr", 512, 1024), 0.0)
+    fill(R("one"), 1.0)
     asel(R("sel4", p=P32), R("zr", 0, 512, p=P32), [[-1, 4], [-4, 8], [0, 16]], ALU.not_equal, 1.0, 0, 1)
+    asel(R("selt"), R("zr", 0, 128), [[-256, 4], [-16, 8], [256, 4]], ALU.not_equal, 1.0, 0, 1)
     iota(R("pci", 0, 1), [[0, 1]], 0, 1)
     iota(R("j8"), [[1, 8]], 0, 0)
     asel(R("bones"), R("zr", 0, 128), [[-16, 8], [0, 16]], ALU.is_ge, 1.0, -16, 1)
     asel(R("bones"), R("bones"), [[-16, 8], [0, 16]], ALU.is_ge, 0.0, 0, 1)
-    asel(R("idn"), R("zr", 0, 128), [[-1, 128]], ALU.not_equal, 1.0, 0, 1)
-    asel(R("nid"), R("zr", 0, 128), [[-1, 128]], ALU.not_equal, -1.0, 0, 1)
+    asel(M("idn"), R("zr", 0, 128), [[-1, 128]], ALU.not_equal, 1.0, 0, 1)
+    for name, c in list(MB.items())[1:] + list(MF.items()):
+        lin(M(name), M("idn"), c, eng="a")
+    for k in range(16):
+        asel(blk("wk", k), R("zr", 0, 128), [[-1, 128]], ALU.not_equal, 2.0 ** (k - 1) * (1.0 if k == 15 else -1.0), 0, 1)
+    for name, c in CM.items():
+        if name in ("flag", "up"):
+            lin(M(name), R("one", 0, 128), c / 128, eng="a")
+        elif c is not None:
+            asel(M(name), R("zr", 0, 128), [[0, 128]], ALU.not_equal, c / 128, 0, 0)
+    fill(M("b2", slice(0, 64)), 2016.0 / 64)
+    fill(M("b2", slice(64, 128)), -OWN / 64)
+    asel(R("o16"), R("zr", 0, 128), [[0, 128]], ALU.not_equal, 0.0625, 0, 0)
     for hh in range(2):
-        asel(R("dg", 1024 * hh, 1024 * (hh + 1)), R("zr"), [[-256, 8], [-16, 8], [255, 16]], ALU.not_equal, -32.0, -2048 * hh, 1)
-    iota(R("base"), [[16, 60]], L, 0)
+        cols, z = (1024 * hh, 1024 * (hh + 1)), R("zr")
+        asel(R("dg", *cols), z, [[-256, 8], [-16, 8], [255, 16]], ALU.not_equal, -32.0, -2048 * hh, 1)
+        asel(R("dd", *cols), R("dg", *cols), [[-256, 8], [-16, 8], [255, 16]], ALU.not_equal, 32.0, -2048 * hh - 256, 1)
+        asel(R("ox", *cols), z, [[-256, 8], [-16, 8], [256, 16]], ALU.not_equal, 1.0, -2048 * hh, 1)
+        asel(R("ox", *cols), R("ox", *cols), [[-256, 8], [-16, 8], [256, 16]], ALU.not_equal, 1.0, -2048 * hh - 1, 1)
+    asel(blk("dd", 16), R("zr", 0, 128), [[-16, 8], [255, 16]], ALU.not_equal, 32.0, 0, 1)
+    iota(R("bhi"), [[16, 60]], L, 0)
     for m in range(2):
         iota(R("vlo%d" % m), [[0, 16], [ST, 16]], m, 0)
     iota(R("vhi"), [[16 * ST, 16], [0, 16]], 0, 0)
     iota(R("ib"), [[1, L]], 0, 0)
-    for name, c in (("i32", 1.0), ("p32", 1.0 / 64), ("n4k", -4096.0), ("ni32", -1.0), ("m32", -64.0), ("n256", -1.0 / L)):
-        lin(R(name), R("idn"), c, eng="a")
-    for k in range(16):
-        lin(blk("wk", k), R("idn"), 2.0 ** (k - 1) * (1.0 if k == 15 else -1.0))
-    lin(R("nbon"), R("bones"), -1.0, eng="a")
-    fill(R("mh"), -0.5)
-    for hh in range(2):
-        o, z = R("ox", 1024 * hh, 1024 * (hh + 1)), R("zr", 0, 1024)
-        asel(o, z, [[-256, 8], [-16, 8], [256, 16]], ALU.not_equal, 1.0, -2048 * hh, 1)
-        asel(o, o, [[-256, 8], [-16, 8], [256, 16]], ALU.not_equal, 1.0, -2048 * hh - 1, 1)
-        asel(R("dgb", 1024 * hh, 1024 * (hh + 1)), z, [[-256, 8], [-16, 8], [255, 16]], ALU.not_equal, 8192.0, -2048 * hh, 1)
+    asel(R("rmask"), R("zr"), [[0, CL], [-1, 16]], ALU.is_ge, 1.0, 0, 0)
+    asel(R("capt"), R("zr", 0, G), [[0, G]], ALU.not_equal, 64.0 * CAP, 0, 0)
     ts(R("pci", 1, 2), R("pci", 0, 1), 15, ALU.bitwise_and)
     ts(R("pci", 2, 3), R("pci", 0, 1), 7, ALU.bitwise_and)
     lin(R("pc", 0, 2), R("pci", 1, 3), eng="v")
     ts(pc(2), pc(0), 8.0, ALU.is_lt)
     ts(pc(3), pc(0), 8.0, ALU.is_ge)
-    lin(R("pc", 4, 6), R("pc", 2, 4), -64.0, eng="v")
-    lin(R("pc", 6, 8), R("pc", 2, 4), U * (144 + 63.0 / 64), -U * 63 / 128, eng="v")
-    lin(R("pc", 8, 10), R("pc", 2, 4), 1.0 / U, eng="v")
-    lin(R("pc", 10, 12), R("pc", 2, 4), 255.5078125, -128.0, eng="v")
-    ts(R("m8"), R("j8"), pc(1), ALU.is_equal)
+    lin(R("pc", 4, 6), R("pc", 2, 4), 16.0, eng="v")
+    ts(pc(12), pc(5), pc(0), ALU.subtract, -1.0, ALU.add)
+    lin(R("pc", 6, 8), R("pc", 2, 4), -1.0, 1.0, eng="v")
+    ts(R("pc", 6, 8), R("pc", 6, 8), pc(12), ALU.mult)
+    lin(R("pc", 16, 18), R("pc", 2, 4), OFF, eng="v")
+    tt(R("pc", 6, 8), R("pc", 6, 8), R("pc", 16, 18), ALU.add)
+    lin(R("pc", 8, 10), R("pc", 2, 4), 1.0 / 4096, eng="v")
+    lin(R("pc", 10, 12), R("pc", 2, 4), 288.0 - 63.0 / 128, -144.0, eng="v")
+    lin(pc(13), pc(12), 1.0 / 16, -OWN, eng="v")
+    ts(R("mend"), M("idn"), pc(13), ALU.mult)
+    fill(R("m8", 0, 1), 0.0)
+    ts(R("m8", 1, 9), R("j8"), pc(1), ALU.is_equal)
+    tt(R("md8"), R("m8", 0, 8), R("m8", 1, 9), ALU.subtract)
+    ts(pc(18), pc(3), -3.0, ALU.mult, 1.0, ALU.add)
     for j in range(8):
-        ts(blk("s1", j), R("bones"), R("m8", j, j + 1), ALU.mult)
+        lin(blk("s1", j), R("bones"), R("m8", j + 1, j + 2))
+        lin(blk("sd", j), R("bones"), R("md8", j, j + 1))
+    lin(R("sx"), blk("s1", 7), pc(18))
+    lin(pc(19), pc(2), 18 * 4096.0 - 1.0 / 16, 1.0 / 16, eng="v")
+    lin(R("s15"), blk("s1", 7), pc(19))
     lin(R("s17"), R("s1"), 17.0)
-    fill(R("o16"), 0.0625)
-    fill(R("c29"), 32 * 128 * U)
-    fill(R("cst"), 1.0)
-    fill(R("cst", 0, 512, 16), -128 * U)
-    fill(R("rmask"), 1.0)
-    fill(R("rmask", 0, CW, 16), 0.0)
-    fill(R("bmask"), 1.0)
-    fill(R("bmask", 0, NG, G), 0.0)
-    fill(R("rb", 0, 16), 0.0)
+    fill(R("qb", 0, 16), 0.0)
     fill(R("wo", 4096, 4112), 0.0)
     fill(R("wo", 8208, 33 * L), 0.0)
-    fill(R("etab", V, W), -BIG)
-    fill(R("etab", W, W + 16), 1.0)
-    ts(R("base"), R("base"), pc(0), ALU.add)
-    lin(R("base"), R("base"), -1.0 / 64, eng="v")
-    lin(R("dlt"), R("shi"), -1.0 / 64, eng="v")
-    fill(R("capc"), -32.0 * (256 - CAP))
+    lin(R("etab", PAD + V, PAD + W), R("zr", 0, NG), 1.0, -BIG, eng="a")
+    fill(R("etab", 0, PAD), 1.0)
+    ts(R("blo"), R("one", 0, 60), pc(0), ALU.mult)
     lin(R("shu"), R("shi"), eng="v")
 
     lin(R("fb", p=P32), R("fi", p=P32), BIG, -BIG, eng="v")
+    lin(R("ff", p=P32), R("fi", p=P32), eng="g")
     for j, ps in enumerate(("psw", "psd", "psx")):
         cuts = sorted(set([1024 * j, 1024 * j + 512, 1024 * j + 1024] + [c for c in range(0, V, 768) if 1024 * j < c < 1024 * j + 1024]))
         ms = []
         for a, b in zip(cuts[:-1], cuts[1:]):
             s = a // 768
-            ms.append((R(ps, a - 1024 * j, b - 1024 * j), R("sel4", 128 * s, 128 * (s + 1), p=P32),
-                       R("fb", a - 768 * s, b - 768 * s, p=P32), True, True))
+            ms.append((R(ps, a - 1024 * j, b - 1024 * j), blk("sel4", s, P32), R("fb", a - 768 * s, b - 768 * s, p=P32), True, True))
         mm(ms)
-        lin(R("fout", 1024 * j, 1024 * (j + 1)), R(ps), 1.0 / BIG, 1.0, eng="a")
         for a, b in pieces:
             if a // 1024 == j:
-                tt(R("etab", a, b), R("kti", a, b), R(ps, a - 1024 * j, b - 1024 * j), ALU.add)
+                tt(R("etab", PAD + a, PAD + b), R("kti", a, b), R(ps, a - 1024 * j, b - 1024 * j), ALU.add)
     lin(R("thn", p=P32), R("thi", p=P32), -1.0, eng="v")
-    lin(R("thh", p=P32), R("thn", p=P32))
+    lin(R("thh", p=P32), R("thn", p=P32), eng="g")
     tt(R("thl", p=P32), R("thn", p=P32), R("thh", p=P32), ALU.subtract)
-    for m in range(2):
-        lin(R("nbo%d" % m), lanes("fout", m), BIG, -BIG)
 
     exchange(RO, lambda q: [(d, (q + 1 + d) % N) for d in range(N - 1)],
-             lambda d: R("xw", NG + V + G * d, NG + V + G * (d + 1)), lambda d: R("mir0", L + G * d, L + G * (d + 1)))
+             lambda d: R("xw0", V + G * d, V + G * (d + 1)), lambda d, r: R("mir0", *place(r, d)))
+
+    def master(kf, a, b):
+        return [(M("n16"), R("wexp", 2 + 2 * a, 2 + 2 * b, 2)), (M("n16"), R("wexp", 3 + 2 * a, 2 + 2 * b, 2)), K("up", b - a),
+                (M("i32"), R(kf, a, b)), (R("mend"), R("one", 0, b - a))]
+
+    def entries(kf, hi, lo, direct):
+        for a, b in H:
+            for kk in range(2):
+                lin(R("wexp", 2 + 2 * a + kk, 2 + 2 * b, 2), R(kf, a, b), pc(4 + kk), pc(6 + kk), eng="a")
+            if not direct:
+                mm(group(R("psb", a, b), master(kf, a, b)))
+                lin(R("cu", a, b), R("psb", a, b), eng="v")
+        if direct:
+            mm(group(R("psb", 0, L), master(kf, 0, L)))
+        lin(R(hi), R("psb", 0, L), eng="a")
+        if PAR["lo"] == "v":
+            tt(R(lo), R("psb", 0, L), R(hi), ALU.subtract)
+        else:
+            mm(group(R("psb", L, 2 * L), master(kf, 0, L) + [(M("nid"), R(hi))]))
+            lin(R(lo), R("psb", L, 2 * L), eng="a")
+
+    lifted = {}
+
+    def whole(times, kn, a, b):
+        return [(M(times), R(kn, a, b))] + ([K("m" + times, b - a)] if lifted[R(kn)["reg"][0][0]] else [])
+
+    def origins(ps, at):
+        for a, b in H:
+            mm(group(R(ps, at + a, at + b), [(blk("ox", k), R("og", 16 * a + k, 16 * b, 16)) for k in range(16)]))
+
+    for m in range(2):
+        cls[0] = m
+        fill(R("wexp", 0, 2), 0.0)
+        for a, b in H:
+            lin(R("kf", a, b), lanes("kti", m, a, b), 1.0, OWN, eng="v")
+        entries("kf", "chi", "clo", False)
+        both = [(M("idn"), R("chi")), (M("idn"), R("clo"))]
+        mm(group(R("psb", 0, L), both + [(M("nid"), R("vhi")), (M("nid"), R("vlo%d" % m))]))
+        ts(R("self"), R("psb", 0, L), 0.0, ALU.is_equal, -8192.0, ALU.mult)
+        mm(group(R("psb", L, 2 * L), both + [(M("idn"), R("self"))]))
+        ts(R("fu"), R("psb", L, 2 * L), float(PAD), ALU.add, 0.0, ALU.max)
 
     for t in range(RO):
         m, late, last = t % 2, t >= 2, t == RO - 1
-        cls[0], early[0] = m, 0.0
-        kn, dk, fu, nbo = ["%s%d" % (x, m) for x in ("kn", "dk", "fu", "nbo")]
-        tb, tb0 = ("wo", 0) if t == 0 else ("tb", 0)
-        xg, xg0 = "xg", 0
-        rb = (lambda a, b, s=1: R("wo", 4096 + a, 4096 + b, s)) if t == 0 else (lambda a, b, s=1: R("rb", a, b, s))
-        H = [(HL * h, HL * (h + 1)) for h in range(NH)]
+        cls[0] = m
+        kf, xw, new = "kg" if late else "kf", "xw%d" % m, "new%d" % t
+        wb = (lambda a, b, s=1: R("wo", a, b, s)) if t == 0 else (lambda a, b, s=1: R("wb", a, b, s))
+        qb = (lambda a, b, s=1: R("wo", 4096 + a, 4096 + b, s)) if t == 0 else (lambda a, b, s=1: R("qb", a, b, s))
+        code = lambda a, b: whole("ni32", "kn", a, b) + [(M("i32"), R("zf", a, b))]
         if late:
+            mm(group(R("psw", 0, L), whole("ni16", "kn", 0, L) + [(M("i16"), R("kf")), K("dk", L)]))
+            mm(group(R("psw", 2 * L, 3 * L), [(M("nid"), R("new%d" % m)), K("own", L)]))
             for c in range(NC):
-                out, src = R("xg", CW * c, CW * (c + 1)), IND(R("etab"), R(fu, CL * c, CL * (c + 1)))
-                if FO[c] == "a":
+                out, src = R("xg", CW * c, CW * (c + 1)), IND(R("etab"), R("fu", CL * c, CL * (c + 1)))
+                if PAR["fo"][c] == "a":
                     act(out, src, AF.Sign, bias=0.5)
                 else:
                     ts(out, src, 0.0, ALU.is_lt, -2.0, ALU.mult)
-                mm(group(R("psw", CL * c, CL * (c + 1)), [(blk("wk", k), R("xg", CW * c + k, CW * (c + 1), 16)) for k in range(16)]
-                         + ([(R("idn"), R("mh", 0, CL))] if FO[c] == "a" else [])))
+                if c % 2:
+                    wd = R("psx", L + CL * (c - 1), L + CL * (c + 1))
+                    mm([(wd, blk("wk", k), R("xg", CW * (c - 1) + k, CW * (c + 1), 16), k == 0, k == 15) for k in range(15)]
+                       + [(R("psx", L + CL * x, L + CL * (x + 1)),) + K("half", CL) + (False, False) for x in (c - 1, c) if PAR["fo"][x] == "a"]
+                       + [(wd, blk("wk", 15), R("xg", CW * (c - 1) + 15, CW * (c + 1), 16), False, True)])
             for a, b in H:
-                bk, pk = R("bit", a, b), R("psw", 512 + a, 512 + b)
-                tt(bk, R("pw", a, b), R("psw", a, b), ALU.mult)
-                ts(bk, bk, 15, ALU.arith_shift_right, 1, ALU.bitwise_and)
-                tt(pk, R(dk, a, b), bk, ALU.mult)
-                tt(R("ci", a, b), R(kn, a, b), pk, ALU.add)
-                ts(R("ci", a, b), R("ci", a, b), 4095, ALU.bitwise_and)
-                lin(R("cu", a, b), R("ci", a, b), eng="v")
-                tt(R("kf", a, b), R(kn, a, b), pk, ALU.add)
+                bk, pk = R("bit", a, b), R("psw", a, b)
+                tt(bk, R("pw", a, b), R("psx", L + a, L + b), ALU.mult)
+                ts(bk, bk, 11, ALU.arith_shift_right, 16, ALU.bitwise_and)
+                tt(pk, bk, pk, ALU.mult)
                 tt(lanes("etab", m, a, b), lanes("etab", m, a, b), pk, ALU.add)
-                tt(R("psw", 768 + a, 768 + b), R("d2", a, b), bk, ALU.mult)
-                tt(R("kc", a, b), R("z16", a, b), R("psw", 768 + a, 768 + b), ALU.add)
-        master = lambda a, b: [(R("i32"), R("kf", a, b)), (R("p32"), R("wexp", 2 * a, 2 * b, 2)), (R("p32"), R("wexp", 2 * a + 1, 2 * b, 2))]
-        for a, b in H:
-            if not late:
-                lin(R("kf", a, b), lanes("kti", m, a, b), eng="v")
-            for kk in range(2):
-                lin(R("wexp", 2 * a + kk, 2 * b, 2), R("kf", a, b), pc(4 + kk), pc(6 + kk), eng=SM)
-            if not late:
-                ts(R("ci", a, b), lanes("kti", m, a, b), 4095, ALU.bitwise_and)
-                lin(R("cu", a, b), R("ci", a, b), eng="v")
-            if not late:
-                lin(R("kc", a, b), R("kf", a, b), 64.0, 16.0, eng=SM)
-        for c0, c1 in PARTS:
+                tt(R(kf, a, b), lanes("etab", m, a, b), R("psw", 2 * L + a, 2 * L + b), ALU.add)
+                if PAR["int1"]:
+                    tt(R("ci", a, b), R("kn", a, b), pk, ALU.add)
+                    ts(R("ci", a, b), R("ci", a, b), 4095, ALU.bitwise_and)
+                    lin(R("cu", a, b), R("ci", a, b), eng="v")
+            entries(kf, "ohi", "olo", PAR["int1"])
+        for c0, c1 in PAR["parts"][t]:
             a, b = 32 * c0, 32 * c1
-            for u0, u1, e in [x for x in CH2 if c0 <= x[0] < c1]:
+            for u0, u1, e, e2 in [x for x in PAR["ch2"] if c0 <= x[0] < c1]:
                 w0, w1, ps = 512 * u0, 512 * u1, ("psx", "psw")[u0 // 2 % 2]
-                lin(R("eg", w0, w1), IND(R("etab"), R("cu", 32 * u0, 32 * u1)), 64.0, eng=e)
-                mm([(R(ps, 512 * (k % 2) + j, 512 * (k % 2 + 1), 8), blk("s1", j), R("wexp", 64 * k, 64 * (k + 1)), True, True)
+                lin(R("eg", w0, w1), IND(R("etab", PAD, PAD + W), R("cu", 32 * u0, 32 * u1)), 16.0, OFF, eng=e)
+                mm([(R(ps, 512 * (k % 2) + j, 512 * (k % 2 + 1), 8), blk("s1", j), R("wexp", 2 + 64 * k, 2 + 64 * (k + 1)), True, True)
                     for k in range(u0, u1) for j in range(8)])
-                tt(R(tb, tb0 + w0, tb0 + w1), R("eg", w0, w1), R(ps, w0 % CW, w0 % CW + w1 - w0), ALU.add)
-                ts(rb(16 + w0, 16 + w1), R(tb, tb0 + w0, tb0 + w1), 144.0 * U, ALU.max, 144.0 * U, ALU.subtract)
+                tt(qb(16 + w0, 16 + w1), R("eg", w0, w1), R(ps, w0 % CW, w0 % CW + w1 - w0), ALU.max)
+                for k, e3 in enumerate(e2):
+                    x0, x1 = w0 + k * (w1 - w0) // len(e2), w0 + (k + 1) * (w1 - w0) // len(e2)
+                    lin(wb(x0, x1), R("eg", x0, x1), eng=e3)
                 for k in range(u0, u1):
                     x = 512 * k
                     d0 = R("psd", x % CW, x % CW + 512)
-                    mm(group(d0, [(R("idn"), R("cst")), (R("idn"), rb(x + 16, x + 528)), (R("nid"), rb(x + 15, x + 527))]))
+                    mm([(d0, M("idn"), qb(x + 16, x + 528), True, False), (d0, M("nid"), qb(x + 15, x + 527), False, False)]
+                       + [(R("psd", x % CW + j, x % CW + 512, 8), blk("sd", j), R("wexp", 2 + 64 * k, 2 + 64 * (k + 1)), False, False)
+                          for j in range(8)]
+                       + [(R("psd", x % CW, x % CW + 512, 8), R("sx"), R("wexp", 1 + 64 * k, 1 + 64 * (k + 1)), False, True)])
                     scan(R("vs", x, x + 512), d0, R("eg", x, x + 512), 0.0, ALU.add, ALU.max)
-            mm(group(R("psa", a, b), [(R("idn"), R("c29", 0, b - a))]
-                     + [(blk("dg", k), R(tb, tb0 + 16 * a + k, tb0 + 16 * b, 16)) for k in range(16)]))
-            tt(R("own", a, b), R("kc", a, b), R("psa", a, b), ALU.min)
-            mm(group(R("psa", L + a, L + b), [(R("nid"), rb(16 + 16 * a + 15, 16 + 16 * b, 16)), (R("i32"), R("vs", 16 * a + 15, 16 * b, 16))]))
+            mm(group(R("psa", a, b), [K("flag", b - a)] + [(blk("dg", k), wb(16 * a + k, 16 * b, 16)) for k in range(16)]))
+            tt(R("own", a, b), R(kf, a, b), R("psa", a, b), ALU.min)
+            mm(group(R("psa", L + a, L + b), [(M("n16"), qb(16 + 16 * a + 15, 16 + 16 * b, 16)), (M("i16"), R("vs", 16 * a + 15, 16 * b, 16)),
+                                              (R("s15"), R("wexp", 3 + 2 * a, 2 + 2 * b, 2)), K("b2", b - a)]))
             tt(R("zf", a, b), R("own", a, b), R("psa", L + a, L + b), ALU.max)
-            lin(R("za", a, b), R("zf", a, b), 1.0 / 64, -0.25, eng=ZA)
-            ts(R(kn, a, b), R("za", a, b), 0.5 * MAGIC, ALU.add, 0.5 * MAGIC, ALU.subtract)
-            for kk in range(2):
-                lin(R("w17", 2 * a + kk, 2 * b, 2), R("zf", a, b), pc(8 + kk), pc(10 + kk), eng=SM)
-            if INT1:
-                zi = R("zi", a, b)
-                tt(zi, R("own", a, b), R("psa", L + a, L + b), ALU.max)
-                ts(zi, zi, 6, ALU.arith_shift_right, 4095, ALU.bitwise_and)
-                if m:
-                    ts(R("own", a, b), zi, float(V), ALU.is_ge, -float(W), ALU.mult)
-                    tt(zi, zi, R("own", a, b), ALU.add)
-                lin(R("cu2", a, b), zi, 1.0, float(NG * m), eng="v")
-                continue
-            mm(group(R("psa", a, b), [(R("n4k"), R("w17", 2 * a, 2 * b, 2)), (R("n4k"), R("w17", 2 * a + 1, 2 * b, 2)), (R("i32"), R(kn, a, b))]))
-            if m:
-                ts(R("za", a, b), R("psa", a, b), float(V), ALU.is_ge, -float(W), ALU.mult)
-                tt(R("za", a, b), R("za", a, b), R("psa", a, b), ALU.add)
-                lin(R("cu2", a, b), R("za", a, b), 1.0, float(NG), eng="v")
+            lifted["kn%d" % m] = PAR["kn"][t] == "a"
+            if PAR["kn"][t] == "a":
+                lin(R("kn", a, b), R("zf", a, b), 1.0, MAGIC, eng="a")
             else:
-                lin(R("cu2", a, b), R("psa", a, b), eng="v")
-        early[0] = EARLY[t]
-        p0, p1 = R("psb", 0, L), R("psb", L, 2 * L)
-        pa, pb = R("psd", L, 2 * L), R("psd", 3 * L, 4 * L)
-        hi, lo = ("ohi", "olo") if late else ("chi", "clo")
-        mm(group(pa, master(0, L)))
-        lin(R(hi), pa, 1.0, -COFF, eng=SM)
-        mm(group(pb, master(0, L) + [(R("nid"), R(hi))]))
-        lin(R(lo), pb, 1.0, -COFF, eng=SM)
+                ts(R("kn", a, b), R("zf", a, b), MAGIC, ALU.add, MAGIC, ALU.subtract)
+            for kk in range(2):
+                lin(R("w17", 2 * a + kk, 2 * b, 2), R("zf", a, b), pc(8 + kk), pc(10 + kk), eng="a")
+            mm(group(R("psa", a, b), [(M("n4k"), R("w17", 2 * a, 2 * b, 2)), (M("n4k"), R("w17", 2 * a + 1, 2 * b, 2)), (M("i32"), R("kn", a, b))]))
+            ts(R("cu2", a, b), R("psa", a, b), MAGIC if PAR["kn"][t] == "a" else 0.0, ALU.subtract)
         if late:
-            for a, b in H:
-                mm(group(R("psb", L + a, L + b), [(R("i32"), R("zf", a, b)), (R("m32"), R(kn, a, b)), (R("n256"), R("ib", a, b))]))
-                lin(R("ou", a, b), R("psb", L + a, L + b), -float(L), 32.0 * L, eng="v")
+            mm(group(R("psb", 0, L), [(M("idn"), R("keep"))]) + group(R("psb", L, 2 * L), code(0, L) + [K("now", L)]))
+            lin(R("oc"), R("psb", L, 2 * L), 512.0, -232.0 - 512 * 14.5, eng="a")
+            tt(R("psb", 0, L), R("bit"), R("psb", 0, L), ALU.max)
+            tt(R("oa"), R("oc"), R("psb", 0, L), ALU.min)
+            tt(R("slot"), R("oa"), R("psb", L, 2 * L), ALU.max)
+            mm(group(R("psb", 0, L), [(M("n4k"), R("slot")), (M("idn"), R("ib"))]))
+            lin(R("ou"), R("psb", 0, L), 1.0, 65536.0, eng="v")
+            if last:
+                origins("psa", L)
+                lin(R("on0"), R("psa", L, 2 * L))
         else:
-            mm(group(p0, master(0, L) + [(R("nid"), R("vhi")), (R("nid"), R("vlo%d" % m))]))
-            ts(R("junk"), p0, COFF, ALU.is_equal, COFF + W, ALU.mult)
-            tt(R("junk"), R("junk"), pa, ALU.max)
-            lin(R(fu), R("junk"), 1.0, -COFF, eng="v")
-            mm(group(p1, [(R("i32"), R("zf")), (R("m32"), R(kn))]))
-            act(R("pw"), p1, AF.Exp, scale=math.log(2.0))
-            mm(group(p0, [(R("i32"), R("kf")), (R("ni32"), R(kn))]))
-            lin(R(dk), p0, eng="a")
-            mm(group(p1, [(R("i32"), R("kc")), (R("ni32"), R("zf"))]))
-            lin(R("d2"), p1, eng="a")
-            lin(R("z16"), R("zf"), 1.0, 16.0, eng="a")
-        early[0] = 0.0
-        for u0, u1, e in CH3:
+            mm(group(R("psb", 0, L), code(0, L)))
+            act(R("pw"), R("psb", 0, L), AF.Exp, scale=16 * math.log(2.0), bias=7.75 * math.log(2.0), table=0.0 if t else 1400.0)
+            lin(R("keep"), R("psb", 0, L), 1.0, 15.5, eng="a")
+        for u0, u1, e in PAR["ch3"]:
             w0, w1, ps = 512 * u0, 512 * u1, ("psx", "psw")[u0 // 2 % 2]
-            lin(R(xg, xg0 + w0, xg0 + w1), IND(R("xw", NG * (1 - m), NG * (1 - m) + W), R("cu2", 32 * u0, 32 * u1)), eng=e)
+            lin(R("xg", w0, w1), IND(R(xw), R("cu2", 32 * u0, 32 * u1)), eng=e)
             mm([(R(ps, 512 * (k % 2) + j, 512 * (k % 2 + 1), 8), blk("s17", j), R("w17", 64 * k, 64 * (k + 1)), True, True)
                 for k in range(u0, u1) for j in range(8)])
             mn = R("mn", w0 % (2 * CW), w0 % (2 * CW) + w1 - w0)
-            tt(mn, R(xg, xg0 + w0, xg0 + w1), R(ps, w0 % CW, w0 % CW + w1 - w0), ALU.min)
+            tt(mn, R("xg", w0, w1), R(ps, w0 % CW, w0 % CW + w1 - w0), ALU.min)
             scan(R("ys", w0, w1), R("rmask", 0, w1 - w0), mn, 0.0, ALU.mult, ALU.max)
         mir, nxt = "mir%d" % t, "mir%d" % (t + 1)
-        old, new = ("nbe%d" % m, "nbn") if late else (nbo, "nbe%d" % m)
-        for a, b in [(32 * c0, 32 * c1) for c0, c1 in PARTS4]:
-            y, xv = R("ys", 16 * a + 15, 16 * b, 16), lanes("xw", m, a, b)
-            nb, dm, nx, ex = R("psd", a, b), R("psd", 512 + a, 512 + b), R("psx", 512 + a, 512 + b), R("psx", 768 + a, 768 + b)
-            mm(group(dm, [(R("idn"), R("mh", 0, b - a)), (R("idn"), xv), (R("nid"), y)]))
-            if AB == "a":
-                act(R("rl", a, b), dm, AF.Abs, bias=0.5)
-            else:
-                ts(R("rl", a, b), dm, 0.5, ALU.add, 0.0, ALU.min)
+        for a, b in [(32 * c0, 32 * c1) for c0, c1 in PAR["parts4"]]:
+            y, xv = R("ys", 16 * a + 15, 16 * b, 16), lanes(xw, m, a, b)
+            dd, dm, dh = R("psd", a, b), R("psd", 512 + a, 512 + b), R("psx", a, b)
+            nx, ex = R("psx", 512 + a, 512 + b), R("psx", 768 + a, 768 + b)
+            diff = [K("half", b - a), (M("idn"), xv), (M("nid"), y)]
+            mm(group(dm, diff))
+            act(R("rl", a, b), dm, AF.Abs, bias=0.5)
             ms = []
             for s in range(a // 128, -(-b // 128)):
                 a1, b1 = max(a, 128 * s), min(b, 128 * (s + 1))
-                sel = R("sel4", 128 * (2 * m + s), 128 * (2 * m + s + 1), p=P32)
-                dist = [(R("bones"), R("rl", a1, b1))] if AB == "a" else [
-                    (R("bones"), lanes("xw", m, a1, b1)), (R("nbon"), R("ys", 16 * a1 + 15, 16 * b1, 16)),
-                    (R("nbon"), R("rl", a1, b1)), (R("nbon"), R("rl", a1, b1))]
+                sel = blk("sel4", 2 * m + s, P32)
                 ms += group(R("psd", a1, b1), [(sel, R("thh", a1 - 128 * s, b1 - 128 * s, p=P32)),
-                                               (sel, R("thl", a1 - 128 * s, b1 - 128 * s, p=P32))] + dist)
+                                               (sel, R("thl", a1 - 128 * s, b1 - 128 * s, p=P32)), (R("bones"), R("rl", a1, b1))])
             mm(ms)
-            lin(R("a2", a, b), dm, 1.0, MAGIC, eng=SM)
-            lin(R("hd", a, b), R("a2", a, b), -0.5 / BIG, 0.5 * MAGIC / BIG, eng=SM)
-            ts(nb, nb, R("am", 0, 1) if t else 0.0, ALU.is_ge, -BIG, ALU.mult)
-            if not last:
-                tt(lanes("etab", m, a, b), R(kn, a, b), nb, ALU.add)
-            tt(R("ub", a, b), R("hd", a, b), nb, ALU.mult)
-            if not last:
-                lin(R(new, a, b), nb, eng=SM)
-            if late:
-                lin(lanes("fout", m, a, b), nb, 1.0 / BIG, 1.0, eng=SM)
-            if CH[t] == "a":
-                mm(group(ex, [(R("idn"), y), (R("nid"), xv), (R("idn"), R("ub", a, b))])
-                   + group(nx, [(R("idn"), y), (R("idn"), R("ub", a, b))]))
-                act(R("chg", a, b), ex, AF.Abs)
+            if PAR["h2"][t] == "v":
+                ts(dh, dm, 2 * MAGIC, ALU.add, 2 * MAGIC, ALU.subtract)
             else:
-                mm(group(ex, [(R("idn"), xv), (R("nid"), y)]))
+                lin(R("a2", a, b), dm, 1.0, 2 * MAGIC, eng="a")
+                if PAR["h2"][t] == "p":
+                    mm(group(dh, [(M("i32"), R("a2", a, b)), K("m2", b - a)]))
+                else:
+                    lin(dh, R("a2", a, b), 1.0, -2 * MAGIC, eng="a")
+            ts(R(new, a, b), dd, R("am", 0, 1) if t else 0.0, ALU.is_ge, -BIG, ALU.mult)
+            if not last and (PAR["kn"][t] == "a" or PAR["et"][t] == "p"):
+                mm(group(R("psx", L + a, L + b), whole("i32", "kn", a, b)))
+                tt(lanes("etab", m, a, b), R(new, a, b), R("psx", L + a, L + b), ALU.add)
+            elif not last:
+                tt(lanes("etab", m, a, b), R(new, a, b), R("kn", a, b), ALU.add)
+            tt(R("ub", a, b), R(new, a, b), dh, ALU.mult)
+            if PAR["chg"][t] == "n":
+                mm(group(nx, [(M("idn"), y), (M("nub"), R("ub", a, b))]))
+                tt(R("chg", a, b), xv, nx, ALU.not_equal)
+            elif PAR["chg"][t] == "v":
+                mm(group(ex, [(M("n2b"), xv), (M("p2b"), y)]))
                 tt(R("chg", a, b), R("ub", a, b), ex, ALU.not_equal)
-                mm(group(nx, [(R("idn"), y), (R("idn"), R("ub", a, b))]))
-            lin(R(mir, a, b), nx, eng="va" if last else SM)
+                mm(group(nx, [(M("idn"), y), (M("nub"), R("ub", a, b))]))
+            else:
+                mm(group(ex, [(M("nid"), xv), (M("idn"), y), (M("nub"), R("ub", a, b))])
+                   + group(nx, [(M("idn"), y), (M("nub"), R("ub", a, b))]))
+                act(R("chg", a, b), ex, AF.Abs)
+            lin(R(mir, a, b), nx, eng="va" if last else "a")
             mm([(R("psa", a, b), R("bones"), R("chg", a, b), True, True)])
             act(R("chw", a, b), R("psa", a, b), AF.Sign)
-        lin(lanes("xw", m), R(mir, 0, L), eng="va" if last else SM)
+        lin(lanes("xw%d" % (1 - m), m), R(mir, 0, L), eng="va" if last else "g")
         if not last:
-            mm(group(R("psb", L, 2 * L), [(R("idn"), R(new)), (R("nid"), R(old))]))
-            act(R("nq"), R("psb", L, 2 * L), AF.Abs, scale=1.0 / BIG)
-            mm([(R("psb", L, 2 * L), R("o16"), R("nq"), True, True)])
-            act(R("junk"), R("psb", L, 2 * L), AF.Copy, accum=R("asum", 0, 1))
-            lin(R("ai", 0, 1), R("asum", 0, 1), eng="v")
-            ts(R("ai", 1, 2), R("ai", 0, 1), 63, ALU.bitwise_and)
-            lin(R("am", 0, 1), R("ai", 1, 2), eng="v")
-        for (a, b), e in zip(((0, 3), (3, 5)), HB[t]):
-            lin(R("hb", G * a, G * b), IND(R("chw"), R("shu", 12 * a, 12 * b)), eng=e)
-            scan(R("cnt", G * a, G * b), R("bmask", G * a, G * b), R("hb", G * a, G * b), 0.0, ALU.mult, ALU.add)
-        qp = R("psa", L, L + 60)
-        mm(group(qp, [(R("idn"), R("capc"))] + [(blk("dgb", k), R("hb", k, NG, 16)) for k in range(16)]
-                 + [(blk("dg", k), R("cnt", k, NG, 16)) for k in range(16)]))
-        tt(R("q1"), R("dlt"), qp, ALU.min)
-        tt(R("q2"), R("q1"), R("base"), ALU.max)
-        lin(R("qu"), R("q2"), -64.0, eng="v")
-        down = lambda q: [(d, (q - 1 - d) % N) for d in range(N - 1)]
-        for (d, r, es), e in zip([x for call in calls_of(T, topo, rank, down(rank)) for x in call], MG[t]):
-            lin(R(nxt, L + G * d, L + G * (d + 1)), IND(R(mir), R("qu", 12 * d, 12 * (d + 1))), eng=e)
-        g0 = (NG + V) * m
-        exchange(t, down, lambda d: R(nxt, L + G * d, L + G * (d + 1)), lambda d: R("xw", g0 + G * d, g0 + G * (d + 1)))
+            lin(lanes(xw, m), R(mir, 0, L), eng="g")
+            pn = "psd" if late else "psb"
+            if late:
+                mm(group(R(pn, L, 2 * L), [(M("nid"), R(new)), (M("idn"), R("new%d" % m))]))
+            else:
+                mm([x for s in range(4) for x in group(R(pn, L + 64 * s, L + 64 * (s + 1)), [
+                    (M("nid"), R(new, 64 * s, 64 * (s + 1))), (blk("sel4", s, P32), R("fb", m, 768, ST, p=P32))])])
+            act(R("junk"), R(pn, L, 2 * L), AF.Abs, scale=1.0 / BIG, accum=R("asum", 0, 1))
+            mm([(R(pn, L, L + 1), R("o16"), R("asum", 0, 1), True, True)])
+            lin(R("asum", 1, 2), R(pn, L, L + 1), 1.0, -31.5, eng="a")
+            lin(R("asum", 2, 3), R("asum", 1, 2), 1.0, 64 * MAGIC, eng="a")
+            lin(R("asum", 3, 4), R("asum", 2, 3), -1.0, 64 * MAGIC, eng="a")
+            lin(R("am", 0, 1), R(pn, L, L + 1), 1.0, R("asum", 3, 4), eng="a")
+        if late:
+            fo = R("psd", 3 * L, 3 * L + 64, p=P32)
+            mm(group(fo, [(R("selt", 32 * s, 32 * (s + 1)), R(new, 64 * s, 64 * (s + 1))) for s in range(4)]))
+            lin(R("ff", m, 768, ST, p=P32), fo, 1.0 / BIG, 1.0, eng="a")
+        for a, b, e in PAR["hb"][t]:
+            lin(R("hb", G * a, G * b), IND(R("chw"), R("shu", 12 * a, 12 * b)), 64.0, eng=e)
+            for d in range(a, b):
+                scan(R("cnt", G * d, G * (d + 1)), R("hb", G * d, G * (d + 1)), R("capt"), 0.0, ALU.add, ALU.min)
+        for a, b in PAR["qp"][t]:
+            qp = R("psa", L + 12 * a, L + 12 * b)
+            mm([(qp, M("idn"), R("bhi", 12 * a, 12 * b), True, False), (qp, M("idn"), R("blo", 12 * a, 12 * b), False, False)]
+               + [(R("psa", L + 12 * d + 1, L + 12 * (d + 1)), blk("dd", 16), R("cnt", G * d + 15, G * (d + 1) - 16, 16), False, False)
+                  for d in range(a, b)]
+               + [(qp, blk("dd", k), R("cnt", G * a + k, G * b, 16), False, k == 15) for k in range(16)])
+            tt(R("q1", 12 * a, 12 * b), R("shi", 12 * a, 12 * b), qp, ALU.max)
+            lin(R("qu", 12 * a, 12 * b), R("q1", 12 * a, 12 * b), eng="v")
+        for a, b, e in PAR["mg"][t]:
+            lin(R(nxt, L + G * a, L + G * b), IND(R(mir), R("qu", 12 * a, 12 * b)), eng=e)
+        xn = "xw%d" % (1 - m)
+        exchange(t, down, lambda d: R(nxt, *place(rank, d)), lambda d, r: R(xn, V + G * d, V + G * (d + 1)))
         if last:
             for d in range(N - 1):
-                dma(T.yx[:, V + G * d:V + G * (d + 1)], R("xw", g0 + G * d, g0 + G * (d + 1)), 128 * G * 2, eng="sa"[d % 2])
-            dma(T.yx[:, 0:V], R("xw", NG, NG + V), 128 * V * 2)
-            dma(T.yf[:], R("fout", p=slice(0, 128, 16)), 98304)
-            tt(R("dk0"), R("kn0"), R("kn1"), ALU.add)
-            dma(T.yk[:], R("dk0"), 131072)
-        early[0] = EARLY[t]
+                dma(T.yx[:, V + G * d:V + G * (d + 1)], R(xn, V + G * d, V + G * (d + 1)), 128 * G * 2, eng="sa"[d % 2])
+            dma(T.yx[:, 0:V], R(xn, 0, V), 128 * V * 2)
+            dma(T.yf[:], R("ff", p=P32), 98304)
+            mm(group(R("psb", L, 2 * L), whole("i32", "kn0", 0, L) + whole("i32", "kn1", 0, L)))
+            lin(R("yks"), R("psb", L, 2 * L))
+            dma(T.yk[:], R("yks"), 131072)
         if not late:
             continue
         for row, (x0, x1, x2) in enumerate((("vhi", "chi", "ohi"), ("vlo%d" % m, "clo", "olo"))):
@@ -520,17 +586,12 @@ def build(g, rank, T, topo):
             dma(R("wo", 0, L, p=rows), R(x0, p=rows), 4096)
             dma(R("wo", L, 17 * L, p=rows), R(x1), 65536)
             dma(R("wo", 17 * L, 33 * L, p=rows), R(x2), 65536)
-        for c, e in enumerate(OG[t]):
-            n = L // len(OG[t])
-            lin(R("og", 16 * n * c, 16 * n * (c + 1)), IND(R("wo"), R("ou", n * c, n * (c + 1))), eng=e)
-        onat = R("psb", 0, L)
-        for c in range(NC):
-            mm(group(R("psb", CL * c, CL * (c + 1)), [(blk("ox", k), R("og", CW * c + k, CW * (c + 1), 16)) for k in range(16)]))
+        for c in range(8):
+            lin(R("og", 512 * c, 512 * (c + 1)), IND(R("wo"), R("ou", 32 * c, 32 * (c + 1))), eng=PAR["og"][t][c])
         if last:
-            tt(R("dk1"), R("on0"), onat, ALU.add)
-            dma(T.yo[:], R("dk1"), 131072)
-        else:
-            lin(R("on0"), onat, eng="a")
+            origins("psb", 0)
+            tt(R("yos"), R("on0"), R("psb", 0, L), ALU.add)
+            dma(T.yo[:], R("yos"), 131072)
     return ops, Q
 
 
@@ -541,6 +602,8 @@ def schedule(ops, noise=None):
     for i in range(n):
         for j in deps[i]:
             users[j].append(i)
+    if "order" in FOUND:
+        return keep_order(deps, users, FOUND["order"]), FOUND["eng"]
     prio = [0.0] * n
     for i in range(n - 1, -1, -1):
         o = ops[i]
@@ -554,62 +617,317 @@ def schedule(ops, noise=None):
         now = lay_out(ops, deps, users, back[3], False)
         if max(now[3]) < max(best[3]):
             best = now
-    if "start" in FOUND:
-        return lay_out(ops, deps, users, [-s for s in FOUND["start"]], False)
-    rng = np.random.default_rng(SEED)
-    ends = lambda s: [replay(ops, deps, s[0], s[1], x) for x in SPEEDS]
-    unit = ends(best)
-    score = lambda s: sum(x / y for x, y in zip(ends(s), unit)) / len(unit)
-    now, sn, sb = best, 1.0, 1.0
-    for k in range(TRIES):
-        at = np.array(now[2])
-        near = np.abs(at - rng.uniform(0, max(now[3]))) < (2000, 5000, 10000)[k % 3]
-        move = rng.normal(0, (300, 1000, 2500)[int(rng.integers(3))], n) * (rng.random(n) < 0.4) * near
-        s = lay_out(ops, deps, users, [float(x) for x in move - at], False)
-        if k % 10 == 9:
-            s = lay_out(ops, deps, users, lay_out(ops, users, deps, s[3], True)[3], False)
-        x = score(s)
-        if x <= sn + 0.0003:
-            now, sn = s, x
-        if x < sb:
-            best, sb = s, x
-    if TRIES:
-        FOUND["start"] = best[2]
-    return best
+    order, eng = improve(ops, deps, best[0], best[1])
+    FOUND["order"], FOUND["eng"] = order, eng
+    return order, eng
 
 
-def replay(ops, deps, order, eng, speed):
-    cyc, gath = speed
-    free, fin, bank, wire = {}, [0.0] * len(ops), {}, 0.0
-    for i in order:
-        o, e = ops[i], eng[i]
-        at = free.get(e, 0.0)
+def tables(ops, deps):
+    n, above, few, names = len(ops), [], [], {}
+    for i in range(n):
+        implied = 0
         for j in deps[i]:
+            implied |= above[j]
+        few.append([j for j in deps[i] if not implied >> j & 1])
+        for j in deps[i]:
+            implied |= 1 << j
+        above.append(implied)
+    banks = [[names.setdefault(b, len(names)) for b in o["banks"]] for o in ops]
+    cost = [[{e: (FIX[e] * s["fix"] + (c - FIX[e]) * s["cyc"] / CYC * (s["gath"] / GATH if o["ind"] else 1.0) if o["kind"] == "c" else
+                  c * (s["issue"] if o["kind"] == "r" else 1.0)) for e, (c, _) in o["alts"].items()} for o in ops] for s in SPEEDS]
+    for k, s in enumerate(SPEEDS):
+        for i in [i for i, o in enumerate(ops) if o["kind"] == "r"][:2]:
+            cost[k][i]["g"] += FIRST * s["issue"]
+    wire = [[o["lat"] * s["dma"] if o["kind"] == "d" and o["lat"] >= 450.0 else 0.0 for o in ops] for s in SPEEDS]
+    lat = [[(o["lat"] + 2000.0) * s["dma"] if o["kind"] == "d" else o["lat"] * s["far"] for o in ops] for s in SPEEDS]
+    waits = [(HOP * s["fix"], SELF * s["fix"], 1300.0 * s["dma"], 700.0 * s["dma"]) for s in SPEEDS]
+    return few, banks, cost, wire, lat, len(names), waits
+
+
+def replay(tab, order, eng, k, run=None, same=0):
+    few, banks, cost, wire, lat, nb = tab
+    n, cost, lat, mark = len(order), cost[k], lat[k], same // STRIDE
+    if mark:
+        marks = run[3][:mark]
+        free, last, bt, be, bi, ot, oi = [x.copy() for x in marks[-1][:7]]
+        line, lastw = marks[-1][7:]
+        start, fin, why = run[0].copy(), run[1].copy(), run[2].copy()
+    else:
+        marks, free, last, line, lastw = [], {}, {}, 0.0, -1
+        bt, be, bi, ot, oi = [0.0] * nb, [""] * nb, [-1] * nb, [0.0] * nb, [-1] * nb
+        start, fin, why = [0.0] * n, [0.0] * n, [-1] * n
+    for p in range(mark * STRIDE, n):
+        if p % STRIDE == 0 and p > mark * STRIDE:
+            marks.append((free.copy(), last.copy(), bt.copy(), be.copy(), bi.copy(), ot.copy(), oi.copy(), line, lastw))
+        i = order[p]
+        e = eng[i]
+        at, by = free.get(e, 0.0), last.get(e, -1)
+        for j in few[i]:
             x = fin[j] + (HOP if eng[j] != e else SELF)
             if x > at:
-                at = x
-        for b in o["banks"]:
-            for e2, x in bank.setdefault(b, {}).items():
-                if e2 != e and x + HOP > at:
-                    at = x + HOP
-        c = o["alts"][e][0]
-        if o["kind"] == "c":
-            c = FIX[e] + (c - FIX[e]) * cyc / CYC * (gath / GATH if o["ind"] else 1.0)
-        free[e] = at + c
-        for b in o["banks"]:
-            bank[b][e] = at + c
-        if o["kind"] == "d" and o["lat"] >= 500.0:
-            wire = max(wire, at + c + 1300.0) + o["lat"]
-            fin[i] = wire + 700.0
+                at, by = x, j
+        for b in banks[i]:
+            if be[b] != e:
+                ot[b], oi[b], be[b] = bt[b] + HOP, bi[b], e
+            if ot[b] > at:
+                at, by = ot[b], oi[b]
+        end = at + cost[i][e]
+        free[e], last[e], start[i] = end, i, at
+        for b in banks[i]:
+            bt[b], bi[b] = end, i
+        if wire[i]:
+            if line > end + 1300.0:
+                by = lastw
+            line, lastw = max(line, end + 1300.0) + wire[i], i
+            fin[i] = line + 700.0
         else:
-            fin[i] = at + c + o["lat"] + (2000.0 if o["kind"] == "d" else 0.0)
-    return max(fin)
+            fin[i] = end + lat[i]
+        why[i] = by
+    return start, fin, why, marks
+
+
+def improve(ops, deps, order, eng):
+    n, tab, rng = len(ops), tables(ops, deps), np.random.default_rng(SEED)
+    few, users = tab[0], [[] for _ in range(n)]
+    for i in range(n):
+        for j in few[i]:
+            users[j].append(i)
+    runs = [replay(tab, order, eng, k) for k in range(len(SPEEDS))]
+    unit = [max(r[1]) for r in runs]
+    now, best = 9.0, (9.0, order, eng)
+    for k in range(TRIES):
+        if k % 64 == 0:
+            at, place = runs[0][0], {y: p for p, y in enumerate(order)}
+            order = sorted(order, key=lambda y: (at[y], place[y]))
+            runs = [replay(tab, order, eng, s) for s in range(len(SPEEDS))]
+        start, fin, why, _ = runs[int(rng.integers(len(runs)))]
+        i, chain = fin.index(max(fin)), []
+        while why[i] >= 0:
+            if why[i] not in few[i] or len(ops[i]["alts"]) > 1:
+                chain.append(i)
+            i = why[i]
+        i = chain[int(rng.integers(len(chain)))]
+        j, kind, eng2 = why[i], rng.random(), eng
+        if j in few[i] or (len(ops[i]["alts"]) > 1 and kind < 0.2):
+            order2, eng2, a = order, list(eng), order.index(i)
+            eng2[i] = [e for e in ops[i]["alts"] if e != eng[i]][0]
+        elif len(ops[j]["alts"]) > 1 and kind < 0.4:
+            order2, eng2, a = order, list(eng), order.index(j)
+            eng2[j] = [e for e in ops[j]["alts"] if e != eng[j]][0]
+        else:
+            a, b = order.index(j), order.index(i)
+            step = int(rng.geometric(0.15)) - 1 if rng.random() < 0.4 else 0
+            if rng.random() < 0.5:
+                a = max(0, a - step)
+                need, up, stay = set(few[i]), [i], []
+                for x in order[b - 1:a - 1 if a else None:-1]:
+                    if x in need:
+                        up.append(x)
+                        need.update(few[x])
+                    else:
+                        stay.append(x)
+                if j in need:
+                    continue
+                order2 = order[:a] + up[::-1] + stay[::-1] + order[b + 1:]
+            else:
+                b = min(n - 1, b + step)
+                need, down, stay = set(users[j]), [j], []
+                for x in order[a + 1:b + 1]:
+                    if x in need:
+                        down.append(x)
+                        need.update(users[x])
+                    else:
+                        stay.append(x)
+                if i in need:
+                    continue
+                order2 = order[:a] + stay + down + order[b + 1:]
+        heat = HEAT * (1.0 - k / TRIES) ** 2
+        bar, runs2, x = now - heat * math.log(rng.random() + 1e-12), [], 0.0
+        for s in range(len(SPEEDS)):
+            runs2.append(replay(tab, order2, eng2, s, runs[s], a))
+            x += (max(runs2[-1][1]) + MEAN * sum(runs2[-1][1]) / n) / unit[s] / len(unit)
+        if x <= bar:
+            order, eng, runs, now = order2, eng2, runs2, x
+            if x < best[0]:
+                best = (x, order, eng)
+    return best[1], best[2]
+
+
+def replay(tab, order, eng, k, state=None, fin=None):
+    few, banks, cost, wire, lat, nb, waits = tab
+    cost, wire, lat, (HOP, SELF, pre, post) = cost[k], wire[k], lat[k], waits[k]
+    if state is None:
+        state = ({}, {}, [0.0] * nb, [""] * nb, [-1] * nb, [0.0] * nb, [-1] * nb, [0.0, -1])
+        fin = [0.0] * len(few)
+    free, last, bt, be, bi, ot, oi, (line, lastw) = [x.copy() for x in state]
+    start, why = {}, {}
+    for i in order:
+        e = eng[i]
+        at, by = free.get(e, 0.0), last.get(e, -1)
+        for j in few[i]:
+            x = fin[j] + (HOP if eng[j] != e else SELF)
+            if x > at:
+                at, by = x, j
+        for b in banks[i]:
+            if be[b] != e:
+                ot[b], oi[b], be[b] = bt[b] + HOP, bi[b], e
+            if ot[b] > at:
+                at, by = ot[b], oi[b]
+        end = at + cost[i][e]
+        free[e], last[e], start[i] = end, i, at
+        for b in banks[i]:
+            bt[b], bi[b] = end, i
+        if wire[i]:
+            if line > end + pre:
+                by = lastw
+            line, lastw = max(line, end + pre) + wire[i], i
+            fin[i] = line + post
+        else:
+            fin[i] = end + lat[i]
+        why[i] = by
+    return start, fin, why, (free, last, bt, be, bi, ot, oi, [line, lastw])
+
+
+def tails(tab, users, rest, eng, k):
+    few, banks, cost, wire, lat, nb, waits = tab
+    wire, (HOP, SELF, pre, post) = wire[k], waits[k]
+    tail, queue, bank, line = {}, {}, [{} for _ in range(nb)], -1e9
+    for i in rest[::-1]:
+        e = eng[i]
+        after = max([0.0] + [tail[u] + (HOP if eng[u] != e else SELF) for u in users[i]])
+        if wire[i]:
+            line = wire[i] + max(post + after, line)
+            after = pre + line
+        else:
+            after += lat[k][i]
+        after = max(after, queue.get(e, 0.0))
+        for b in banks[i]:
+            for e2, x in bank[b].items():
+                if e2 != e and x + HOP > after:
+                    after = x + HOP
+        tail[i] = queue[e] = after + cost[k][i][e]
+        for b in banks[i]:
+            bank[b][e] = tail[i]
+    return tail, queue, bank, line
+
+
+def improve(ops, deps, order, eng):
+    n, tab, rng = len(ops), tables(ops, deps), np.random.default_rng(SEED)
+    few, users, ks, eng = tab[0], [[] for _ in range(n)], range(len(SPEEDS)), list(eng)
+    for i in range(n):
+        for j in few[i]:
+            users[j].append(i)
+    unit = [max(replay(tab, order, eng, k)[1]) * len(ks) for k in ks]
+    best, done = (9.0, order, eng), 0
+    while done < TRIES:
+        at, place = replay(tab, order, eng, 0)[0], {y: p for p, y in enumerate(order)}
+        order = sorted(order, key=lambda y: (at[y], place[y]))
+        x = sum(max(replay(tab, order, eng, k)[1]) / unit[k] for k in ks)
+        if x < best[0]:
+            best = (x, order, list(eng))
+        lo = max(0, int(rng.integers(-WINDOW // 2, n - WINDOW // 2)))
+        head, win, rest = order[:lo], order[lo:lo + WINDOW], order[lo + WINDOW:]
+        inside, before, after = set(win), [replay(tab, head, eng, k) for k in ks], [tails(tab, users, rest, eng, k) for k in ks]
+        out = [{i: max([0.0] + [after[k][0][u] + tab[6][k][0] for u in users[i] if u in after[k][0]]) for i in order[:lo + WINDOW]} for k in ks]
+        fixed = [max([0.0] + [before[k][1][i] + out[k][i] for i in head]) for k in ks]
+
+        def run(win, k):
+            start, fin, why, (free, last, bt, be, bi, ot, oi, line) = replay(tab, win, eng, k, before[k][3], before[k][1])
+            top, by, o, total, HOP = fixed[k], -1, out[k], 0.0, tab[6][k][0]
+            for i in win:
+                x = fin[i]
+                total += x
+                x += o[i]
+                if x > top:
+                    top, by = x, i
+            for e, x in after[k][1].items():
+                if free.get(e, 0.0) + x > top:
+                    top, by = free[e] + x, last[e]
+            for b, at in enumerate(after[k][2]):
+                for e, x in at.items():
+                    if e != be[b] and bt[b] + HOP + x > top:
+                        top, by = bt[b] + HOP + x, bi[b]
+            if line[0] + after[k][3] > top:
+                top, by = line[0] + after[k][3], line[1]
+            chain = []
+            while by in inside:
+                j = why[by]
+                if j in inside and (j not in few[by] or len(ops[by]["alts"]) > 1):
+                    chain.append((by, j))
+                by = j
+            return (top + MEAN * total / n) / unit[k], chain
+
+        runs = [run(win, k) for k in ks]
+        now = sum(r[0] for r in runs)
+        heat = HEAT * (1.0 - done / TRIES) ** 2
+        done += STAY
+        for pick, kind, side, far, luck in rng.random((STAY, 5)).tolist():
+            chain = runs[int(side * 64) % len(runs)][1]
+            if not chain:
+                continue
+            i, j = chain[int(pick * len(chain))]
+            flip, win2 = -1, win
+            if j in few[i] or (len(ops[i]["alts"]) > 1 and kind < 0.2):
+                flip = i
+            elif len(ops[j]["alts"]) > 1 and kind < 0.4:
+                flip = j
+            else:
+                if kind > 0.8:
+                    i, j = (j, j) if side < 0.5 else (i, i)
+                a, b, step = win.index(j), win.index(i), int(-(6.0, REACH)[kind > 0.6] * math.log(far / 0.6 + 1e-9)) if far < 0.6 else 0
+                if side < 0.5:
+                    a = max(0, a - step)
+                    need, up, stay = set(few[i]), [i], []
+                    for x in win[a:b][::-1]:
+                        if x in need:
+                            up.append(x)
+                            need.update(few[x])
+                        else:
+                            stay.append(x)
+                    if j in need:
+                        continue
+                    win2 = win[:a] + up[::-1] + stay[::-1] + win[b + 1:]
+                else:
+                    b = min(len(win) - 1, b + step)
+                    need, down, stay = set(users[j]), [j], []
+                    for x in win[a + 1:b + 1]:
+                        if x in need:
+                            down.append(x)
+                            need.update(users[x])
+                        else:
+                            stay.append(x)
+                    if i in need:
+                        continue
+                    win2 = win[:a] + stay + down + win[b + 1:]
+            if flip >= 0:
+                was = eng[flip]
+                eng[flip] = [e for e in ops[flip]["alts"] if e != was][0]
+            runs2 = [run(win2, k) for k in ks]
+            x = sum(r[0] for r in runs2)
+            if x <= now - heat * math.log(luck + 1e-12):
+                win, runs, now = win2, runs2, x
+            elif flip >= 0:
+                eng[flip] = was
+        order = head + win + rest
+    x = sum(max(replay(tab, order, eng, k)[1]) / unit[k] for k in ks)
+    return (order, eng) if x < best[0] else best[1:]
+
+
+def keep_order(deps, users, order):
+    left, done, out = [len(d) for d in deps], [False] * len(deps), []
+    while len(out) < len(order):
+        for i in order:
+            if not done[i] and left[i] == 0:
+                done[i] = True
+                out.append(i)
+                for u in users[i]:
+                    left[u] -= 1
+                break
+    return out
 
 
 def lay_out(ops, deps, users, prio, back):
     n = len(ops)
-    if not back:
-        prio = [p + o["early"] for p, o in zip(prio, ops)]
     left = [len(d) for d in deps]
     ready = [i for i in range(n) if left[i] == 0]
     busy = {}
@@ -621,22 +939,38 @@ def lay_out(ops, deps, users, prio, back):
         while moved:
             moved = False
             for iv, pad in lanes:
-                for s, f, who in iv:
+                lo, hi = 0, len(iv)
+                while lo < hi:
+                    mid = (lo + hi) // 2
+                    if iv[mid][1] + pad > at:
+                        hi = mid
+                    else:
+                        lo = mid + 1
+                while lo < len(iv):
+                    s, f, who = iv[lo]
                     if s - pad >= at + c:
                         break
                     if f + pad > at and (pad == 0.0 or who != e):
                         at, moved = f + pad, True
+                    lo += 1
         return at
 
     def put(key, item):
         iv = busy.setdefault(key, [])
-        k = len(iv)
-        while k and iv[k - 1] > item:
-            k -= 1
-        iv.insert(k, item)
+        lo, hi = 0, len(iv)
+        while lo < hi:
+            mid = (lo + hi) // 2
+            if iv[mid] > item:
+                hi = mid
+            else:
+                lo = mid + 1
+        iv.insert(lo, item)
 
+    rank = [0] * n
+    for k, i in enumerate(sorted(range(n), key=lambda x: (prio[x], -x))):
+        rank[i] = k
     while ready:
-        i = max(ready, key=lambda x: (prio[x], -x))
+        i = max(ready, key=lambda x: rank[x])
         o = ops[i]
         cand = []
         for e, (c, _) in o["alts"].items():
@@ -684,7 +1018,7 @@ def rank_program(g, core, T, topo):
     if rank is None:
         return
     ops, Q = build(g, rank, T, topo)
-    order, eng, start, fin = schedule(ops)
+    order, eng = schedule(ops)
     bank_order(ops, order, eng)
     need = [False] * len(ops)
     for i, o in enumerate(ops):

import math
import numpy as np
from concourse.bass import DstId, RemoteDMATransfer
from concourse.mybir import AluOpType as ALU, ActivationFunctionType as AF

N, V, W, G, CAP, ST, L, RO = 6, 3072, 4032, 192, 48, 12, 256, 4
NG = (N - 1) * G
BIG = 131072.0
U = 65536.0
OFF = 144 * U - 32256
OWN = 7.75 / 16
MAGIC = 12582912.0
PAD = 8
NC, NH = 4, 2
CL, HL = L // NC, L // NH
CW = 16 * CL
TWICE = ("kf", "wexp", "cu", "keep", "chi", "clo", "pw", "fu", "kn", "ou")
PASSES, TRIES, HEAT, MEAN, WINDOW, STAY, FIRST, SEED, FOUND = 3, 380000, 0.002, 2.0, 130, 400, 1000.0, 0, {}
MF = {"i32": 1.0, "ni32": -1.0, "i16": 1.0 / 16, "ni16": -1.0 / 16}
MB = {"idn": 1.0, "nid": -1.0, "n16": -1.0 / 16, "n4k": -4096.0, "nub": -0.5 / BIG, "p2b": 2 * BIG, "n2b": -2 * BIG}
CM = {"flag": 32 * 136 * U, "up": 144 * 4096.0, "b2": None, "half": -0.5,
      "own": OWN, "dk": -OWN / 16, "now": 14.5, "mi32": -MAGIC, "mni32": MAGIC, "mni16": MAGIC / 16, "m2": -2 * MAGIC}

SCRATCH = {
    "psw": ("psum", [128, 1024], "float32"), "psd": ("psum", [128, 1024], "float32"),
    "psx": ("psum", [128, 1024], "float32"), "psa": ("psum", [128, 512], "float32"),
    "psb": ("psum", [128, 512], "float32"),
}
for _n, _c, _d in [
    ("kti", V, "int32"), ("etab", PAD + W, "float32"), ("xw0", W, "bfloat16"), ("xw1", W, "bfloat16"),
    ("ff", 768, "float32"), ("fi", 768, "int32"), ("fb", 768, "bfloat16"), ("thi", 128, "int32"), ("thh", 128, "bfloat16"),
    ("thl", 128, "bfloat16"), ("thn", 128, "float32"), ("shi", 60, "int32"), ("shu", 60, "uint16"),
    ("eg", 4096, "float32"), ("wb", 4096, "bfloat16"), ("qb", 4112, "bfloat16"), ("vs", 4096, "float32"),
    ("xg", 4096, "bfloat16"), ("mn", 2 * CW, "bfloat16"), ("ys", 4096, "bfloat16"), ("og", 4096, "bfloat16"),
    ("wo", 33 * L, "bfloat16"), ("wk", 2048, "bfloat16"),
    ("zr", 1024, "bfloat16"), ("sel4", 512, "bfloat16"), ("selt", 128, "bfloat16"),
    ("mf", 128 * len(MF), "float32"), ("mb", 128 * len(MB), "bfloat16"), ("cm", 128 * len(CM), "bfloat16"),
    ("bones", 128, "bfloat16"), ("s1", 1024, "bfloat16"), ("sd", 1024, "bfloat16"), ("s17", 1024, "bfloat16"),
    ("sx", 128, "bfloat16"), ("s15", 128, "bfloat16"), ("mend", 128, "bfloat16"), ("dg", 2048, "bfloat16"),
    ("dd", 2048 + 128, "bfloat16"), ("ox", 2048, "bfloat16"), ("o16", 128, "float32"), ("one", L, "bfloat16"),
    ("rmask", CW, "bfloat16"), ("capt", G, "bfloat16"),
    ("pci", 4, "int32"), ("pc", 24, "float32"), ("j8", 8, "float32"), ("m8", 12, "float32"), ("md8", 8, "float32"),
    ("ib", L, "bfloat16"), ("vhi", L, "bfloat16"), ("vlo0", L, "bfloat16"), ("vlo1", L, "bfloat16"),
    ("bhi", 60, "bfloat16"), ("blo", 60, "bfloat16"),
    ("ci", L, "int32"), ("cu", L, "uint16"), ("wexp", 2 * L + 2, "bfloat16"),
    ("chi", L, "bfloat16"), ("clo", L, "bfloat16"), ("ohi", L, "bfloat16"), ("olo", L, "bfloat16"),
    ("own", L, "float32"), ("cu2", L, "uint16"), ("w17", 2 * L, "bfloat16"),
    ("kn", L, "float32"), ("kf", L, "float32"), ("kg", L, "float32"), ("zf", L, "float32"), ("pk", L, "float32"),
    ("ou", L, "uint16"), ("oc", L, "bfloat16"), ("oa", L, "bfloat16"), ("slot", L, "bfloat16"), ("self", L, "bfloat16"),
    ("on0", L, "float32"), ("fu", L, "uint16"), ("yks", L, "float32"), ("yos", L, "float32"),
    ("pw", L, "bfloat16"), ("keep", L, "bfloat16"), ("bit", L, "int32"), ("a2", L, "float32"),
    ("ub", L, "bfloat16"), ("rl", L, "bfloat16"), ("chg", L, "bfloat16"), ("chw", L, "bfloat16"),
    ("new0", L, "bfloat16"), ("new1", L, "bfloat16"), ("new2", L, "bfloat16"), ("new3", L, "bfloat16"),
    ("junk", L, "bfloat16"), ("asum", 4, "float32"), ("ai", 4, "int32"), ("am", 4, "float32"),
    ("hb", NG, "bfloat16"), ("cnt", NG, "bfloat16"), ("q1", 60, "float32"), ("qu", 60, "uint16"),
    ("mir0", L + NG, "bfloat16"), ("mir1", L + NG, "bfloat16"), ("mir2", L + NG, "bfloat16"),
    ("mir3", L + NG, "bfloat16"), ("mir4", L + NG, "bfloat16"),
]:
    for _s in (("0", "1") if _n in TWICE else ("",)):
        SCRATCH[_n + _s] = ("sbuf", [128, _c], _d)

NDMA = 40
SEMAPHORES = (["ev", "ea", "ep", "eg"] + ["d%d" % _i for _i in range(NDMA)]
              + ["arr%d" % _i for _i in range(2 * RO + 2)] + ["snt%d" % _i for _i in range(2 * RO + 2)])

SIZE = {"float32": 4, "int32": 4, "bfloat16": 2, "uint16": 2}
CYC, PCYC, GATH = 0.96, 0.48, 1.56
FIX = {"v": 60.0, "a": 90.0, "p": 30.0, "g": 160.0, "s": 60.0}
PAR = {
    "fo": "avav", "int1": True, "h2": "aavv", "chg": "vvvv", "kn": "vvvv", "et": "vvvv", "lo": "v",
    "og": ["", "", ["a", "va"] * 4, ["va"] * 8],
    "parts": [[(0, 4), (4, 6), (6, 8)]] * 4, "parts4": [(0, 4), (4, 8)],
    "ch2": [(0, 1, "a", "g"), (1, 2, "a", "g"), (2, 4, "a", "g"), (4, 6, "a", ["g", "ga"]), (6, 8, "a", ["g", "ga"])],
    "ch3": [(0, 2, "a"), (2, 4, "a"), (4, 6, "a"), (6, 7, "a"), (7, 8, "va")],
    "hb": [[(0, 2, "va"), (2, 5, "va")]] * 4, "qp": [[(0, 5)]] * 3 + [[(0, 2), (2, 5)]],
    "mg": [[(0, 2, "va"), (2, 5, "va")]] * 3 + [[(0, 1, "va"), (1, 2, "va"), (2, 4, "va"), (4, 5, "va")]],
}
REACH, EACH = 50.0, 5.0
SPEEDS = [{"cyc": 1.0, "gath": 1.75, "issue": 1.0, "far": 1.0, "dma": 1.0, "fix": 1.0},
          {"cyc": 0.87, "gath": 1.25, "issue": 2.0, "far": 1.6, "dma": 0.55, "fix": 1.6}]
HOP, SELF = 120.0, 60.0


def calls_of(T, topo, src, dests):
    me = T.cores[src]
    far = [x for x in dests if topo.chip(T.cores[x[1]]) != topo.chip(me)]
    near = [x for x in dests if topo.chip(T.cores[x[1]]) == topo.chip(me)]
    fe = topo.engines(me, T.cores[far[0][1]])
    ne = [e for e in topo.engines(me, T.cores[near[0][1]]) if e not in fe]
    hf, hn = len(fe) // 2, len(ne) // len(near)
    first = [(far[0][0], far[0][1], fe[:hf]), (far[1][0], far[1][1], fe[hf:])]
    second = [(far[2][0], far[2][1], fe)] + [(x[0], x[1], ne[hn * i:hn * (i + 1)]) for i, x in enumerate(near)]
    return [first, second]


def build(g, rank, T, topo):
    ops, hist, cls = [], {}, [0]
    Q = {"v": g.vector, "a": g.scalar, "p": g.tensor, "g": g, "s": g.sync}

    def R(name, a=0, b=None, s=1, p=None):
        if name in TWICE:
            name += str(cls[0])
        if b is None:
            b = SCRATCH[name][1][1]
        cols = slice(a, b) if s == 1 else slice(a, b, s)
        n = len(range(a, b, s))
        return {"ap": T[name][(slice(None) if p is None else p, cols)], "reg": [(name, a, a + (n - 1) * s + 1)], "n": n,
                "ps": name[:2] == "ps", "b": SIZE[SCRATCH[name][2]], "ind": False}

    def IND(win, off):
        return {"ap": win["ap"].indirect(off["ap"]), "reg": win["reg"] + off["reg"], "n": 16 * off["n"], "ps": False,
                "b": win["b"], "ind": True}

    def add(alts, outs, ins, kind="c", extra=(), lat=0.0, sem=None):
        me, deps = len(ops), {}
        for e in extra:
            deps[e] = True
        acc = [(r, True) for x in outs for r in x["reg"]] + [(r, False) for x in ins for r in x["reg"]]
        for (name, a, b), wr in acc:
            ps = name[:2] == "ps"
            gr = 512 if ps else 16 // SIZE[SCRATCH[name][2]]
            lo, hi = a // gr * gr, -(-b // gr) * gr
            for j, a2, b2, lo2, hi2, wr2 in hist.setdefault(name, []):
                if lo < hi2 and lo2 < hi and (wr or wr2):
                    if (a < b2 and a2 < b) or kind != "c" or ops[j]["kind"] != "c":
                        deps[j] = True
        for (name, a, b), wr in acc:
            gr = 512 if name[:2] == "ps" else 16 // SIZE[SCRATCH[name][2]]
            hist[name].append((me, a, b, a // gr * gr, -(-b // gr) * gr, wr))
        banks = sorted(set((name, k) for (name, a, b), wr in acc if name[:2] == "ps" for k in range(a // 512, (b - 1) // 512 + 1)))
        ops.append({"alts": alts, "deps": deps, "kind": kind, "lat": lat, "sem": sem, "banks": banks,
                    "ind": any(x.get("ind") for x in ins)})
        return me

    def one(x, *rest):
        if x["ind"]:
            return GATH
        return 0.5 if all(y["b"] == 2 for y in (x,) + rest) else 1.0

    def vc(n, k):
        return FIX["v"] + max(64.0, n * k) * CYC

    def act_alt(out, in_, func, bias, scale, accum=None):
        kw = {}
        if bias is not None:
            kw["bias"] = bias
        if scale is not None:
            kw["scale"] = scale
        if accum is not None:
            kw["accum_out"] = accum["ap"]
        return (FIX["a"] + max(64.0, in_["n"] * (GATH if in_["ind"] else 1.0)) * CYC,
                lambda q: q.activation(out["ap"], in_["ap"], func, **kw))

    def act(out, in_, func, bias=None, scale=None, accum=None, table=0.0):
        c, f = act_alt(out, in_, func, bias, scale, accum)
        return add({"a": (c + table, f)}, [out] + ([accum] if accum else []), [in_])

    def tt(out, a, b, op):
        k = 1.0 if (a["ps"] or b["ps"]) else 2.0
        return add({"v": (vc(out["n"], k), lambda q: q.tensor_tensor(out["ap"], a["ap"], b["ap"], op))}, [out], [a, b])

    def val(s):
        return s["ap"] if isinstance(s, dict) else s

    def ts(out, a, s1, op0, s2=None, op1=None):
        ins = [a] + [s for s in (s1, s2) if isinstance(s, dict)]
        if s2 is None:
            f = lambda q: q.tensor_scalar(out["ap"], a["ap"], val(s1), None, op0)
        else:
            f = lambda q: q.tensor_scalar(out["ap"], a["ap"], val(s1), val(s2), op0, op1)
        return add({"v": (vc(out["n"], one(a, out)), f)}, [out], ins)

    def lin(out, a, scale=None, bias=None, eng="va"):
        alts = {}
        if "v" in eng:
            if scale is None and bias is None:
                f = lambda q: q.tensor_copy(out["ap"], a["ap"])
            elif bias is None:
                f = lambda q: q.tensor_scalar(out["ap"], a["ap"], val(scale), None, ALU.mult)
            else:
                f = lambda q: q.tensor_scalar(out["ap"], a["ap"], val(scale), val(bias), ALU.mult, ALU.add)
            alts["v"] = (vc(out["n"], one(a, out)), f)
        if "a" in eng:
            alts["a"] = act_alt(out, a, AF.Copy if bias is None else AF.Identity, val(bias), val(scale))
        if "g" in eng:
            alts["g"] = (FIX["g"] + 2 * out["n"] * CYC,
                         lambda q: q.affine_select(out["ap"], a["ap"], [[0, out["n"]]], ALU.is_ge, 0.0, 0, 0))
        return add(alts, [out], [a] + [s for s in (scale, bias) if isinstance(s, dict)])

    def scan(out, d0, d1, init, op0, op1):
        return add({"v": (vc(out["n"], one(d0, d1, out)),
                          lambda q: q.tensor_tensor_scan(out["ap"], d0["ap"], d1["ap"], init, op0, op1))}, [out], [d0, d1])

    def fill(out, c):
        return add({"v": (vc(out["n"], one(out)), lambda q: q.memset(out["ap"], c))}, [out], [])

    def mm(ms):
        def f(q):
            for o, l, r, st, sp in ms:
                last = q.matmul(o["ap"], l["ap"], r["ap"], st, sp)
            return last
        cost = FIX["p"] + sum(max(64, m[0]["n"]) * PCYC * (4 if m[2]["b"] == 4 else 1) + EACH for m in ms)
        return add({"p": (cost, f)}, [m[0] for m in ms], [m[1] for m in ms] + [m[2] for m in ms])

    def group(out, pairs):
        return [(out, l, r, i == 0, i == len(pairs) - 1) for i, (l, r) in enumerate(pairs)]

    def iota(out, pat, base, cm):
        kw = {} if SCRATCH[out["reg"][0][0]][2] == "int32" else {"allow_small_or_imprecise_dtypes": True}
        return add({"g": (FIX["g"] + 2 * out["n"] * CYC, lambda q: q.iota(out["ap"], pat, base, cm, **kw))}, [out], [])

    def asel(out, in_, pat, op, fl, base, cm):
        return add({"g": (FIX["g"] + 2 * out["n"] * CYC,
                          lambda q: q.affine_select(out["ap"], in_["ap"], pat, op, fl, base, cm))}, [out], [in_])

    ndma = [0]

    def dma(out, in_, nbytes, eng="s", extra=()):
        sem = "d%d" % ndma[0]
        ndma[0] += 1
        hb = lambda x: x if isinstance(x, dict) else {"ap": x, "reg": []}
        o, i = hb(out), hb(in_)
        return add({eng: (FIX["s"], lambda q: q.dma_start(o["ap"], i["ap"]))}, [o], [i], kind="d", extra=extra,
                   lat=nbytes / 200.0, sem=(sem, 16))

    nsnt = [0]

    def exchange(k, dests_of, src, dst):
        mine = []
        for c, call in enumerate(calls_of(T, topo, rank, dests_of(rank))):
            sem = "snt%d" % nsnt[0]
            nsnt[0] += 1
            trs = []
            for d, r, es in call:
                rid, pid, _ = topo.addr(T.cores[r])
                trs.append(RemoteDMATransfer(dst_ids=[DstId(rid=rid, pnc=pid)], dma_engine_mask=sum(1 << e for e in es),
                                             remote_sem=T.sem["arr%d" % (2 * k + c)], src=src(d)["ap"], dst=dst(d, r)["ap"]))
            f = lambda q, trs=trs, sem=sem: q.remote_dma_fused(trs, local_sem=T.sem[sem])
            mine.append(add({"g": (900.0, f)}, [], [src(c[0]) for c in call], kind="r", lat=3500.0,
                            sem=(sem, sum(len(c[2]) for c in call))))
        for c in range(2):
            got = [(d, len(es)) for q in range(N) if q != rank for d, r, es in calls_of(T, topo, q, dests_of(q))[c] if r == rank]
            add({"x": (0.0, None)}, [dst(d, rank) for d, n in got], [], kind="x", extra=mine[:c + 1], lat=1500.0,
                sem=("arr%d" % (2 * k + c), sum(n for d, n in got)) if got else None)

    down = lambda q: [(d, (q - 1 - d) % N) for d in range(N - 1)]
    turn = lambda q: [x[0] for call in calls_of(T, topo, q, down(q)) for x in call]
    place = lambda q, d: (L + G * turn(q).index(d), L + G * (turn(q).index(d) + 1))

    def lanes(name, m, a=0, b=L):
        o = m + (PAD if name == "etab" else 0)
        return R(name, ST * a + o, ST * (b - 1) + o + 1, ST)

    P32 = slice(0, 32)
    pc = lambda j: R("pc", j, j + 1)
    blk = lambda name, k, p=None: R(name, 128 * k, 128 * (k + 1), p=p)

    def M(name, p=None):
        for buf, tab in (("mf", MF), ("mb", MB), ("cm", CM)):
            if name in tab:
                return blk(buf, list(tab).index(name), p)

    K = lambda name, n: (M(name), R("one", 0, n))
    H = [(HL * h, HL * (h + 1)) for h in range(NH)]

    dma(R("fi", p=P32), T.f0[:], 98304)
    pieces = ((0, 1024), (1024, 2048), (2048, 2560), (2560, V))
    kts = [dma(R("kti", a, b), T.kt[:, a:b], 512 * (b - a), eng="sa"[j % 2]) for j, (a, b) in enumerate(pieces)]
    dma(R("xw0", V, W), T.x0[:, V:W], 128 * NG * 2, extra=kts[2:3])
    x0 = dma(R("xw0", 0, V), T.x0[:, 0:V], 128 * V * 2, extra=kts[2:3])
    dma(R("thi", p=P32), T.th[:], 16384, extra=[x0])
    for e, d in enumerate(turn(rank)):
        dma(R("shi", 12 * e, 12 * (e + 1)), T.shw[:, 12 * d:12 * (d + 1)], 6144, extra=[x0])
    dma(R("xw1", 0, V), T.x0[:, 0:V], 128 * V * 2, extra=[x0])

    fill(R("zr", 0, 512), 0.0)
    fill(R("zr", 512, 1024), 0.0)
    fill(R("one"), 1.0)
    asel(R("sel4", p=P32), R("zr", 0, 512, p=P32), [[-1, 4], [-4, 8], [0, 16]], ALU.not_equal, 1.0, 0, 1)
    asel(R("selt"), R("zr", 0, 128), [[-256, 4], [-16, 8], [256, 4]], ALU.not_equal, 1.0, 0, 1)
    iota(R("pci", 0, 1), [[0, 1]], 0, 1)
    iota(R("j8"), [[1, 8]], 0, 0)
    asel(R("bones"), R("zr", 0, 128), [[-16, 8], [0, 16]], ALU.is_ge, 1.0, -16, 1)
    asel(R("bones"), R("bones"), [[-16, 8], [0, 16]], ALU.is_ge, 0.0, 0, 1)
    asel(M("idn"), R("zr", 0, 128), [[-1, 128]], ALU.not_equal, 1.0, 0, 1)
    for name, c in list(MB.items())[1:] + list(MF.items()):
        lin(M(name), M("idn"), c, eng="a")
    for k in range(16):
        asel(blk("wk", k), R("zr", 0, 128), [[-1, 128]], ALU.not_equal, 2.0 ** (k - 1) * (1.0 if k == 15 else -1.0), 0, 1)
    for name, c in CM.items():
        if name in ("flag", "up"):
            lin(M(name), R("one", 0, 128), c / 128, eng="a")
        elif c is not None:
            asel(M(name), R("zr", 0, 128), [[0, 128]], ALU.not_equal, c / 128, 0, 0)
    fill(M("b2", slice(0, 64)), 2016.0 / 64)
    fill(M("b2", slice(64, 128)), -OWN / 64)
    asel(R("o16"), R("zr", 0, 128), [[0, 128]], ALU.not_equal, 0.0625, 0, 0)
    for hh in range(2):
        cols, z = (1024 * hh, 1024 * (hh + 1)), R("zr")
        asel(R("dg", *cols), z, [[-256, 8], [-16, 8], [255, 16]], ALU.not_equal, -32.0, -2048 * hh, 1)
        asel(R("dd", *cols), R("dg", *cols), [[-256, 8], [-16, 8], [255, 16]], ALU.not_equal, 32.0, -2048 * hh - 256, 1)
        asel(R("ox", *cols), z, [[-256, 8], [-16, 8], [256, 16]], ALU.not_equal, 1.0, -2048 * hh, 1)
        asel(R("ox", *cols), R("ox", *cols), [[-256, 8], [-16, 8], [256, 16]], ALU.not_equal, 1.0, -2048 * hh - 1, 1)
    asel(blk("dd", 16), R("zr", 0, 128), [[-16, 8], [255, 16]], ALU.not_equal, 32.0, 0, 1)
    iota(R("bhi"), [[16, 60]], L, 0)
    for m in range(2):
        iota(R("vlo%d" % m), [[0, 16], [ST, 16]], m, 0)
    iota(R("vhi"), [[16 * ST, 16], [0, 16]], 0, 0)
    iota(R("ib"), [[1, L]], 0, 0)
    asel(R("rmask"), R("zr"), [[0, CL], [-1, 16]], ALU.is_ge, 1.0, 0, 0)
    asel(R("capt"), R("zr", 0, G), [[0, G]], ALU.not_equal, 64.0 * CAP, 0, 0)
    ts(R("pci", 1, 2), R("pci", 0, 1), 15, ALU.bitwise_and)
    ts(R("pci", 2, 3), R("pci", 0, 1), 7, ALU.bitwise_and)
    lin(R("pc", 0, 2), R("pci", 1, 3), eng="v")
    ts(pc(2), pc(0), 8.0, ALU.is_lt)
    ts(pc(3), pc(0), 8.0, ALU.is_ge)
    lin(R("pc", 4, 6), R("pc", 2, 4), 16.0, eng="v")
    ts(pc(12), pc(5), pc(0), ALU.subtract, -1.0, ALU.add)
    lin(R("pc", 6, 8), R("pc", 2, 4), -1.0, 1.0, eng="v")
    ts(R("pc", 6, 8), R("pc", 6, 8), pc(12), ALU.mult)
    lin(R("pc", 16, 18), R("pc", 2, 4), OFF, eng="v")
    tt(R("pc", 6, 8), R("pc", 6, 8), R("pc", 16, 18), ALU.add)
    lin(R("pc", 8, 10), R("pc", 2, 4), 1.0 / 4096, eng="v")
    lin(R("pc", 10, 12), R("pc", 2, 4), 288.0 - 63.0 / 128, -144.0, eng="v")
    lin(pc(13), pc(12), 1.0 / 16, -OWN, eng="v")
    ts(R("mend"), M("idn"), pc(13), ALU.mult)
    fill(R("m8", 0, 1), 0.0)
    ts(R("m8", 1, 9), R("j8"), pc(1), ALU.is_equal)
    tt(R("md8"), R("m8", 0, 8), R("m8", 1, 9), ALU.subtract)
    ts(pc(18), pc(3), -3.0, ALU.mult, 1.0, ALU.add)
    for j in range(8):
        lin(blk("s1", j), R("bones"), R("m8", j + 1, j + 2))
        lin(blk("sd", j), R("bones"), R("md8", j, j + 1))
    lin(R("sx"), blk("s1", 7), pc(18))
    lin(pc(19), pc(2), 18 * 4096.0 - 1.0 / 16, 1.0 / 16, eng="v")
    lin(R("s15"), blk("s1", 7), pc(19))
    lin(R("s17"), R("s1"), 17.0)
    fill(R("qb", 0, 16), 0.0)
    fill(R("wo", 4096, 4112), 0.0)
    fill(R("wo", 8208, 33 * L), 0.0)
    lin(R("etab", PAD + V, PAD + W), R("zr", 0, NG), 1.0, -BIG, eng="a")
    fill(R("etab", 0, PAD), 1.0)
    ts(R("blo"), R("one", 0, 60), pc(0), ALU.mult)
    lin(R("shu"), R("shi"), eng="v")

    lin(R("fb", p=P32), R("fi", p=P32), BIG, -BIG, eng="v")
    lin(R("ff", p=P32), R("fi", p=P32), eng="g")
    for j, ps in enumerate(("psw", "psd", "psx")):
        cuts = sorted(set([1024 * j, 1024 * j + 512, 1024 * j + 1024] + [c for c in range(0, V, 768) if 1024 * j < c < 1024 * j + 1024]))
        ms = []
        for a, b in zip(cuts[:-1], cuts[1:]):
            s = a // 768
            ms.append((R(ps, a - 1024 * j, b - 1024 * j), blk("sel4", s, P32), R("fb", a - 768 * s, b - 768 * s, p=P32), True, True))
        mm(ms)
        for a, b in pieces:
            if a // 1024 == j:
                tt(R("etab", PAD + a, PAD + b), R("kti", a, b), R(ps, a - 1024 * j, b - 1024 * j), ALU.add)
    lin(R("thn", p=P32), R("thi", p=P32), -1.0, eng="v")
    lin(R("thh", p=P32), R("thn", p=P32), eng="g")
    tt(R("thl", p=P32), R("thn", p=P32), R("thh", p=P32), ALU.subtract)

    exchange(RO, lambda q: [(d, (q + 1 + d) % N) for d in range(N - 1)],
             lambda d: R("xw0", V + G * d, V + G * (d + 1)), lambda d, r: R("mir0", *place(r, d)))

    def master(kf, a, b):
        return [(M("n16"), R("wexp", 2 + 2 * a, 2 + 2 * b, 2)), (M("n16"), R("wexp", 3 + 2 * a, 2 + 2 * b, 2)), K("up", b - a),
                (M("i32"), R(kf, a, b)), (R("mend"), R("one", 0, b - a))]

    def entries(kf, hi, lo, direct):
        for a, b in H:
            for kk in range(2):
                lin(R("wexp", 2 + 2 * a + kk, 2 + 2 * b, 2), R(kf, a, b), pc(4 + kk), pc(6 + kk), eng="a")
            if not direct:
                mm(group(R("psb", a, b), master(kf, a, b)))
                lin(R("cu", a, b), R("psb", a, b), eng="v")
        if direct:
            mm(group(R("psb", 0, L), master(kf, 0, L)))
        lin(R(hi), R("psb", 0, L), eng="a")
        if PAR["lo"] == "v":
            tt(R(lo), R("psb", 0, L), R(hi), ALU.subtract)
        else:
            mm(group(R("psb", L, 2 * L), master(kf, 0, L) + [(M("nid"), R(hi))]))
            lin(R(lo), R("psb", L, 2 * L), eng="a")

    lifted = {}

    def whole(times, kn, a, b):
        return [(M(times), R(kn, a, b))] + ([K("m" + times, b - a)] if lifted[R(kn)["reg"][0][0]] else [])

    def origins(ps, at):
        for a, b in H:
            mm(group(R(ps, at + a, at + b), [(blk("ox", k), R("og", 16 * a + k, 16 * b, 16)) for k in range(16)]))

    for m in range(2):
        cls[0] = m
        fill(R("wexp", 0, 2), 0.0)
        for a, b in H:
            lin(R("kf", a, b), lanes("kti", m, a, b), 1.0, OWN, eng="v")
        entries("kf", "chi", "clo", False)
        both = [(M("idn"), R("chi")), (M("idn"), R("clo"))]
        mm(group(R("psb", 0, L), both + [(M("nid"), R("vhi")), (M("nid"), R("vlo%d" % m))]))
        ts(R("self"), R("psb", 0, L), 0.0, ALU.is_equal, -8192.0, ALU.mult)
        mm(group(R("psb", L, 2 * L), both + [(M("idn"), R("self"))]))
        ts(R("fu"), R("psb", L, 2 * L), float(PAD), ALU.add, 0.0, ALU.max)

    for t in range(RO):
        m, late, last = t % 2, t >= 2, t == RO - 1
        cls[0] = m
        kf, xw, new = "kg" if late else "kf", "xw%d" % m, "new%d" % t
        wb = (lambda a, b, s=1: R("wo", a, b, s)) if t == 0 else (lambda a, b, s=1: R("wb", a, b, s))
        qb = (lambda a, b, s=1: R("wo", 4096 + a, 4096 + b, s)) if t == 0 else (lambda a, b, s=1: R("qb", a, b, s))
        code = lambda a, b: whole("ni32", "kn", a, b) + [(M("i32"), R("zf", a, b))]
        if late:
            mm(group(R("psw", 0, L), whole("ni16", "kn", 0, L) + [(M("i16"), R("kf")), K("dk", L)]))
            mm(group(R("psw", 2 * L, 3 * L), [(M("nid"), R("new%d" % m)), K("own", L)]))
            for c in range(NC):
                out, src = R("xg", CW * c, CW * (c + 1)), IND(R("etab"), R("fu", CL * c, CL * (c + 1)))
                if PAR["fo"][c] == "a":
                    act(out, src, AF.Sign, bias=0.5)
                else:
                    ts(out, src, 0.0, ALU.is_lt, -2.0, ALU.mult)
                if c % 2:
                    wd = R("psx", L + CL * (c - 1), L + CL * (c + 1))
                    mm([(wd, blk("wk", k), R("xg", CW * (c - 1) + k, CW * (c + 1), 16), k == 0, k == 15) for k in range(15)]
                       + [(R("psx", L + CL * x, L + CL * (x + 1)),) + K("half", CL) + (False, False) for x in (c - 1, c) if PAR["fo"][x] == "a"]
                       + [(wd, blk("wk", 15), R("xg", CW * (c - 1) + 15, CW * (c + 1), 16), False, True)])
            for a, b in H:
                bk, pk = R("bit", a, b), R("psw", a, b)
                tt(bk, R("pw", a, b), R("psx", L + a, L + b), ALU.mult)
                ts(bk, bk, 11, ALU.arith_shift_right, 16, ALU.bitwise_and)
                tt(pk, bk, pk, ALU.mult)
                tt(lanes("etab", m, a, b), lanes("etab", m, a, b), pk, ALU.add)
                tt(R(kf, a, b), lanes("etab", m, a, b), R("psw", 2 * L + a, 2 * L + b), ALU.add)
                if PAR["int1"]:
                    tt(R("ci", a, b), R("kn", a, b), pk, ALU.add)
                    ts(R("ci", a, b), R("ci", a, b), 4095, ALU.bitwise_and)
                    lin(R("cu", a, b), R("ci", a, b), eng="v")
            entries(kf, "ohi", "olo", PAR["int1"])
        for c0, c1 in PAR["parts"][t]:
            a, b = 32 * c0, 32 * c1
            for u0, u1, e, e2 in [x for x in PAR["ch2"] if c0 <= x[0] < c1]:
                w0, w1, ps = 512 * u0, 512 * u1, ("psx", "psw")[u0 // 2 % 2]
                lin(R("eg", w0, w1), IND(R("etab", PAD, PAD + W), R("cu", 32 * u0, 32 * u1)), 16.0, OFF, eng=e)
                mm([(R(ps, 512 * (k % 2) + j, 512 * (k % 2 + 1), 8), blk("s1", j), R("wexp", 2 + 64 * k, 2 + 64 * (k + 1)), True, True)
                    for k in range(u0, u1) for j in range(8)])
                tt(qb(16 + w0, 16 + w1), R("eg", w0, w1), R(ps, w0 % CW, w0 % CW + w1 - w0), ALU.max)
                for k, e3 in enumerate(e2):
                    x0, x1 = w0 + k * (w1 - w0) // len(e2), w0 + (k + 1) * (w1 - w0) // len(e2)
                    lin(wb(x0, x1), R("eg", x0, x1), eng=e3)
                for k in range(u0, u1):
                    x = 512 * k
                    d0 = R("psd", x % CW, x % CW + 512)
                    mm([(d0, M("idn"), qb(x + 16, x + 528), True, False), (d0, M("nid"), qb(x + 15, x + 527), False, False)]
                       + [(R("psd", x % CW + j, x % CW + 512, 8), blk("sd", j), R("wexp", 2 + 64 * k, 2 + 64 * (k + 1)), False, False)
                          for j in range(8)]
                       + [(R("psd", x % CW, x % CW + 512, 8), R("sx"), R("wexp", 1 + 64 * k, 1 + 64 * (k + 1)), False, True)])
                    scan(R("vs", x, x + 512), d0, R("eg", x, x + 512), 0.0, ALU.add, ALU.max)
            mm(group(R("psa", a, b), [K("flag", b - a)] + [(blk("dg", k), wb(16 * a + k, 16 * b, 16)) for k in range(16)]))
            tt(R("own", a, b), R(kf, a, b), R("psa", a, b), ALU.min)
            mm(group(R("psa", L + a, L + b), [(M("n16"), qb(16 + 16 * a + 15, 16 + 16 * b, 16)), (M("i16"), R("vs", 16 * a + 15, 16 * b, 16)),
                                              (R("s15"), R("wexp", 3 + 2 * a, 2 + 2 * b, 2)), K("b2", b - a)]))
            tt(R("zf", a, b), R("own", a, b), R("psa", L + a, L + b), ALU.max)
            lifted["kn%d" % m] = PAR["kn"][t] == "a"
            if PAR["kn"][t] == "a":
                lin(R("kn", a, b), R("zf", a, b), 1.0, MAGIC, eng="a")
            else:
                ts(R("kn", a, b), R("zf", a, b), MAGIC, ALU.add, MAGIC, ALU.subtract)
            for kk in range(2):
                lin(R("w17", 2 * a + kk, 2 * b, 2), R("zf", a, b), pc(8 + kk), pc(10 + kk), eng="a")
            mm(group(R("psa", a, b), [(M("n4k"), R("w17", 2 * a, 2 * b, 2)), (M("n4k"), R("w17", 2 * a + 1, 2 * b, 2)), (M("i32"), R("kn", a, b))]))
            ts(R("cu2", a, b), R("psa", a, b), MAGIC if PAR["kn"][t] == "a" else 0.0, ALU.subtract)
        if late:
            mm(group(R("psb", 0, L), [(M("idn"), R("keep"))]) + group(R("psb", L, 2 * L), code(0, L) + [K("now", L)]))
            lin(R("oc"), R("psb", L, 2 * L), 512.0, -232.0 - 512 * 14.5, eng="a")
            tt(R("psb", 0, L), R("bit"), R("psb", 0, L), ALU.max)
            tt(R("oa"), R("oc"), R("psb", 0, L), ALU.min)
            tt(R("slot"), R("oa"), R("psb", L, 2 * L), ALU.max)
            mm(group(R("psb", 0, L), [(M("n4k"), R("slot")), (M("idn"), R("ib"))]))
            lin(R("ou"), R("psb", 0, L), 1.0, 65536.0, eng="v")
            if last:
                origins("psa", L)
                lin(R("on0"), R("psa", L, 2 * L))
        else:
            mm(group(R("psb", 0, L), code(0, L)))
            act(R("pw"), R("psb", 0, L), AF.Exp, scale=16 * math.log(2.0), bias=7.75 * math.log(2.0), table=0.0 if t else 1400.0)
            lin(R("keep"), R("psb", 0, L), 1.0, 15.5, eng="a")
        for u0, u1, e in PAR["ch3"]:
            w0, w1, ps = 512 * u0, 512 * u1, ("psx", "psw")[u0 // 2 % 2]
            lin(R("xg", w0, w1), IND(R(xw), R("cu2", 32 * u0, 32 * u1)), eng=e)
            mm([(R(ps, 512 * (k % 2) + j, 512 * (k % 2 + 1), 8), blk("s17", j), R("w17", 64 * k, 64 * (k + 1)), True, True)
                for k in range(u0, u1) for j in range(8)])
            mn = R("mn", w0 % (2 * CW), w0 % (2 * CW) + w1 - w0)
            tt(mn, R("xg", w0, w1), R(ps, w0 % CW, w0 % CW + w1 - w0), ALU.min)
            scan(R("ys", w0, w1), R("rmask", 0, w1 - w0), mn, 0.0, ALU.mult, ALU.max)
        mir, nxt = "mir%d" % t, "mir%d" % (t + 1)
        for a, b in [(32 * c0, 32 * c1) for c0, c1 in PAR["parts4"]]:
            y, xv = R("ys", 16 * a + 15, 16 * b, 16), lanes(xw, m, a, b)
            dd, dm, dh = R("psd", a, b), R("psd", 512 + a, 512 + b), R("psx", a, b)
            nx, ex = R("psx", 512 + a, 512 + b), R("psx", 768 + a, 768 + b)
            diff = [K("half", b - a), (M("idn"), xv), (M("nid"), y)]
            mm(group(dm, diff))
            act(R("rl", a, b), dm, AF.Abs, bias=0.5)
            ms = []
            for s in range(a // 128, -(-b // 128)):
                a1, b1 = max(a, 128 * s), min(b, 128 * (s + 1))
                sel = blk("sel4", 2 * m + s, P32)
                ms += group(R("psd", a1, b1), [(sel, R("thh", a1 - 128 * s, b1 - 128 * s, p=P32)),
                                               (sel, R("thl", a1 - 128 * s, b1 - 128 * s, p=P32)), (R("bones"), R("rl", a1, b1))])
            mm(ms)
            if PAR["h2"][t] == "v":
                ts(dh, dm, 2 * MAGIC, ALU.add, 2 * MAGIC, ALU.subtract)
            else:
                lin(R("a2", a, b), dm, 1.0, 2 * MAGIC, eng="a")
                if PAR["h2"][t] == "p":
                    mm(group(dh, [(M("i32"), R("a2", a, b)), K("m2", b - a)]))
                else:
                    lin(dh, R("a2", a, b), 1.0, -2 * MAGIC, eng="a")
            ts(R(new, a, b), dd, R("am", 0, 1) if t else 0.0, ALU.is_ge, -BIG, ALU.mult)
            if not last and (PAR["kn"][t] == "a" or PAR["et"][t] == "p"):
                mm(group(R("psx", L + a, L + b), whole("i32", "kn", a, b)))
                tt(lanes("etab", m, a, b), R(new, a, b), R("psx", L + a, L + b), ALU.add)
            elif not last:
                tt(lanes("etab", m, a, b), R(new, a, b), R("kn", a, b), ALU.add)
            tt(R("ub", a, b), R(new, a, b), dh, ALU.mult)
            if PAR["chg"][t] == "n":
                mm(group(nx, [(M("idn"), y), (M("nub"), R("ub", a, b))]))
                tt(R("chg", a, b), xv, nx, ALU.not_equal)
            elif PAR["chg"][t] == "v":
                mm(group(ex, [(M("n2b"), xv), (M("p2b"), y)]))
                tt(R("chg", a, b), R("ub", a, b), ex, ALU.not_equal)
                mm(group(nx, [(M("idn"), y), (M("nub"), R("ub", a, b))]))
            else:
                mm(group(ex, [(M("nid"), xv), (M("idn"), y), (M("nub"), R("ub", a, b))])
                   + group(nx, [(M("idn"), y), (M("nub"), R("ub", a, b))]))
                act(R("chg", a, b), ex, AF.Abs)
            lin(R(mir, a, b), nx, eng="va" if last else "a")
            mm([(R("psa", a, b), R("bones"), R("chg", a, b), True, True)])
            act(R("chw", a, b), R("psa", a, b), AF.Sign)
        lin(lanes("xw%d" % (1 - m), m), R(mir, 0, L), eng="va" if last else "g")
        if not last:
            lin(lanes(xw, m), R(mir, 0, L), eng="g")
            pn = "psd" if late else "psb"
            if late:
                mm(group(R(pn, L, 2 * L), [(M("nid"), R(new)), (M("idn"), R("new%d" % m))]))
            else:
                mm([x for s in range(4) for x in group(R(pn, L + 64 * s, L + 64 * (s + 1)), [
                    (M("nid"), R(new, 64 * s, 64 * (s + 1))), (blk("sel4", s, P32), R("fb", m, 768, ST, p=P32))])])
            act(R("junk"), R(pn, L, 2 * L), AF.Abs, scale=1.0 / BIG, accum=R("asum", 0, 1))
            mm([(R(pn, L, L + 1), R("o16"), R("asum", 0, 1), True, True)])
            lin(R("asum", 1, 2), R(pn, L, L + 1), 1.0, -31.5, eng="a")
            lin(R("asum", 2, 3), R("asum", 1, 2), 1.0, 64 * MAGIC, eng="a")
            lin(R("asum", 3, 4), R("asum", 2, 3), -1.0, 64 * MAGIC, eng="a")
            lin(R("am", 0, 1), R(pn, L, L + 1), 1.0, R("asum", 3, 4), eng="a")
        if late:
            fo = R("psd", 3 * L, 3 * L + 64, p=P32)
            mm(group(fo, [(R("selt", 32 * s, 32 * (s + 1)), R(new, 64 * s, 64 * (s + 1))) for s in range(4)]))
            lin(R("ff", m, 768, ST, p=P32), fo, 1.0 / BIG, 1.0, eng="a")
        for a, b, e in PAR["hb"][t]:
            lin(R("hb", G * a, G * b), IND(R("chw"), R("shu", 12 * a, 12 * b)), 64.0, eng=e)
            for d in range(a, b):
                scan(R("cnt", G * d, G * (d + 1)), R("hb", G * d, G * (d + 1)), R("capt"), 0.0, ALU.add, ALU.min)
        for a, b in PAR["qp"][t]:
            qp = R("psa", L + 12 * a, L + 12 * b)
            mm([(qp, M("idn"), R("bhi", 12 * a, 12 * b), True, False), (qp, M("idn"), R("blo", 12 * a, 12 * b), False, False)]
               + [(R("psa", L + 12 * d + 1, L + 12 * (d + 1)), blk("dd", 16), R("cnt", G * d + 15, G * (d + 1) - 16, 16), False, False)
                  for d in range(a, b)]
               + [(qp, blk("dd", k), R("cnt", G * a + k, G * b, 16), False, k == 15) for k in range(16)])
            tt(R("q1", 12 * a, 12 * b), R("shi", 12 * a, 12 * b), qp, ALU.max)
            lin(R("qu", 12 * a, 12 * b), R("q1", 12 * a, 12 * b), eng="v")
        for a, b, e in PAR["mg"][t]:
            lin(R(nxt, L + G * a, L + G * b), IND(R(mir), R("qu", 12 * a, 12 * b)), eng=e)
        xn = "xw%d" % (1 - m)
        exchange(t, down, lambda d: R(nxt, *place(rank, d)), lambda d, r: R(xn, V + G * d, V + G * (d + 1)))
        if last:
            for d in range(N - 1):
                dma(T.yx[:, V + G * d:V + G * (d + 1)], R(xn, V + G * d, V + G * (d + 1)), 128 * G * 2, eng="sa"[d % 2])
            dma(T.yx[:, 0:V], R(xn, 0, V), 128 * V * 2)
            dma(T.yf[:], R("ff", p=P32), 98304)
            mm(group(R("psb", L, 2 * L), whole("i32", "kn0", 0, L) + whole("i32", "kn1", 0, L)))
            lin(R("yks"), R("psb", L, 2 * L))
            dma(T.yk[:], R("yks"), 131072)
        if not late:
            continue
        for row, (x0, x1, x2) in enumerate((("vhi", "chi", "ohi"), ("vlo%d" % m, "clo", "olo"))):
            rows = slice(row, 128, 16)
            dma(R("wo", 0, L, p=rows), R(x0, p=rows), 4096)
            dma(R("wo", L, 17 * L, p=rows), R(x1), 65536)
            dma(R("wo", 17 * L, 33 * L, p=rows), R(x2), 65536)
        for c in range(8):
            lin(R("og", 512 * c, 512 * (c + 1)), IND(R("wo"), R("ou", 32 * c, 32 * (c + 1))), eng=PAR["og"][t][c])
        if last:
            origins("psb", 0)
            tt(R("yos"), R("on0"), R("psb", 0, L), ALU.add)
            dma(T.yo[:], R("yos"), 131072)
    return ops, Q


def schedule(ops, noise=None):
    n = len(ops)
    deps = [list(o["deps"]) for o in ops]
    users = [[] for _ in range(n)]
    for i in range(n):
        for j in deps[i]:
            users[j].append(i)
    if "order" in FOUND:
        return keep_order(deps, users, FOUND["order"]), FOUND["eng"]
    prio = [0.0] * n
    for i in range(n - 1, -1, -1):
        o = ops[i]
        own = min(c for c, _ in o["alts"].values()) + o["lat"] + (2000.0 if o["kind"] == "d" else 0.0)
        prio[i] = own + max([prio[u] + SELF for u in users[i]] + [0.0])
    if noise is not None:
        prio = [p + x for p, x in zip(prio, noise)]
    best = now = lay_out(ops, deps, users, prio, False)
    for _ in range(PASSES):
        back = lay_out(ops, users, deps, now[3], True)
        now = lay_out(ops, deps, users, back[3], False)
        if max(now[3]) < max(best[3]):
            best = now
    order, eng = improve(ops, deps, best[0], best[1])
    FOUND["order"], FOUND["eng"] = order, eng
    return order, eng


def tables(ops, deps):
    n, above, few, names = len(ops), [], [], {}
    for i in range(n):
        implied = 0
        for j in deps[i]:
            implied |= above[j]
        few.append([j for j in deps[i] if not implied >> j & 1])
        for j in deps[i]:
            implied |= 1 << j
        above.append(implied)
    banks = [[names.setdefault(b, len(names)) for b in o["banks"]] for o in ops]
    cost = [[{e: (FIX[e] * s["fix"] + (c - FIX[e]) * s["cyc"] / CYC * (s["gath"] / GATH if o["ind"] else 1.0) if o["kind"] == "c" else
                  c * (s["issue"] if o["kind"] == "r" else 1.0)) for e, (c, _) in o["alts"].items()} for o in ops] for s in SPEEDS]
    for k, s in enumerate(SPEEDS):
        for i in [i for i, o in enumerate(ops) if o["kind"] == "r"][:2]:
            cost[k][i]["g"] += FIRST * s["issue"]
    wire = [[o["lat"] * s["dma"] if o["kind"] == "d" and o["lat"] >= 450.0 else 0.0 for o in ops] for s in SPEEDS]
    lat = [[(o["lat"] + 2000.0) * s["dma"] if o["kind"] == "d" else o["lat"] * s["far"] for o in ops] for s in SPEEDS]
    waits = [(HOP * s["fix"], SELF * s["fix"], 1300.0 * s["dma"], 700.0 * s["dma"]) for s in SPEEDS]
    return few, banks, cost, wire, lat, len(names), waits


def replay(tab, order, eng, k, run=None, same=0):
    few, banks, cost, wire, lat, nb = tab
    n, cost, lat, mark = len(order), cost[k], lat[k], same // STRIDE
    if mark:
        marks = run[3][:mark]
        free, last, bt, be, bi, ot, oi = [x.copy() for x in marks[-1][:7]]
        line, lastw = marks[-1][7:]
        start, fin, why = run[0].copy(), run[1].copy(), run[2].copy()
    else:
        marks, free, last, line, lastw = [], {}, {}, 0.0, -1
        bt, be, bi, ot, oi = [0.0] * nb, [""] * nb, [-1] * nb, [0.0] * nb, [-1] * nb
        start, fin, why = [0.0] * n, [0.0] * n, [-1] * n
    for p in range(mark * STRIDE, n):
        if p % STRIDE == 0 and p > mark * STRIDE:
            marks.append((free.copy(), last.copy(), bt.copy(), be.copy(), bi.copy(), ot.copy(), oi.copy(), line, lastw))
        i = order[p]
        e = eng[i]
        at, by = free.get(e, 0.0), last.get(e, -1)
        for j in few[i]:
            x = fin[j] + (HOP if eng[j] != e else SELF)
            if x > at:
                at, by = x, j
        for b in banks[i]:
            if be[b] != e:
                ot[b], oi[b], be[b] = bt[b] + HOP, bi[b], e
            if ot[b] > at:
                at, by = ot[b], oi[b]
        end = at + cost[i][e]
        free[e], last[e], start[i] = end, i, at
        for b in banks[i]:
            bt[b], bi[b] = end, i
        if wire[i]:
            if line > end + 1300.0:
                by = lastw
            line, lastw = max(line, end + 1300.0) + wire[i], i
            fin[i] = line + 700.0
        else:
            fin[i] = end + lat[i]
        why[i] = by
    return start, fin, why, marks


def improve(ops, deps, order, eng):
    n, tab, rng = len(ops), tables(ops, deps), np.random.default_rng(SEED)
    few, users = tab[0], [[] for _ in range(n)]
    for i in range(n):
        for j in few[i]:
            users[j].append(i)
    runs = [replay(tab, order, eng, k) for k in range(len(SPEEDS))]
    unit = [max(r[1]) for r in runs]
    now, best = 9.0, (9.0, order, eng)
    for k in range(TRIES):
        if k % 64 == 0:
            at, place = runs[0][0], {y: p for p, y in enumerate(order)}
            order = sorted(order, key=lambda y: (at[y], place[y]))
            runs = [replay(tab, order, eng, s) for s in range(len(SPEEDS))]
        start, fin, why, _ = runs[int(rng.integers(len(runs)))]
        i, chain = fin.index(max(fin)), []
        while why[i] >= 0:
            if why[i] not in few[i] or len(ops[i]["alts"]) > 1:
                chain.append(i)
            i = why[i]
        i = chain[int(rng.integers(len(chain)))]
        j, kind, eng2 = why[i], rng.random(), eng
        if j in few[i] or (len(ops[i]["alts"]) > 1 and kind < 0.2):
            order2, eng2, a = order, list(eng), order.index(i)
            eng2[i] = [e for e in ops[i]["alts"] if e != eng[i]][0]
        elif len(ops[j]["alts"]) > 1 and kind < 0.4:
            order2, eng2, a = order, list(eng), order.index(j)
            eng2[j] = [e for e in ops[j]["alts"] if e != eng[j]][0]
        else:
            a, b = order.index(j), order.index(i)
            step = int(rng.geometric(0.15)) - 1 if rng.random() < 0.4 else 0
            if rng.random() < 0.5:
                a = max(0, a - step)
                need, up, stay = set(few[i]), [i], []
                for x in order[b - 1:a - 1 if a else None:-1]:
                    if x in need:
                        up.append(x)
                        need.update(few[x])
                    else:
                        stay.append(x)
                if j in need:
                    continue
                order2 = order[:a] + up[::-1] + stay[::-1] + order[b + 1:]
            else:
                b = min(n - 1, b + step)
                need, down, stay = set(users[j]), [j], []
                for x in order[a + 1:b + 1]:
                    if x in need:
                        down.append(x)
                        need.update(users[x])
                    else:
                        stay.append(x)
                if i in need:
                    continue
                order2 = order[:a] + stay + down + order[b + 1:]
        heat = HEAT * (1.0 - k / TRIES) ** 2
        bar, runs2, x = now - heat * math.log(rng.random() + 1e-12), [], 0.0
        for s in range(len(SPEEDS)):
            runs2.append(replay(tab, order2, eng2, s, runs[s], a))
            x += (max(runs2[-1][1]) + MEAN * sum(runs2[-1][1]) / n) / unit[s] / len(unit)
        if x <= bar:
            order, eng, runs, now = order2, eng2, runs2, x
            if x < best[0]:
                best = (x, order, eng)
    return best[1], best[2]


def replay(tab, order, eng, k, state=None, fin=None):
    few, banks, cost, wire, lat, nb, waits = tab
    cost, wire, lat, (HOP, SELF, pre, post) = cost[k], wire[k], lat[k], waits[k]
    if state is None:
        state = ({}, {}, [0.0] * nb, [""] * nb, [-1] * nb, [0.0] * nb, [-1] * nb, [0.0, -1])
        fin = [0.0] * len(few)
    free, last, bt, be, bi, ot, oi, (line, lastw) = [x.copy() for x in state]
    start, why = {}, {}
    for i in order:
        e = eng[i]
        at, by = free.get(e, 0.0), last.get(e, -1)
        for j in few[i]:
            x = fin[j] + (HOP if eng[j] != e else SELF)
            if x > at:
                at, by = x, j
        for b in banks[i]:
            if be[b] != e:
                ot[b], oi[b], be[b] = bt[b] + HOP, bi[b], e
            if ot[b] > at:
                at, by = ot[b], oi[b]
        end = at + cost[i][e]
        free[e], last[e], start[i] = end, i, at
        for b in banks[i]:
            bt[b], bi[b] = end, i
        if wire[i]:
            if line > end + pre:
                by = lastw
            line, lastw = max(line, end + pre) + wire[i], i
            fin[i] = line + post
        else:
            fin[i] = end + lat[i]
        why[i] = by
    return start, fin, why, (free, last, bt, be, bi, ot, oi, [line, lastw])


def tails(tab, users, rest, eng, k):
    few, banks, cost, wire, lat, nb, waits = tab
    wire, (HOP, SELF, pre, post) = wire[k], waits[k]
    tail, queue, bank, line = {}, {}, [{} for _ in range(nb)], -1e9
    for i in rest[::-1]:
        e = eng[i]
        after = max([0.0] + [tail[u] + (HOP if eng[u] != e else SELF) for u in users[i]])
        if wire[i]:
            line = wire[i] + max(post + after, line)
            after = pre + line
        else:
            after += lat[k][i]
        after = max(after, queue.get(e, 0.0))
        for b in banks[i]:
            for e2, x in bank[b].items():
                if e2 != e and x + HOP > after:
                    after = x + HOP
        tail[i] = queue[e] = after + cost[k][i][e]
        for b in banks[i]:
            bank[b][e] = tail[i]
    return tail, queue, bank, line


def improve(ops, deps, order, eng):
    n, tab, rng = len(ops), tables(ops, deps), np.random.default_rng(SEED)
    few, users, ks, eng = tab[0], [[] for _ in range(n)], range(len(SPEEDS)), list(eng)
    for i in range(n):
        for j in few[i]:
            users[j].append(i)
    unit = [max(replay(tab, order, eng, k)[1]) * len(ks) for k in ks]
    best, done = (9.0, order, eng), 0
    while done < TRIES:
        at, place = replay(tab, order, eng, 0)[0], {y: p for p, y in enumerate(order)}
        order = sorted(order, key=lambda y: (at[y], place[y]))
        x = sum(max(replay(tab, order, eng, k)[1]) / unit[k] for k in ks)
        if x < best[0]:
            best = (x, order, list(eng))
        lo = max(0, int(rng.integers(-WINDOW // 2, n - WINDOW // 2)))
        head, win, rest = order[:lo], order[lo:lo + WINDOW], order[lo + WINDOW:]
        inside, before, after = set(win), [replay(tab, head, eng, k) for k in ks], [tails(tab, users, rest, eng, k) for k in ks]
        out = [{i: max([0.0] + [after[k][0][u] + tab[6][k][0] for u in users[i] if u in after[k][0]]) for i in order[:lo + WINDOW]} for k in ks]
        fixed = [max([0.0] + [before[k][1][i] + out[k][i] for i in head]) for k in ks]

        def run(win, k):
            start, fin, why, (free, last, bt, be, bi, ot, oi, line) = replay(tab, win, eng, k, before[k][3], before[k][1])
            top, by, o, total, HOP = fixed[k], -1, out[k], 0.0, tab[6][k][0]
            for i in win:
                x = fin[i]
                total += x
                x += o[i]
                if x > top:
                    top, by = x, i
            for e, x in after[k][1].items():
                if free.get(e, 0.0) + x > top:
                    top, by = free[e] + x, last[e]
            for b, at in enumerate(after[k][2]):
                for e, x in at.items():
                    if e != be[b] and bt[b] + HOP + x > top:
                        top, by = bt[b] + HOP + x, bi[b]
            if line[0] + after[k][3] > top:
                top, by = line[0] + after[k][3], line[1]
            chain = []
            while by in inside:
                j = why[by]
                if j in inside and (j not in few[by] or len(ops[by]["alts"]) > 1):
                    chain.append((by, j))
                by = j
            return (top + MEAN * total / n) / unit[k], chain

        runs = [run(win, k) for k in ks]
        now = sum(r[0] for r in runs)
        heat = HEAT * (1.0 - done / TRIES) ** 2
        done += STAY
        for pick, kind, side, far, luck in rng.random((STAY, 5)).tolist():
            chain = runs[int(side * 64) % len(runs)][1]
            if not chain:
                continue
            i, j = chain[int(pick * len(chain))]
            flip, win2 = -1, win
            if j in few[i] or (len(ops[i]["alts"]) > 1 and kind < 0.2):
                flip = i
            elif len(ops[j]["alts"]) > 1 and kind < 0.4:
                flip = j
            else:
                if kind > 0.8:
                    i, j = (j, j) if side < 0.5 else (i, i)
                a, b, step = win.index(j), win.index(i), int(-(6.0, REACH)[kind > 0.6] * math.log(far / 0.6 + 1e-9)) if far < 0.6 else 0
                if side < 0.5:
                    a = max(0, a - step)
                    need, up, stay = set(few[i]), [i], []
                    for x in win[a:b][::-1]:
                        if x in need:
                            up.append(x)
                            need.update(few[x])
                        else:
                            stay.append(x)
                    if j in need:
                        continue
                    win2 = win[:a] + up[::-1] + stay[::-1] + win[b + 1:]
                else:
                    b = min(len(win) - 1, b + step)
                    need, down, stay = set(users[j]), [j], []
                    for x in win[a + 1:b + 1]:
                        if x in need:
                            down.append(x)
                            need.update(users[x])
                        else:
                            stay.append(x)
                    if i in need:
                        continue
                    win2 = win[:a] + stay + down + win[b + 1:]
            if flip >= 0:
                was = eng[flip]
                eng[flip] = [e for e in ops[flip]["alts"] if e != was][0]
            runs2 = [run(win2, k) for k in ks]
            x = sum(r[0] for r in runs2)
            if x <= now - heat * math.log(luck + 1e-12):
                win, runs, now = win2, runs2, x
            elif flip >= 0:
                eng[flip] = was
        order = head + win + rest
    x = sum(max(replay(tab, order, eng, k)[1]) / unit[k] for k in ks)
    return (order, eng) if x < best[0] else best[1:]


def keep_order(deps, users, order):
    left, done, out = [len(d) for d in deps], [False] * len(deps), []
    while len(out) < len(order):
        for i in order:
            if not done[i] and left[i] == 0:
                done[i] = True
                out.append(i)
                for u in users[i]:
                    left[u] -= 1
                break
    return out


def lay_out(ops, deps, users, prio, back):
    n = len(ops)
    left = [len(d) for d in deps]
    ready = [i for i in range(n) if left[i] == 0]
    busy = {}
    eng, fin, start = [None] * n, [0.0] * n, [0.0] * n

    def gap(at, c, e, banks):
        lanes = [(busy.setdefault(e, []), 0.0)] + [(busy.setdefault(b, []), HOP) for b in banks]
        moved = True
        while moved:
            moved = False
            for iv, pad in lanes:
                lo, hi = 0, len(iv)
                while lo < hi:
                    mid = (lo + hi) // 2
                    if iv[mid][1] + pad > at:
                        hi = mid
                    else:
                        lo = mid + 1
                while lo < len(iv):
                    s, f, who = iv[lo]
                    if s - pad >= at + c:
                        break
                    if f + pad > at and (pad == 0.0 or who != e):
                        at, moved = f + pad, True
                    lo += 1
        return at

    def put(key, item):
        iv = busy.setdefault(key, [])
        lo, hi = 0, len(iv)
        while lo < hi:
            mid = (lo + hi) // 2
            if iv[mid] > item:
                hi = mid
            else:
                lo = mid + 1
        iv.insert(lo, item)

    rank = [0] * n
    for k, i in enumerate(sorted(range(n), key=lambda x: (prio[x], -x))):
        rank[i] = k
    while ready:
        i = max(ready, key=lambda x: rank[x])
        o = ops[i]
        cand = []
        for e, (c, _) in o["alts"].items():
            at = max([0.0] + [fin[j] + (HOP if eng[j] != e else SELF) for j in deps[i]])
            if back:
                at += o["lat"] + (2000.0 if o["kind"] == "d" else 0.0)
            at = gap(at, max(c, 1.0), e, o["banks"])
            cand.append((at + c, at, e))
        end, at, e = min(cand)
        eng[i], start[i] = e, at
        for key in [e] + o["banks"]:
            put(key, (at, max(end, at + 1.0), e))
        if back:
            fin[i] = end
        elif o["kind"] == "d" and o["lat"] < 500.0:
            fin[i] = end + 2000.0 + o["lat"]
        elif o["kind"] == "d":
            w = gap(end + 1300.0, o["lat"], "w", [])
            put("w", (w, w + o["lat"], "w"))
            fin[i] = w + o["lat"] + 700.0
        else:
            fin[i] = end + o["lat"]
        ready.remove(i)
        for u in users[i]:
            left[u] -= 1
            if left[u] == 0:
                ready.append(u)
    order = sorted(range(n), key=lambda x: (start[x], x))
    return order, eng, start, fin


def bank_order(ops, order, eng):
    lastop = {}
    for i in order:
        for b in ops[i]["banks"]:
            at = lastop.setdefault(b, {})
            for e, j in at.items():
                if e != eng[i]:
                    ops[i]["deps"][j] = True
            at[eng[i]] = i


def rank_program(g, core, T, topo):
    rank = T.rank_of(core)
    if rank is None:
        return
    ops, Q = build(g, rank, T, topo)
    order, eng = schedule(ops)
    bank_order(ops, order, eng)
    need = [False] * len(ops)
    for i, o in enumerate(ops):
        o["wait"] = [j for j in o["deps"] if o["kind"] != "x"]
        for j in o["wait"]:
            need[j] = True
    count, seen, top, known = {}, {}, {}, {}
    place = {i: k for k, i in enumerate(order)}
    for i in order:
        o, e = ops[i], eng[i]
        if o["kind"] == "c" and need[i]:
            count[e] = count.get(e, 0) + 1
            o["sem"] = ("e" + e, count[e])
        if o["sem"]:
            top[o["sem"][0]] = o["sem"][1]
        if o["kind"] == "x":
            continue
        mine = known.setdefault(e, {})
        for j in sorted(o["wait"], key=lambda x: -place[x]):
            s, c = ops[j]["sem"]
            if mine.get(s, 0) < c:
                Q[e].wait_ge(T.sem[s], c)
                seen[(e, s)] = mine[s] = c
                for s2, c2 in ops[j].get("knew", {}).items():
                    if mine.get(s2, 0) < c2:
                        mine[s2] = c2
        o["knew"] = dict(mine)
        ins = o["alts"][e][1](Q[e])
        if o["kind"] == "d":
            ins.then_inc(T.sem[o["sem"][0]], 16)
        elif o["kind"] == "c" and need[i]:
            ins.then_inc(T.sem[o["sem"][0]], 1)
    for s, c in top.items():
        if max(seen.get((e, s), 0) for e in Q) < c:
            g.wait_ge(T.sem[s], c)
